import numpy as np, ml_dtypes
CORES = [24,25,26,27,28,29,30,31]
N = 8
import mx_ref
BF = ml_dtypes.bfloat16
def gcols(t, e):
    v = np.concatenate([t.reshape(8, 16, -1, 4), np.zeros((8, 16, 1, 4), BF)], axis=2)
    return np.ascontiguousarray(np.stack([v[g][:, e[g]] for g in range(8)])).reshape(128, -1)
def tile(rs):
    return np.stack(rs, axis=2).reshape(128, -1).astype(BF)
def cut(t, i, w=512):
    return t[:, w * i:w * i + w]
def pick(q, e):
    c = np.concatenate([q[0].reshape(128, -1, 4), np.zeros((128, 1, 4), np.uint8)], axis=1); s = np.concatenate([q[1], np.ones((16, 1), np.uint8)], axis=1)
    return (np.ascontiguousarray(c[:, e].reshape(128, -1)), np.ascontiguousarray(s[:, e]))
def join(*qs):
    return (np.concatenate([q[0] for q in qs], axis=1), np.concatenate([q[1] for q in qs], axis=1))
def put(q, e, v):
    c, s = q[0].reshape(128, -1, 4).copy(), q[1].copy(); c[:, e] = v[0].reshape(128, -1, 4); s[:, e] = v[1]
    return (c.reshape(128, -1), s)
def pk(c, s):
    return (np.ascontiguousarray(c), mx_ref.live(s))
def emit(q):
    return q[0], q[1]
def packed(v, rng):
    q = [mx_ref.quantize(np.ascontiguousarray(v[r])) for r in range(N)]
    return np.stack([a for a, b in q]), np.stack([mx_ref.plane(b, rng) for a, b in q])
def values_of_codes():
    e, c = np.zeros((128, 128, 4), np.float32), np.zeros((128, 2, 4), np.uint8)
    e[np.arange(128), np.arange(128), 0] = 1
    c[:127, :, 0] = np.arange(256).reshape(2, 128).T[:127]
    return mx_ref.matmul(mx_ref.quantize(e.reshape(128, 512).astype(BF)), (c.reshape(128, 8), np.full((16, 2), 127, np.uint8))).T.reshape(-1).astype(np.float64)
CODE_VALUE, SCALE_VALUE = values_of_codes(), 2.0 ** (np.arange(256) - 127.0)
def decode(q):
    return (CODE_VALUE[q[0]].reshape(16, 8, -1, 4) * SCALE_VALUE[q[1]][:, None, :, None] + 0.0).reshape(128, -1).astype(np.float32)
def f(rng, *shape):
    return mx_ref.flush((rng.standard_normal(shape, dtype=np.float32) * np.exp2(rng.integers(-2, 3, shape[:-1] + (1,)))).astype(BF))
def wide(rng, *shape, cols=0):
    v = rng.standard_normal(shape, dtype=np.float32) * np.exp2(rng.integers(-12, 13, shape)).astype(np.float32)
    if cols: v *= np.repeat(np.exp2(rng.integers(-cols, cols + 1, shape[:-2] + (1, shape[-1] // 4))) * (rng.random(shape[:-2] + (1, shape[-1] // 4)) > 0.0625), 4, axis=-1).astype(np.float32)
    return mx_ref.flush(v.astype(BF))
C, K, R = 448, 64, 2
def partner(r, t):
    return r ^ (1 << t)
def highest(p):
    return np.argsort(-(p[::16] + np.float32(0.0)), axis=1, kind="stable")[:, :K]
def warp(own, other):
    n = len(own)
    rows, i = np.arange(n), np.argsort(own, axis=1)
    a, b = np.take_along_axis(own, i, axis=1), np.take_along_axis(other, i, axis=1)
    length, back = np.ones((n, K), np.int64), np.full((n, K), -1)
    for j in range(1, K):
        l = np.where(b[:, :j] < b[:, j:j + 1], length[:, :j], 0)
        best = np.argmax(l, axis=1)
        length[:, j] = 1 + l[rows, best]
        back[:, j] = np.where(l[rows, best] > 0, best, -1)
    on = np.zeros((n, K), bool)
    e = np.argmax(length, axis=1)
    for j in range(K):
        on[rows[e >= 0], e[e >= 0]] = True
        e = np.where(e >= 0, back[rows, e], -1)
    w, p = np.zeros((n, C), np.int64), np.arange(C)
    for k in range(n):
        c, d = a[k][on[k]], b[k][on[k]]
        i = np.searchsorted(c, p, side="right") - 1
        w[k] = np.where(i < 0, np.maximum(0, d[0] - c[0] + p), np.minimum(d[i] + p - c[i], np.append(d[1:] - 1, C - 1)[i]))
    return w
def clear(v):
    v = v.astype(np.float32)
    v[np.abs(v) < np.float32(2.0 ** -16)] = 0
    return v.astype(BF)
def numbers_of(rng):
    return {"x": clear(f(rng, N, 128, 4 * C)), "u": np.array(f(rng, N, 128, 512)), "v": np.array(f(rng, N, 128, 512))}
def weights(rng, w):
    c, p = packed(w, rng)
    return {"wc": c, "ws": p}
def quiet(rng, a, b):
    w = np.array(f(rng, N, 128, 2048)).reshape(N, 8, 16, 4, 8, 16, 4)
    w[:, :, 0] = 0
    w[:, :, :, :, :, :a] = 0
    w[:, :, :, :, :, b:] = 0
    return weights(rng, w.reshape(N, 128, 2048))
def signs(rng):
    return np.stack([rng.permutation(8) % 2 * 2.0 - 1.0 for r in range(N)])
def planted(d, rng, s, m, unit, k):
    x = d["x"].astype(np.float32).reshape(N, 8, 16, C, 4)
    g = ((s[..., None] >> np.arange(8)) & 1) * 2.0 ** np.arange(8) * unit[:, None, None, None]
    x[:, :, 0] = 0
    x[:, :, 0, :, 0] = m
    x[:, :, 8] = g[..., :4]
    x[:, :, 9] = g[..., 4:]
    x[:, :, 10:] = rng.integers(4, 8, (N, 8, 6, C, 4)) * rng.choice([-8.0, 8.0], (N, 8, 6, C, 4)) * unit[:, None, None, None, None]
    u = d["u"].reshape(N, 128, 128, 4)
    k = k.astype(np.float32).astype(BF)
    u[:, :, ::16] = 0
    for h in range(0, 128, 16):
        u[:, h, h, 0] = k
        u[:, h + 8:h + 10, h] = k[:, None, None]
    return {"x": x.reshape(N, 128, 4 * C).astype(BF), "u": u.reshape(N, 128, 512), "v": d["v"], **quiet(rng, 1, 8)}
def patterns(rng):
    i = np.arange(K)
    return np.stack([i, i[::-1], i + 7 - 2 * (i % 8), K - 8 - i + 2 * (i % 8), i ^ 1, rng.permutation(K), (i - 1) % K, (i + K // 2) % K])
def setup_inputs(rng):
    return {**numbers_of(rng), **weights(rng, f(rng, N, 128, 2048))}
def setup_inputs_ties(rng):
    d = numbers_of(rng)
    o = rng.permutation(N)
    x = d["x"].reshape(N, 8, 16, C, 4)
    for r in range(N):
        n = 1 if o[r] == 0 else (3, 9, 24)[o[r] % 3]
        a = x[r][:, :8, :n].copy()
        if n > 1: a[:, :, 2] = 0
        x[r][:, :8] = a[:, :, rng.permutation(C) % n]
        if o[r] == 1: x[r] = 0
    u = d["u"].reshape(N, 8, 16, 8, 16, 4)
    for h in range(8):
        a = u[:, h, :8, h, 0].copy()
        u[:, :, :, h, 0] = 0
        u[:, h, :8, h, 0] = a
    return {"x": x.reshape(N, 128, 4 * C), "u": u.reshape(N, 128, 512), "v": d["v"], **quiet(rng, 8, 16)}
def setup_inputs_near(rng):
    d = numbers_of(rng)
    s = (np.argsort(rng.random((N, 8, C)), axis=2) + 1) // 2
    tiny = (np.arange(N) // 2 + int(rng.integers(2))) % 2 == 0
    m = np.repeat((signs(rng) * ~tiny[:, None])[:, :, None], C, axis=2)
    for r in range(N):
        m[r, rng.permutation(8)[:4], rng.integers(0, C, 4)] = 2.0 ** 30 * rng.choice([-1.0, 1.0], 4)
    return planted(d, rng, s, m, np.where(tiny, 2.0 ** -29, 2.0 ** -23), np.where(tiny, 2.0 ** -30, 1.0))
def setup_inputs_chains(rng):
    d = numbers_of(rng)
    s, m = np.zeros((N, 8, C), np.int64), -1.0 * rng.integers(1, 8, (N, 8, C))
    for o in range(0, N, 4):
        k, to = rng.permutation(8), patterns(rng)
        for g in range(8):
            a, b, t = rng.permutation(K), rng.permutation(K), to[k[g]]
            four = (a, a, t[a], t[a]) if (k[g] + o // 4) % 2 == 0 else (a, t[a], b, t[b])
            for i in range(4):
                e = (np.arange(K), np.arange(C - K, C), np.sort(rng.permutation(C)[:K]))[(k[g] + i) % 3]
                m[o + i, g, e] = 0
                s[o + i, g, e[four[i]]] = K - np.arange(K)
    return planted(d, rng, s, m, np.full(N, 2.0 ** -23), np.ones(N))
def setup_inputs_huge(rng):
    d = numbers_of(rng)
    x = 2.0 ** 30 * (0.6 + 0.4 * rng.random((N, 128, C, 4)))
    c = np.stack([rng.permutation(C) % 2 * 2.0 - 1.0 for r in range(N)])
    c[rng.permutation(N) < N // 2] = 1
    x *= c[:, None, :, None]
    u = d["u"].reshape(N, 128, 128, 4)
    a = 2.0 ** 30 * (1 - 0.25 * rng.random((N, 128, 8, 4))) * signs(rng)[:, None, :, None]
    u[:, :, ::16] = a.astype(np.float32).astype(BF)
    w = np.zeros((N, 128, 4, 128, 4), np.float32)
    i = np.arange(128)
    for b in range(4): w[:, i, b, i, b] = -16
    return {"x": x.astype(np.float32).reshape(N, 128, 4 * C).astype(BF), "u": u.reshape(N, 128, 512), "v": d["v"], **weights(rng, w.reshape(N, 128, 2048).astype(BF))}
def setup_inputs_spread(rng):
    d = setup_inputs(rng)
    d["x"] = clear(wide(rng, N, 128, 4 * C, cols=6))
    return d
def check_inputs(d):
    b = []
    for k in ("x", "u", "v"):
        a = np.abs(d[k].astype(np.float32))
        if not (np.isfinite(a).all() and ((a == 0) | (a >= 2.0 ** -30) & (a <= 2.0 ** 30)).all()): b.append("a value of " + k)
    return b
def reference(x, u, v, wc, ws):
    qu = [mx_ref.quantize(u[r]) for r in range(N)]
    lay = [pk(wc[r], ws[r]) for r in range(N)]
    now = [x[r] for r in range(N)]
    y, oq = np.zeros((N, 128, C), np.float32), np.zeros((N, 8, R * C), np.float32)
    oc, osc = np.zeros((N, 128, 4 * C), np.uint8), np.zeros((N, 16, C), np.uint8)
    for t in range(R):
        state = [mx_ref.quantize(now[r]) for r in range(N)]
        top = [highest(mx_ref.matmul(qu[r], state[r])) for r in range(N)]
        held = decode(join(*state)).astype(BF)
        for r in range(N):
            e = partner(r, t)
            q = warp(top[r], top[e])
            oq[r, :, C * t:C * t + C] = q
            came = gcols(cut(held, e, 4 * C), q)
            mid = ((now[r].astype(np.float32) + came.astype(np.float32)) * np.float32(0.5)).astype(BF)
            g, z = mid.astype(np.float32), mx_ref.quantize(mid)
            now[r] = tile([g[:, b::4] + np.maximum(mx_ref.matmul(pick(lay[r], np.arange(128 * b, 128 * b + 128)), z), np.float32(0.0)) * np.float32(0.015625) for b in range(4)])
    for r in range(N):
        z = mx_ref.quantize(now[r])
        y[r] = mx_ref.matmul(mx_ref.quantize(v[r]), z)
        oc[r], osc[r] = emit(z)
    return {"y": y, "oq": oq, "oc": oc, "osc": osc}

@@ -1,0 +1,468 @@
+from concourse.mybir import dt, AluOpType, ActivationFunctionType
+
+C, H, K = 448, 224, 64
+S = 130
+TB = 32 * S
+BIG = 1.0e29
+F32, BF, I32, U16, X4, U8 = "float32", "bfloat16", "int32", "uint16", "float8_e4m3fn_x4", "uint8"
+
+
+def _sb(n, d):
+    return ("sbuf", [128, n], d)
+
+
+SCRATCH = {
+    "xin": _sb(4 * C, BF), "x1": _sb(4 * C, BF), "x2": _sb(4 * C, BF), "xh": _sb(4 * C, BF), "gt": _sb(4 * C, BF),
+    "dh": _sb(4 * C, BF), "rl": _sb(4 * C, F32), "ysb": _sb(C, F32),
+    "uin": _sb(512, BF), "vin": _sb(512, BF), "uq": _sb(128, X4), "us": _sb(128, U8), "ur": _sb(128, X4),
+    "urs": _sb(128, U8), "vq": _sb(128, X4), "vs": _sb(128, U8), "wq": _sb(512, X4), "wsc": _sb(512, U8),
+    "tq0": _sb(C, X4), "tq1": _sb(C, X4), "tq2": _sb(C, X4), "ts0": _sb(C, U8), "ts1": _sb(C, U8), "ts2": _sb(C, U8),
+    "lq0": _sb(C, X4), "lq1": _sb(C, X4), "ls0": _sb(C, U8), "ls1": _sb(C, U8), "gq": _sb(C, X4), "gs": _sb(C, U8),
+    "eb": _sb(2048, BF), "ebq": _sb(512, X4), "ebs": _sb(512, U8), "ek": _sb(512, BF), "ekq": _sb(128, X4),
+    "eks": _sb(128, U8),
+    "ct": _sb(16 * H, BF), "cq": _sb(4 * H, X4), "cs": _sb(4 * H, U8), "sg": _sb(6 * H, BF),
+    "et": _sb(12 * 128, BF), "eq": _sb(3 * 128, X4), "es": _sb(3 * 128, U8), "sg2": _sb(4 * 128, BF),
+    "iw": _sb(C, I32), "pw": _sb(C, I32), "km": _sb(H, F32), "r16": _sb(H, F32), "r01": _sb(128, F32),
+    "iof": _sb(C, F32), "iblk": _sb(8, I32), "ibs": _sb(8, I32), "blk": _sb(8, F32), "ones": _sb(64, BF),
+    "iul": _sb(8, I32), "oul": _sb(8, U16), "ip": _sb(2, I32), "ipa": _sb(2, I32), "pc": _sb(8, F32),
+    "thr": _sb(28, F32), "bex": _sb(4, F32), "bs": _sb(12, F32), "ksg": _sb(128, F32), "wt": _sb(128, F32),
+    "sv": _sb(192, BF), "zt": _sb(4 * S, BF),
+    "mx": _sb(H, F32), "am": _sb(H, F32), "wm": _sb(H, F32), "se": _sb(H, F32), "so": _sb(H, F32),
+    "f1": _sb(H, BF), "p1": _sb(H, BF), "cb": _sb(384, BF), "cn": _sb(384, BF), "jk": _sb(384, BF),
+    "jv": _sb(28 * K, BF), "acc": _sb(2, F32), "oa": _sb(4, U16), "cd": _sb(128, F32), "col": _sb(128, F32),
+    "a2": _sb(128, F32), "w2": _sb(128, F32), "f2": _sb(128, BF), "p2": _sb(128, BF), "a3": _sb(128, F32),
+    "w3": _sb(128, F32), "or2": _sb(8, U16),
+    "ra0": _sb(128, BF), "ra1": _sb(128, BF), "ht0": _sb(128, F32), "ht1": _sb(128, F32),
+    "lr0": _sb(K, BF), "lr1": _sb(K, BF), "lh0": _sb(K, F32), "lh1": _sb(K, F32),
+    "ora": _sb(4, U16), "kt": _sb(K, F32), "at": _sb(K, F32), "ok": _sb(8, U16), "vacc": _sb(28, F32),
+    "ov": _sb(28, U16),
+    "a4": _sb(128, F32), "w4": _sb(128, F32), "sm": _sb(40, F32), "od": _sb(12, U16),
+    "oe": _sb(8, U16), "tb0": _sb(3 * TB + 16, BF), "tb1": _sb(3 * TB + 16, BF), "ft": _sb(33 * S, BF),
+    "lr": _sb(128, F32), "key": _sb(K, F32), "pm": _sb(K + 1, F32), "cc": _sb(4 * K, F32), "bm": _sb(2 * K, F32),
+    "dl": _sb(K, F32), "zz": _sb(129, F32), "ut": _sb(K + 1, F32), "fw": _sb(C, F32), "ug": _sb(C, F32),
+    "qs": _sb(C, F32), "oqo": _sb(28, U16), "qr0": _sb(C, F32), "qr1": _sb(C, F32),
+    "ps": ("psum", [128, 4096], F32),
+}
+SEMAPHORES = (["ev", "ea", "ep", "eg", "loc", "z0", "z1"] + ["ar%d" % i for i in range(6)]
+              + ["dm%d" % i for i in range(24)])
+
+
+def rank_program(g, core, T, topo):
+    rank = T.rank_of(core)
+    if rank is None:
+        return
+    A, F = AluOpType, ActivationFunctionType
+    V, ACT, PE = g.vector, g.scalar, g.tensor
+    queue = {"v": V, "a": ACT, "p": PE, "g": g, "s": g.sync}
+    semof = {"v": "ev", "a": "ea", "p": "ep", "g": "eg"}
+    total, waited = {}, {}
+    clock = {q: {} for q in queue}
+    wrote, readers = {}, {}
+    ndma = [0]
+
+    def need(q, toks):
+        c = clock[q]
+        best = {}
+        for s, val, ck in toks:
+            if c.get(s, 0) < val and best.get(s, (0, None))[0] < val:
+                best[s] = (val, ck)
+        for s in sorted(best, key=lambda n: -len(best[n][1])):
+            val, ck = best[s]
+            if c.get(s, 0) >= val:
+                continue
+            queue[q].wait_ge(T.sem[s], val)
+            waited[s] = max(waited.get(s, 0), val)
+            for n in ck:
+                c[n] = max(c.get(n, 0), ck[n])
+            c[s] = val
+
+    def issue(q, fn, r, w, sem, inc):
+        w = list(w) + [n for n in r if n.startswith("ps")]
+        toks = [wrote[n] for n in list(r) + w if n in wrote]
+        for n in w:
+            toks += readers.get(n, [])
+        need(q, toks)
+        ins = fn()
+        if inc:
+            ins.then_inc(T.sem[sem], inc)
+            total[sem] = total.get(sem, 0) + inc
+            tok = (sem, total[sem], dict(clock[q]))
+            for n in r:
+                readers.setdefault(n, []).append(tok)
+            for n in w:
+                wrote[n], readers[n] = tok, []
+
+    def op(q, fn, r="", w=""):
+        issue(q, fn, r.split(), w.split(), semof[q], 1)
+
+    def dma(q, out, in_, r="", w=""):
+        ndma[0] += 1
+        issue(q, lambda: queue[q].dma_start(out, in_), r.split(), w.split(), "dm%d" % (ndma[0] - 1), 16)
+
+    def clear_table(t, after):
+        for j in range(8):
+            issue("s", lambda: g.sync.dma_start(T["tb%d" % t][:, 4 * S * j:4 * S * (j + 1)], T.zt[:]),
+                  ["zt", after], ["tb%d" % t] if j == 7 else [], "z%d" % t, 16)
+
+    def send(t, pairs, r, arr, land):
+        peer = T.cores[rank ^ (1 << t)]
+        rid, pid, _se = topo.addr(peer)
+        back = len(topo.engines(peer, core))
+        for out, in_ in pairs:
+            issue("g", lambda: g.remote_dma(out, in_, T.sem[arr], T.sem.loc, pid, rid, topo.mask(core, peer)),
+                  r.split(), [], None, 0)
+            total["loc"] = total.get("loc", 0) + len(topo.engines(core, peer))
+        total[arr] = back * len(pairs)
+        wrote[land] = (arr, total[arr], {})
+
+    def tt(out, a, b, o, r, w):
+        op("v", lambda: V.tensor_tensor(out, a, b, o), r, w)
+
+    def ts(out, a, s1, o1, r, w, s2=None, o2=None):
+        if o2 is None:
+            op("v", lambda: V.tensor_scalar(out, a, s1, None, o1), r, w)
+        else:
+            op("v", lambda: V.tensor_scalar(out, a, s1, s2, o1, o2), r, w)
+
+    def cp(out, a, r, w):
+        op("v", lambda: V.tensor_copy(out, a), r, w)
+
+    def ms(out, val, w):
+        op("v", lambda: V.memset(out, val), "", w)
+
+    def scan(out, a, b, init, o0, o1, r, w):
+        op("v", lambda: V.tensor_tensor_scan(out, a, b, init, o0, o1), r, w)
+
+    def act(out, a, f, r, w, **kw):
+        op("a", lambda: ACT.activation(out, a, f, **kw), r, w)
+
+    def quant(q, s, a, r, w):
+        op("v", lambda: V.quantize_mx(q, s, a), r, w)
+
+    def mm(bank, n, lq, ls, rq, rs, r, start=True, stop=True):
+        out = T.ps[:, 512 * bank:512 * bank + n]
+        if stop:
+            op("p", lambda: PE.matmul_mx(out, lq, ls, rq, rs, start, stop), r, "ps%d" % bank)
+        else:
+            issue("p", lambda: PE.matmul_mx(out, lq, ls, rq, rs, start, stop), r.split(), ["ps%d" % bank], None, 0)
+
+    def bank(b, lo, hi, step=1):
+        return T.ps[:, 512 * b + lo:512 * b + hi:step]
+
+    def iota(out, pat, base, cm, w, small=False):
+        if small:
+            op("g", lambda: g.iota(out, pat, base, cm, allow_small_or_imprecise_dtypes=True), "", w)
+        else:
+            op("g", lambda: g.iota(out, pat, base, cm), "", w)
+
+    def wrap_scan(out, a, n, r, w):
+        scan(out[:, 0:n], T.r16[:, 0:n], a[:, 0:n], -BIG, A.min, A.max, r + " r16", w)
+
+    dma("s", T.xin[:, 0:4 * H], T.x[:, 0:4 * H], w="X0.0")
+    dma("a", T.xin[:, 4 * H:], T.x[:, 4 * H:], w="X0.1")
+    dma("s", T.uin[:], T.u[:], w="uin")
+    dma("s", T.wq[:].bitcast(dt.uint8), T.wc[:], w="wq")
+    dma("s", T.wsc[:], T.ws[:], w="wsc")
+    dma("s", T.vin[:], T.v[:], w="vin")
+
+    iota(T.iul[:], [[16, 8]], 0, 0, "iul")
+    iota(T.iblk[:], [[-16, 8]], 0, 1, "iblk")
+    iota(T.iw[:], [[1023, C]], 1023, -1024, "iw")
+    iota(T.ip[:], [[0, 2]], 0, 1, "ip")
+    iota(T.iof[:], [[1, C]], 0, 0, "iof", True)
+    iota(T.bex[:], [[8 * S, 4]], 0, 0, "bex", True)
+    ms(T.ones[:], 1.0, "ones")
+    ms(T.r16[:], BIG, "r16")
+    ms(T.zt[:], 0.0, "zt")
+    cp(T.oul[:], T.iul[:], "iul", "oul")
+    ts(T.ibs[:], T.iblk[:], 4, A.arith_shift_right, "iblk", "ibs")
+    ms(T.r16[:, 0::16], -BIG, "r16")
+    ts(T.blk[:], T.ibs[:], 0.0, A.is_equal, "ibs", "blk")
+    ms(T.zt[:, 64::S], -1000.0, "zt")
+    ms(T.ct[:, 12 * H + 3::4], 0.0, "ct.15")
+    ms(T.et[:, 1024:], 0.0, "et.z")
+    ms(T.r01[:], 1.0, "r01")
+    ms(T.wt[:], 1.0, "wt")
+    ms(T.sv[:, 0:128], 1.0, "sv.0")
+    ms(T.sv[:, 128:], -1.0, "sv.1")
+    ms(T.r01[:, 0::16], 0.0, "r01")
+    ts(T.pw[:], T.iw[:], 16383, A.bitwise_and, "iw", "pw")
+    ts(T.ipa[:, 0:1], T.ip[:, 0:1], 15, A.bitwise_and, "ip", "ipa.0")
+    ts(T.ipa[:, 1:2], T.ip[:, 1:2], 1, A.bitwise_and, "ip", "ipa.1")
+    ts(T.km[:], T.pw[:, 0:H], 1024.0, A.is_ge, "pw", "km", -BIG, A.mult)
+    cp(T.pc[:, 0:2], T.ipa[:], "ipa.0 ipa.1", "pc.0")
+    for j in range(8):
+        act(T.ek[:, 64 * j:64 * j + 64], T.ones[:], F.Copy, "ones blk", "ek.%d" % j, scale=T.blk[:, j:j + 1])
+    quant(T.ekq[:], T.eks[:], T.ek[:], " ".join("ek.%d" % j for j in range(8)), "ekq")
+    quant(T.uq[:], T.us[:], T.uin[:], "uin", "uq")
+    cp(T.ur[:].bitcast(dt.uint32), T.uq[:].bitcast(dt.uint32).indirect(T.oul[:]), "uq oul", "ur")
+    act(T.urs[:], T.us[:].indirect(T.oul[:]), F.Copy, "uq oul", "urs")
+
+    later = [
+        lambda: ts(T.thr[:], T.iof[:, 0::16], T.pc[:, 0:1], A.add, "iof pc.0", "thr", 0.5, A.add),
+        lambda: ts(T.pc[:, 2:3], T.pc[:, 1:2], -2.0, A.mult, "pc.0", "pc.2", 1.0, A.add),
+        lambda: ts(T.pc[:, 3:4], T.pc[:, 1:2], float(TB + S // 2), A.mult, "pc.0", "pc.3", -1.0, A.add),
+        lambda: ts(T.pc[:, 4:5], T.pc[:, 0:1], float(S // 2), A.mult, "pc.0 pc.2", "pc.4", T.pc[:, 2:3], A.mult),
+        lambda: ms(T.ft[:, 0:S], 0.0, "ft.0"),
+        lambda: tt(T.pc[:, 5:6], T.pc[:, 4:5], T.pc[:, 3:4], A.add, "pc.3 pc.4", "pc.5"),
+        lambda: ts(T.ksg[:], T.pw[:, 0:128], 1024.0, A.is_lt, "pw pc.2", "ksg", T.pc[:, 2:3], A.mult),
+        lambda: ts(T.bs[:, 0:4], T.bex[:], T.pc[:, 2:3], A.mult, "bex pc.2 pc.5", "bs.0", T.pc[:, 5:6], A.add),
+        lambda: ms(T.wt[:, 0:K:2], 129.0 / 128.0, "wt"),
+        lambda: ts(T.bs[:, 4:8], T.bs[:, 0:4], -1.0, A.mult, "bs.0", "bs.1", float(TB - 2), A.add),
+        lambda: ts(T.bs[:, 8:12], T.bs[:, 0:4], -1.0, A.add, "bs.0", "bs.2"),
+        lambda: ms(T.ut[:, K:K + 1], float(C - 1), "ut.e"),
+        lambda: ms(T.wt[:, K + 1::2], 129.0 / 128.0, "wt"),
+    ]
+
+    def fill(n):
+        for _ in range(min(n, len(later))):
+            later.pop(0)()
+
+    xs = [T.xin, T.x1, T.x2]
+
+    def quant_state(t, h):
+        quant(T["tq%d" % t][:, H * h:H * h + H], T["ts%d" % t][:, H * h:H * h + H],
+              xs[t][:, 4 * H * h:4 * H * (h + 1)], "X%d.%d" % (t, h) if t == 0 else
+              " ".join("X%d.%d.%d" % (t, h, b) for b in range(4)), "tq%d.%d" % (t, h))
+
+    def score(t, h):
+        mm(h, H, T.ur[:], T.urs[:], T["tq%d" % t][:, H * h:H * h + H], T["ts%d" % t][:, H * h:H * h + H],
+           "ur urs tq%d.%d" % (t, h))
+        act(T.so[:, 112 * h:112 * h + 112], bank(h, 1, H, 2), F.Copy, "ps%d" % h, "so.%d" % h)
+
+    def compare(src, n, w, wname, sname, tile, tname, tmp, tmpname, acols, eqslot):
+        def slot(s, lo, hi):
+            o = 4 * n * (s // 4)
+            return tile[:, o + s % 4 + 4 * lo:o + 4 * hi:4]
+
+        def second(k):
+            s, c = acols[k]
+            m = 16 * c + 16
+            act(slot(s, 0, m), tmp[:, n * k:n * k + m], F.Relu, "%s.%d" % (tmpname, k), "%s.%d.0" % (tname, s))
+            if m < n:
+                act(slot(s, m, n), tmp[:, n * k + m:n * k + n], F.Sign, "%s.%d" % (tmpname, k),
+                    "%s.%d.1" % (tname, s), bias=1.0)
+        for k, (s, c) in enumerate(acols):
+            act(tmp[:, n * k:n * k + n], src[:, 0:n], F.Sign, sname + " " + wname, "%s.%d" % (tmpname, k),
+                scale=-1.0, bias=w[:, 16 * c + 15:16 * c + 16])
+            if k:
+                second(k - 1)
+        second(len(acols) - 1)
+
+        def vcol(s, c):
+            m = 16 * c + 16
+            sc = w[:, 16 * c + 15:16 * c + 16]
+            ts(slot(s, 0, m), src[:, 0:m], sc, A.is_lt, sname + " " + wname, "%s.%d.0" % (tname, s))
+            if m < n:
+                ts(slot(s, m, n), src[:, m:n], sc, A.is_le, sname + " " + wname, "%s.%d.1" % (tname, s))
+
+        def eqs():
+            tt(slot(eqslot, 0, n), src[:, 0:n], w[:, 0:n], A.is_equal, sname + " " + wname,
+               "%s.%d.0" % (tname, eqslot))
+        return vcol, eqs
+
+    def names(tname, q):
+        return " ".join("%s.%d.%d" % (tname, s, i) for s in range(4 * q, 4 * q + 4) for i in range(2))
+
+    for h in range(2):
+        quant_state(0, h)
+        score(0, h)
+    fill(1)
+
+    for t in range(2):
+        tq, tsc, lq, ls = T["tq%d" % t], T["ts%d" % t], T["lq%d" % t], T["ls%d" % t]
+        ra, ht, lra, lh, tb = T["ra%d" % t], T["ht%d" % t], T["lr%d" % t], T["lh%d" % t], T["tb%d" % t]
+        send(t, [(lq[:].bitcast(dt.uint8), tq[:].bitcast(dt.uint8)), (ls[:], tsc[:])],
+             "tq%d.0 tq%d.1" % (t, t), "ar%d" % (3 * t), "lq")
+        if t == 0:
+            clear_table(0, "lq")
+            iota(T.eb[:], [[0, 2048]], 0, 0, "eb", True)
+            for b in range(4):
+                v = T.eb[:, 512 * b + b:512 * b + 512:4]
+                op("g", lambda: g.affine_select(v, v, [[-1, 128]], A.not_equal, 1.0, 0, 1), "eb", "eb.%d" % b)
+
+        for h in range(2):
+            v = slice(112 * h, 112 * h + 112)
+            tt(T.mx[:, v], bank(h, 0, H, 2), T.so[:, v], A.max, "ps%d so.%d" % (h, h), "mx.%d" % h)
+            tt(T.am[:, v], T.mx[:, v], T.km[:, v], A.add, "mx.%d km" % h, "am.%d" % h)
+        wrap_scan(T.wm, T.am, H, "am.0 am.1", "wm")
+        vcol, eqs = compare(T.mx, H, T.wm, "wm", "mx.0 mx.1", T.ct, "ct", T.sg, "sg",
+                            [(8 + i, c) for i, c in enumerate([0, 1, 2, 10, 11, 12])], 14)
+        for h in range(2):
+            act(T.se[:, 112 * h:112 * h + 112], bank(h, 0, H, 2), F.Copy, "ps%d" % h, "se.%d" % h)
+
+        def tile1(q):
+            quant(T.cq[:, H * q:H * q + H], T.cs[:, H * q:H * q + H], T.ct[:, 4 * H * q:4 * H * (q + 1)],
+                  names("ct", q) + " ct.15", "cq.%d" % q)
+            mm(2, H, T.ekq[:], T.eks[:], T.cq[:, H * q:H * q + H], T.cs[:, H * q:H * q + H], "ekq cq.%d" % q,
+               q == 0, q == 3)
+        for s, c in enumerate([3, 4, 5, 6, 7, 8, 9, 13]):
+            vcol(s, c)
+            if s == 4:
+                tile1(0)
+        eqs()
+        tile1(1)
+        tile1(2)
+        tile1(3)
+        fill(4)
+
+        ts(T.f1[:], bank(2, 0, H), 64.5, A.is_le, "ps2", "f1")
+        scan(T.p1[:], T.f1[:], T.f1[:], 0.0, A.add, A.max, "f1", "p1")
+        for c in range(2):
+            act(T.jk[:, 192 * c:192 * c + 192], T.p1[:, 0:192], F.Sign, "p1 thr", "acc.%d" % c, scale=-1.0,
+                bias=T.thr[:, c:c + 1], accum_out=T.acc[:, c:c + 1])
+        for c in range(2):
+            ts(T.cb[:, 192 * c:192 * c + 192], T.p1[:, 32:H], T.thr[:, 2 + c:3 + c], A.is_lt, "p1 thr", "cb.%d" % c)
+        for c in range(2):
+            v = T.cb[:, 192 * c:192 * c + 192]
+            scan(T.cn[:, 192 * c:192 * c + 192], v, v, 32.0, A.add, A.max, "cb.%d" % c, "cn.%d" % c)
+        cp(T.oa[:, 2:4], T.cn[:, 191::192], "cn.0 cn.1", "oa.1")
+        ts(T.oa[:, 0:2], T.acc[:], 0.5, A.mult, "acc.0 acc.1", "oa.0", 96.0, A.add)
+        act(T.cd[:, 1::2], T.so[:].indirect(T.oa[:]), F.Copy, "so.0 so.1 oa.0 oa.1", "cd.1")
+        cp(T.cd[:, 0::2], T.se[:].indirect(T.oa[:]), "se.0 se.1 oa.0 oa.1", "cd.0")
+        act(T.col[:, 0::2], T.iof[:].indirect(T.oa[:]), F.Identity, "iof oa.0 oa.1", "col.0", scale=2.0)
+        act(T.col[:, 1::2], T.iof[:].indirect(T.oa[:]), F.Identity, "iof oa.0 oa.1", "col.1", scale=2.0, bias=1.0)
+
+        tt(T.a2[:], T.cd[:], T.km[:, 0:128], A.add, "cd.0 cd.1 km", "a2")
+        wrap_scan(T.w2, T.a2, 128, "a2", "w2")
+        vcol, eqs = compare(T.cd, 128, T.w2, "w2", "cd.0 cd.1", T.et, "et", T.sg2, "sh",
+                            [(4, 0), (5, 1), (6, 5), (7, 6)], 8)
+
+        def tile2(q, first, last):
+            quant(T.eq[:, 128 * q:128 * q + 128], T.es[:, 128 * q:128 * q + 128], T.et[:, 512 * q:512 * q + 512],
+                  names("et", q) + " et.z", "eq.%d" % q)
+            mm(3, 128, T.ekq[:], T.eks[:], T.eq[:, 128 * q:128 * q + 128], T.es[:, 128 * q:128 * q + 128],
+               "ekq eq.%d" % q, first, last)
+        eqs()
+        for s, c in enumerate([7, 3, 4, 2]):
+            vcol(s, c)
+            if s == 0:
+                tile2(2, True, False)
+        tile2(0, False, False)
+        tile2(1, False, True)
+        fill(4)
+        tt(T.a3[:], bank(3, 0, 128), T.km[:, 0:128], A.add, "ps3 km", "a3")
+        ts(T.f2[:], bank(3, 0, 128), 64.5, A.is_le, "ps3", "f2")
+        wrap_scan(T.w3, T.a3, 128, "a3", "w3")
+        scan(T.p2[:], T.f2[:], T.f2[:], 0.0, A.add, A.max, "f2", "p2")
+        ts(T.or2[:], T.w3[:, 15::16], -1.0, A.add, "w3", "or2")
+        cp(ra[:].indirect(T.or2[:]), T.p2[:], "p2 or2", "ra%d" % t)
+        send(t, [(lra[:], ra[:, 0:K])], "ra%d" % t, "ar%d" % (3 * t + 1), "lra")
+
+        tt(T.a3[:, 0:K], ra[:, 0:K], T.km[:, 0:K], A.add, "ra%d km" % t, "a3")
+        cp(ht[:].indirect(T.or2[:]), T.col[:], "col.0 col.1 or2", "ht%d" % t)
+        send(t, [(lh[:], ht[:, 0:K])], "ht%d" % t, "ar%d" % (3 * t + 2), "lh")
+        if t == 0:
+            clear_table(1, "lh")
+        wrap_scan(T.w3, T.a3, K, "a3", "w3")
+        ts(T.ora[:], T.w3[:, 15:K:16], -1.0, A.add, "w3", "ora")
+        cp(T.kt[:].indirect(T.ora[:]), T.iof[:, 0:K], "iof ora", "kt")
+        tt(T.a3[:, 0:K], T.kt[:], T.km[:, 0:K], A.add, "kt km", "a3")
+        tt(T.a3[:, K::2], T.kt[:, 1::2], T.km[:, 0:K:2], A.add, "kt km", "a3.1")
+        tt(T.a3[:, K + 1::2], T.kt[:, 0::2], T.km[:, 1:K:2], A.add, "kt km", "a3.2")
+        cp(T.at[:].indirect(T.ora[:]), ht[:, 0:K], "ht%d ora" % t, "at")
+        wrap_scan(T.w3, T.a3, 128, "a3 a3.1 a3.2", "w3")
+        fill(1)
+        cp(T.ok[:], T.w3[:, 15::16], "w3", "ok")
+        fill(9)
+        for c in range(28):
+            act(T.jv[:, K * c:K * c + K], T.at[:], F.Sign, "at thr", "va.%d" % c, scale=-1.0,
+                bias=T.thr[:, c:c + 1], accum_out=T.vacc[:, c:c + 1])
+        act(T.bm[:, 0:K], lh[:].indirect(T.ok[:, 0:4]), F.Identity, "lh ok", "bm.0", bias=-1.0)
+        act(T.bm[:, K:], lh[:].indirect(T.ok[:, 0:4]), F.Identity, "lh ok", "bm.1", bias=1023.0)
+        act(T.xh[:], xs[t][:], F.Copy, "X0.0 X0.1" if t == 0 else
+            " ".join("X1.%d.%d" % (h, b) for h in range(2) for b in range(4)), "xh", scale=0.5)
+
+        def unpack():
+            for b in range(4):
+                mm(4 + b, C, T.ebq[:, 128 * b:128 * b + 128], T.ebs[:, 128 * b:128 * b + 128], lq[:], ls[:], "ebq lq")
+                act(T.dh[:, C * b:C * b + C], bank(4 + b, 0, C), F.Copy, "ps%d" % (4 + b), "dh.%d" % b, scale=0.5)
+
+        sx, sm = T.w4[:, 15:K:16], T.sm
+        tt(T.a4[:], lra[:].indirect(T.ok[:]), T.ksg[:], A.mult, "lra ok ksg", "a4")
+        scan(T.w4[:], T.r01[:], T.a4[:], 0.0, A.mult, A.add, "r01 a4", "w4")
+        tt(sm[:, 0:4], sx, T.w4[:, K + 15::16], A.subtract, "w4", "sm.0")
+        tt(sm[:, 4:8], T.bs[:, 4:8], sx, A.subtract, "w4 bs.1", "sm.1")
+        tt(sm[:, 8:12], T.bs[:, 8:12], sx, A.add, "w4 bs.2", "sm.2")
+        ts(sm[:, 12:16], sm[:, 0:4], 1.0, A.is_equal, "sm.0", "sm.3", float(TB), A.mult)
+        ts(sm[:, 16:20], sm[:, 0:4], 1.5, A.is_le, "sm.0", "sm.4", float(2 * TB), A.mult)
+        tt(sm[:, 20:24], T.bs[:, 0:4], sx, A.add, "w4 bs.0", "sm.5")
+        tt(sm[:, 24:32], sm[:, 4:12], sm[:, 12:20], A.add, "sm.1 sm.2 sm.3 sm.4", "sm.6")
+        cp(T.od[:], sm[:, 20:32], "sm.5 sm.6", "od")
+        cp(tb[:].indirect(T.od[:]), T.sv[:], "od sv.0 sv.1 tb%d" % t, "tb%d" % t)
+        side = {
+            0: lambda: ts(sm[:, 32:36], sm[:, 0:4], 1.0, A.is_equal, "sm.0", "sm.7"),
+            1: lambda: ts(T.oe[:, 0:4], sm[:, 20:24], float(S), A.add, "sm.5", "oe.0"),
+            2: lambda: tt(sm[:, 36:40], sm[:, 32:36], sm[:, 4:8], A.add, "sm.7 sm.1", "sm.8"),
+            4: lambda: ts(T.oe[:, 4:8], sm[:, 36:40], float(S), A.add, "sm.8", "oe.1"),
+            20: lambda: ts(T.ov[:], T.vacc[:], 0.5, A.mult, " ".join("va.%d" % c for c in range(28)), "ov",
+                           32.0, A.add),
+            22: lambda: tt(T.dl[:], T.bm[:, K:], T.at[:], A.subtract, "bm.1 at", "dl"),
+        }
+        if t == 0:
+            quant(T.ebq[:], T.ebs[:], T.eb[:], "eb.0 eb.1 eb.2 eb.3", "ebq")
+        unpack()
+        for k in range(32):
+            scan(T.ft[:, S * (k + 1):S * (k + 2)], tb[:, S * k:S * (k + 1)], T.ft[:, S * k:S * (k + 1)], 0.0,
+                 A.add, A.max, "tb%d ft.%d" % (t, k), "ft.%d" % (k + 1))
+            if k in side:
+                side[k]()
+
+        fts = " ".join("ft.%d" % k for k in range(33))
+        tt(T.lr[:], T.ft[:].indirect(T.oe[:]), T.wt[:], A.mult, fts + " oe.0 oe.1 wt", "lr")
+        ts(T.pm[:, 0:1], T.ft[:, 32 * S + 63:32 * S + 64], 1.0, A.add, "ft.32", "pm.0")
+        tt(T.key[:], T.lr[:, 0:K], T.lr[:, K:], A.add, "lr", "key")
+        scan(T.pm[:, 1:], T.key[:], T.key[:], T.pm[:, 0:1], A.max, A.max, "key pm.0", "pm.1")
+        cc = T.cc
+        tt(cc[:, 0:K], T.pm[:, 1:], T.pm[:, 0:K], A.is_gt, "pm.0 pm.1", "cc.0")
+        tt(cc[:, K:2 * K], T.pm[:, 1:], T.pm[:, 0:K], A.is_le, "pm.0 pm.1", "cc.1")
+        tt(cc[:, 2 * K:3 * K], cc[:, 0:K], T.dl[:], A.mult, "cc.0 dl", "cc.2")
+        tt(cc[:, 3 * K:], cc[:, 0:K], T.bm[:, 0:K], A.mult, "cc.0 bm.0", "cc.3")
+        scan(T.zz[:, 1:65], cc[:, 2 * K - 1:K - 1:-1], cc[:, 3 * K - 1:2 * K - 1:-1], 0.0, A.mult, A.add,
+             "cc.1 cc.2", "zz.0")
+        scan(T.ut[:, K - 1::-1], cc[:, 2 * K - 1:K - 1:-1], cc[:, 4 * K - 1:3 * K - 1:-1], float(C - 1), A.mult, A.add,
+             "cc.1 cc.3", "ut")
+        scan(T.zz[:, 65:], cc[:, K:2 * K], cc[:, 2 * K:3 * K], T.zz[:, 64:65], A.mult, A.add, "cc.1 cc.2 zz.0", "zz.1")
+        act(T.ug[:], T.ut[:].indirect(T.ov[:]), F.Copy, "ut ut.e ov", "ug")
+        tt(T.fw[:], T.zz[:, 64:].indirect(T.ov[:]), T.pw[:], A.subtract, "zz.0 zz.1 ov pw", "fw")
+        scan(T.qs[:], T.fw[:], T.ug[:], 0.0, A.max, A.min, "fw ug", "qs")
+        cp(T.oqo[:], T.qs[:, 15::16], "qs", "oqo")
+        qr = T["qr%d" % t]
+        act(qr[:], T.iof[:].indirect(T.oqo[:]), F.Copy, "iof oqo", "qr%d" % t)
+        dma("s", T.oq[:, C * t:C * t + C], qr[0:128:16, :], r="qr%d" % t)
+
+        xn = xs[t + 1]
+        for h in range(2):
+            for b in range(4):
+                v = slice(4 * H * h + b, 4 * H * (h + 1), 4)
+                tt(T.gt[:, v], T.dh[:, C * b:C * b + C].indirect(T.oqo[:, 14 * h:14 * h + 14]), T.xh[:, v], A.add,
+                   "dh.%d oqo xh" % b, "gt.%d.%d" % (h, b))
+            quant(T.gq[:, H * h:H * h + H], T.gs[:, H * h:H * h + H], T.gt[:, 4 * H * h:4 * H * (h + 1)],
+                  " ".join("gt.%d.%d" % (h, b) for b in range(4)), "gq.%d" % h)
+            for b in range(4):
+                mm(4 * h + b, H, T.wq[:, 128 * b:128 * b + 128], T.wsc[:, 128 * b:128 * b + 128],
+                   T.gq[:, H * h:H * h + H], T.gs[:, H * h:H * h + H], "wq wsc gq.%d" % h)
+                act(T.rl[:, C * b + H * h:C * b + H * h + H], bank(4 * h + b, 0, H), F.Relu, "ps%d" % (4 * h + b),
+                    "rl.%d.%d" % (h, b), scale=0.015625)
+        for h in range(2):
+            for b in range(4):
+                v = slice(4 * H * h + b, 4 * H * (h + 1), 4)
+                tt(xn[:, v], T.gt[:, v], T.rl[:, C * b + H * h:C * b + H * h + H], A.add,
+                   "gt.%d.%d rl.%d.%d" % (h, b, h, b), "X%d.%d.%d" % (t + 1, h, b))
+            if t == 1 and h == 0:
+                quant(T.vq[:], T.vs[:], T.vin[:], "vin", "vq")
+            quant_state(t + 1, h)
+            if t == 0:
+                score(1, h)
+            else:
+                lo, hi = H * h, H * h + H
+                mm(h, H, T.vq[:], T.vs[:], T.tq2[:, lo:hi], T.ts2[:, lo:hi], "vq tq2.%d" % h)
+                dma("s", T.oc[:, 4 * lo:4 * hi], T.tq2[:, lo:hi].bitcast(dt.uint8), r="tq2.%d" % h)
+                act(T.ysb[:, lo:hi], bank(h, 0, H), F.Copy, "ps%d" % h, "ysb.%d" % h)
+                dma("a", T.y[:, lo:hi], T.ysb[:, lo:hi], r="ysb.%d" % h)
+    for k in range(4):
+        dma("s", T.osc[4 * k:4 * k + 4, :], T.ts2[32 * k:32 * k + 4, :], r="tq2.0 tq2.1")
+
+    for s in total:
+        if waited.get(s, 0) < total[s]:
+            g.wait_ge(T.sem[s], total[s])

@@ -22,12 +22,13 @@ SCRATCH = {
     "eks": _sb(128, U8),
     "ct": _sb(16 * H, BF), "cq": _sb(4 * H, X4), "cs": _sb(4 * H, U8), "sg": _sb(6 * H, BF),
     "et": _sb(12 * 128, BF), "eq": _sb(3 * 128, X4), "es": _sb(3 * 128, U8), "sg2": _sb(4 * 128, BF),
-    "iw": _sb(C, I32), "pw": _sb(C, I32), "km": _sb(H, F32), "r16": _sb(H, F32), "r01": _sb(128, F32),
-    "iof": _sb(C, F32), "iblk": _sb(8, I32), "ibs": _sb(8, I32), "blk": _sb(8, F32), "ones": _sb(64, BF),
-    "iul": _sb(8, I32), "oul": _sb(8, U16), "ip": _sb(2, I32), "ipa": _sb(2, I32), "pc": _sb(8, F32),
+    "iw": _sb(C, I32), "pw": _sb(C, I32), "km": _sb(128, F32), "k2": _sb(H, F32), "r32": _sb(H, F32),
+    "rp": _sb(H, F32), "r16": _sb(128, F32), "r01": _sb(128, F32),
+    "iof": _sb(C, F32), "isml": _sb(32, I32), "blk": _sb(8, F32), "ones": _sb(64, BF),
+    "oul": _sb(8, U16), "pc": _sb(8, F32),
     "thr": _sb(28, F32), "bex": _sb(4, F32), "bs": _sb(12, F32), "ksg": _sb(128, F32), "wt": _sb(128, F32),
     "sv": _sb(192, BF), "zt": _sb(4 * S, BF),
-    "mx": _sb(H, F32), "am": _sb(H, F32), "wm": _sb(H, F32), "se": _sb(H, F32), "so": _sb(H, F32),
+    "mx": _sb(C, F32), "am": _sb(C, F32), "wm": _sb(C, F32), "se": _sb(H, F32), "so": _sb(H, F32),
     "f1": _sb(H, BF), "p1": _sb(H, BF), "cb": _sb(384, BF), "cn": _sb(384, BF), "jk": _sb(384, BF),
     "jv": _sb(28 * K, BF), "acc": _sb(2, F32), "oa": _sb(4, U16), "cd": _sb(128, F32), "col": _sb(128, F32),
     "a2": _sb(128, F32), "w2": _sb(128, F32), "f2": _sb(128, BF), "p2": _sb(128, BF), "a3": _sb(128, F32),
@@ -38,7 +39,7 @@ SCRATCH = {
     "ov": _sb(28, U16),
     "a4": _sb(128, F32), "w4": _sb(128, F32), "sm": _sb(40, F32), "od": _sb(12, U16),
     "oe": _sb(8, U16), "tb0": _sb(3 * TB + 16, BF), "tb1": _sb(3 * TB + 16, BF), "ft": _sb(33 * S, BF),
-    "lr": _sb(128, F32), "key": _sb(K, F32), "pm": _sb(K + 1, F32), "cc": _sb(4 * K, F32), "bm": _sb(2 * K, F32),
+    "lr": _sb(128, F32), "key": _sb(K, F32), "pm": _sb(K + 1, F32), "cc": _sb(6 * K, F32), "bm": _sb(2 * K, F32),
     "dl": _sb(K, F32), "zz": _sb(129, F32), "ut": _sb(K + 1, F32), "fw": _sb(C, F32), "ug": _sb(C, F32),
     "qs": _sb(C, F32), "oqo": _sb(28, U16), "qr0": _sb(C, F32), "qr1": _sb(C, F32),
     "ps": ("psum", [128, 4096], F32),
@@ -77,10 +78,12 @@ def rank_program(g, core, T, topo):
             c[s] = val
 
     def issue(q, fn, r, w, sem, inc):
-        w = list(w) + [n for n in r if n.startswith("ps")]
-        toks = [wrote[n] for n in list(r) + w if n in wrote]
+        toks = [wrote[n] for n in list(r) + list(w) if n in wrote]
         for n in w:
             toks += readers.get(n, [])
+        for n in r:
+            if n.startswith("ps"):
+                toks += [k for k in readers.get(n, []) if k[0] != sem]
         need(q, toks)
         ins = fn()
         if inc:
@@ -165,49 +168,56 @@ def rank_program(g, core, T, topo):
     dma("s", T.wsc[:], T.ws[:], w="wsc")
     dma("s", T.vin[:], T.v[:], w="vin")
 
-    iota(T.iul[:], [[16, 8]], 0, 0, "iul")
-    iota(T.iblk[:], [[-16, 8]], 0, 1, "iblk")
+    iul, iblk, ibs, ip, ipa = T.isml[:, 0:8], T.isml[:, 8:16], T.isml[:, 16:24], T.isml[:, 24:25], T.isml[:, 26:28]
+    iota(iul, [[16, 8]], 0, 0, "iul")
+    iota(iblk, [[-16, 8]], 0, 1, "iblk")
     iota(T.iw[:], [[1023, C]], 1023, -1024, "iw")
-    iota(T.ip[:], [[0, 2]], 0, 1, "ip")
+    iota(ip, [[0, 1]], 0, 1, "ip")
     iota(T.iof[:], [[1, C]], 0, 0, "iof", True)
     iota(T.bex[:], [[8 * S, 4]], 0, 0, "bex", True)
     ms(T.ones[:], 1.0, "ones")
-    ms(T.r16[:], BIG, "r16")
+    ms(T.r32[:], BIG, "r32")
     ms(T.zt[:], 0.0, "zt")
-    cp(T.oul[:], T.iul[:], "iul", "oul")
-    ts(T.ibs[:], T.iblk[:], 4, A.arith_shift_right, "iblk", "ibs")
-    ms(T.r16[:, 0::16], -BIG, "r16")
-    ts(T.blk[:], T.ibs[:], 0.0, A.is_equal, "ibs", "blk")
+    cp(T.oul[:], iul, "iul", "oul")
+    ts(ibs, iblk, 4, A.arith_shift_right, "iblk", "ibs")
+    ms(T.r32[:, 0::32], -BIG, "r32")
     ms(T.zt[:, 64::S], -1000.0, "zt")
+    ts(T.blk[:], ibs, 0.0, A.is_equal, "ibs", "blk")
+    ms(T.rp[:, 0::2], -BIG, "rp.0")
+    ms(T.rp[:, 1::2], BIG, "rp.1")
     ms(T.ct[:, 12 * H + 3::4], 0.0, "ct.15")
-    ms(T.et[:, 1024:], 0.0, "et.z")
+    ms(T.r16[:], BIG, "r16")
     ms(T.r01[:], 1.0, "r01")
-    ms(T.wt[:], 1.0, "wt")
-    ms(T.sv[:, 0:128], 1.0, "sv.0")
-    ms(T.sv[:, 128:], -1.0, "sv.1")
-    ms(T.r01[:, 0::16], 0.0, "r01")
     ts(T.pw[:], T.iw[:], 16383, A.bitwise_and, "iw", "pw")
-    ts(T.ipa[:, 0:1], T.ip[:, 0:1], 15, A.bitwise_and, "ip", "ipa.0")
-    ts(T.ipa[:, 1:2], T.ip[:, 1:2], 1, A.bitwise_and, "ip", "ipa.1")
-    ts(T.km[:], T.pw[:, 0:H], 1024.0, A.is_ge, "pw", "km", -BIG, A.mult)
-    cp(T.pc[:, 0:2], T.ipa[:], "ipa.0 ipa.1", "pc.0")
+    ts(T.isml[:, 26:27], ip, 15, A.bitwise_and, "ip", "ipa.0")
+    ts(T.isml[:, 27:28], ip, 1, A.bitwise_and, "ip", "ipa.1")
+    for e in range(2):
+        ts(T.k2[:, e::2], T.pw[:, 0:112], 1024.0, A.is_ge, "pw", "k2.%d" % e, -BIG, A.mult)
+    cp(T.pc[:, 0:2], ipa, "ipa.0 ipa.1", "pc.0")
     for j in range(8):
         act(T.ek[:, 64 * j:64 * j + 64], T.ones[:], F.Copy, "ones blk", "ek.%d" % j, scale=T.blk[:, j:j + 1])
-    quant(T.ekq[:], T.eks[:], T.ek[:], " ".join("ek.%d" % j for j in range(8)), "ekq")
     quant(T.uq[:], T.us[:], T.uin[:], "uin", "uq")
+    quant(T.ekq[:], T.eks[:], T.ek[:], " ".join("ek.%d" % j for j in range(8)), "ekq")
     cp(T.ur[:].bitcast(dt.uint32), T.uq[:].bitcast(dt.uint32).indirect(T.oul[:]), "uq oul", "ur")
     act(T.urs[:], T.us[:].indirect(T.oul[:]), F.Copy, "uq oul", "urs")
 
     later = [
         lambda: ts(T.thr[:], T.iof[:, 0::16], T.pc[:, 0:1], A.add, "iof pc.0", "thr", 0.5, A.add),
+        lambda: ts(T.km[:], T.pw[:, 0:128], 1024.0, A.is_ge, "pw", "km", -BIG, A.mult),
+        lambda: ms(T.r16[:, 0::16], -BIG, "r16"),
+        lambda: ms(T.et[:, 1024:], 0.0, "et.z"),
         lambda: ts(T.pc[:, 2:3], T.pc[:, 1:2], -2.0, A.mult, "pc.0", "pc.2", 1.0, A.add),
         lambda: ts(T.pc[:, 3:4], T.pc[:, 1:2], float(TB + S // 2), A.mult, "pc.0", "pc.3", -1.0, A.add),
+        lambda: ms(T.r01[:, 0::16], 0.0, "r01"),
         lambda: ts(T.pc[:, 4:5], T.pc[:, 0:1], float(S // 2), A.mult, "pc.0 pc.2", "pc.4", T.pc[:, 2:3], A.mult),
         lambda: ms(T.ft[:, 0:S], 0.0, "ft.0"),
+        lambda: ms(T.wt[:], 1.0, "wt"),
         lambda: tt(T.pc[:, 5:6], T.pc[:, 4:5], T.pc[:, 3:4], A.add, "pc.3 pc.4", "pc.5"),
         lambda: ts(T.ksg[:], T.pw[:, 0:128], 1024.0, A.is_lt, "pw pc.2", "ksg", T.pc[:, 2:3], A.mult),
+        lambda: ms(T.sv[:, 0:128], 1.0, "sv.0"),
         lambda: ts(T.bs[:, 0:4], T.bex[:], T.pc[:, 2:3], A.mult, "bex pc.2 pc.5", "bs.0", T.pc[:, 5:6], A.add),
         lambda: ms(T.wt[:, 0:K:2], 129.0 / 128.0, "wt"),
+        lambda: ms(T.sv[:, 128:], -1.0, "sv.1"),
         lambda: ts(T.bs[:, 4:8], T.bs[:, 0:4], -1.0, A.mult, "bs.0", "bs.1", float(TB - 2), A.add),
         lambda: ts(T.bs[:, 8:12], T.bs[:, 0:4], -1.0, A.add, "bs.0", "bs.2"),
         lambda: ms(T.ut[:, K:K + 1], float(C - 1), "ut.e"),
@@ -228,9 +238,11 @@ def rank_program(g, core, T, topo):
     def score(t, h):
         mm(h, H, T.ur[:], T.urs[:], T["tq%d" % t][:, H * h:H * h + H], T["ts%d" % t][:, H * h:H * h + H],
            "ur urs tq%d.%d" % (t, h))
-        act(T.so[:, 112 * h:112 * h + 112], bank(h, 1, H, 2), F.Copy, "ps%d" % h, "so.%d" % h)
 
-    def compare(src, n, w, wname, sname, tile, tname, tmp, tmpname, acols, eqslot):
+    def compare(src, step, n, w, wname, sname, tile, tname, tmp, tmpname, acols, eqslot):
+        def view(buf, lo, hi):
+            return buf[:, step * lo + step - 1:step * hi:step]
+
         def slot(s, lo, hi):
             o = 4 * n * (s // 4)
             return tile[:, o + s % 4 + 4 * lo:o + 4 * hi:4]
@@ -243,21 +255,22 @@ def rank_program(g, core, T, topo):
                 act(slot(s, m, n), tmp[:, n * k + m:n * k + n], F.Sign, "%s.%d" % (tmpname, k),
                     "%s.%d.1" % (tname, s), bias=1.0)
         for k, (s, c) in enumerate(acols):
-            act(tmp[:, n * k:n * k + n], src[:, 0:n], F.Sign, sname + " " + wname, "%s.%d" % (tmpname, k),
-                scale=-1.0, bias=w[:, 16 * c + 15:16 * c + 16])
+            e = step * (16 * c + 16)
+            act(tmp[:, n * k:n * k + n], view(src, 0, n), F.Sign, sname + " " + wname, "%s.%d" % (tmpname, k),
+                scale=-1.0, bias=w[:, e - 1:e])
             if k:
                 second(k - 1)
         second(len(acols) - 1)
 
         def vcol(s, c):
             m = 16 * c + 16
-            sc = w[:, 16 * c + 15:16 * c + 16]
-            ts(slot(s, 0, m), src[:, 0:m], sc, A.is_lt, sname + " " + wname, "%s.%d.0" % (tname, s))
+            sc = w[:, step * m - 1:step * m]
+            ts(slot(s, 0, m), view(src, 0, m), sc, A.is_lt, sname + " " + wname, "%s.%d.0" % (tname, s))
             if m < n:
-                ts(slot(s, m, n), src[:, m:n], sc, A.is_le, sname + " " + wname, "%s.%d.1" % (tname, s))
+                ts(slot(s, m, n), view(src, m, n), sc, A.is_le, sname + " " + wname, "%s.%d.1" % (tname, s))
 
         def eqs():
-            tt(slot(eqslot, 0, n), src[:, 0:n], w[:, 0:n], A.is_equal, sname + " " + wname,
+            tt(slot(eqslot, 0, n), view(src, 0, n), view(w, 0, n), A.is_equal, sname + " " + wname,
                "%s.%d.0" % (tname, eqslot))
         return vcol, eqs
 
@@ -267,7 +280,6 @@ def rank_program(g, core, T, topo):
     for h in range(2):
         quant_state(0, h)
         score(0, h)
-    fill(1)
 
     for t in range(2):
         tq, tsc, lq, ls = T["tq%d" % t], T["ts%d" % t], T["lq%d" % t], T["ls%d" % t]
@@ -282,14 +294,16 @@ def rank_program(g, core, T, topo):
                 op("g", lambda: g.affine_select(v, v, [[-1, 128]], A.not_equal, 1.0, 0, 1), "eb", "eb.%d" % b)
 
         for h in range(2):
-            v = slice(112 * h, 112 * h + 112)
-            tt(T.mx[:, v], bank(h, 0, H, 2), T.so[:, v], A.max, "ps%d so.%d" % (h, h), "mx.%d" % h)
-            tt(T.am[:, v], T.mx[:, v], T.km[:, v], A.add, "mx.%d km" % h, "am.%d" % h)
-        wrap_scan(T.wm, T.am, H, "am.0 am.1", "wm")
-        vcol, eqs = compare(T.mx, H, T.wm, "wm", "mx.0 mx.1", T.ct, "ct", T.sg, "sg",
+            v = slice(H * h, H * h + H)
+            tt(T.am[:, v], bank(h, 0, H), T.k2[:], A.add, "ps%d k2.0 k2.1" % h, "am.%d" % h)
+            scan(T.mx[:, v], T.rp[:], bank(h, 0, H), -BIG, A.min, A.max, "ps%d rp.0 rp.1" % h, "mx.%d" % h)
+            scan(T.wm[:, v], T.r32[:], T.am[:, v], -BIG, A.min, A.max, "am.%d r32" % h, "wm.%d" % h)
+        fill(2)
+        vcol, eqs = compare(T.mx, 2, H, T.wm, "wm.0 wm.1", "mx.0 mx.1", T.ct, "ct", T.sg, "sg",
                             [(8 + i, c) for i, c in enumerate([0, 1, 2, 10, 11, 12])], 14)
         for h in range(2):
             act(T.se[:, 112 * h:112 * h + 112], bank(h, 0, H, 2), F.Copy, "ps%d" % h, "se.%d" % h)
+            act(T.so[:, 112 * h:112 * h + 112], bank(h, 1, H, 2), F.Copy, "ps%d" % h, "so.%d" % h)
 
         def tile1(q):
             quant(T.cq[:, H * q:H * q + H], T.cs[:, H * q:H * q + H], T.ct[:, 4 * H * q:4 * H * (q + 1)],
@@ -304,29 +318,36 @@ def rank_program(g, core, T, topo):
         tile1(1)
         tile1(2)
         tile1(3)
-        fill(4)
+        fill(5)
 
         ts(T.f1[:], bank(2, 0, H), 64.5, A.is_le, "ps2", "f1")
+        fill(2)
         scan(T.p1[:], T.f1[:], T.f1[:], 0.0, A.add, A.max, "f1", "p1")
+        fill(2)
         for c in range(2):
             act(T.jk[:, 192 * c:192 * c + 192], T.p1[:, 0:192], F.Sign, "p1 thr", "acc.%d" % c, scale=-1.0,
                 bias=T.thr[:, c:c + 1], accum_out=T.acc[:, c:c + 1])
         for c in range(2):
             ts(T.cb[:, 192 * c:192 * c + 192], T.p1[:, 32:H], T.thr[:, 2 + c:3 + c], A.is_lt, "p1 thr", "cb.%d" % c)
+        fill(1)
         for c in range(2):
             v = T.cb[:, 192 * c:192 * c + 192]
             scan(T.cn[:, 192 * c:192 * c + 192], v, v, 32.0, A.add, A.max, "cb.%d" % c, "cn.%d" % c)
-        cp(T.oa[:, 2:4], T.cn[:, 191::192], "cn.0 cn.1", "oa.1")
         ts(T.oa[:, 0:2], T.acc[:], 0.5, A.mult, "acc.0 acc.1", "oa.0", 96.0, A.add)
+        cp(T.oa[:, 2:4], T.cn[:, 191::192], "cn.0 cn.1", "oa.1")
+        fill(2)
+
+        act(T.cd[:, 0::2], T.se[:].indirect(T.oa[:]), F.Copy, "se.0 se.1 oa.0 oa.1", "cd.0")
         act(T.cd[:, 1::2], T.so[:].indirect(T.oa[:]), F.Copy, "so.0 so.1 oa.0 oa.1", "cd.1")
-        cp(T.cd[:, 0::2], T.se[:].indirect(T.oa[:]), "se.0 se.1 oa.0 oa.1", "cd.0")
+        tt(T.a2[:, 0::2], T.se[:].indirect(T.oa[:]), T.km[:, 0::2], A.add, "se.0 se.1 oa.0 oa.1 km", "a2.0")
+        tt(T.a2[:, 1::2], T.so[:].indirect(T.oa[:]), T.km[:, 1::2], A.add, "so.0 so.1 oa.0 oa.1 km", "a2.1")
+        fill(2)
+        wrap_scan(T.w2, T.a2, 128, "a2.0 a2.1", "w2")
+        fill(2)
+        vcol, eqs = compare(T.cd, 1, 128, T.w2, "w2", "cd.0 cd.1", T.et, "et", T.sg2, "sh",
+                            [(4, 0), (5, 1), (6, 6)], 8)
         act(T.col[:, 0::2], T.iof[:].indirect(T.oa[:]), F.Identity, "iof oa.0 oa.1", "col.0", scale=2.0)
         act(T.col[:, 1::2], T.iof[:].indirect(T.oa[:]), F.Identity, "iof oa.0 oa.1", "col.1", scale=2.0, bias=1.0)
-
-        tt(T.a2[:], T.cd[:], T.km[:, 0:128], A.add, "cd.0 cd.1 km", "a2")
-        wrap_scan(T.w2, T.a2, 128, "a2", "w2")
-        vcol, eqs = compare(T.cd, 128, T.w2, "w2", "cd.0 cd.1", T.et, "et", T.sg2, "sh",
-                            [(4, 0), (5, 1), (6, 5), (7, 6)], 8)
 
         def tile2(q, first, last):
             quant(T.eq[:, 128 * q:128 * q + 128], T.es[:, 128 * q:128 * q + 128], T.et[:, 512 * q:512 * q + 512],
@@ -334,14 +355,14 @@ def rank_program(g, core, T, topo):
             mm(3, 128, T.ekq[:], T.eks[:], T.eq[:, 128 * q:128 * q + 128], T.es[:, 128 * q:128 * q + 128],
                "ekq eq.%d" % q, first, last)
         eqs()
-        for s, c in enumerate([7, 3, 4, 2]):
+        for s, c in [(0, 7), (1, 3), (2, 4), (3, 2), (7, 5)]:
             vcol(s, c)
-            if s == 0:
+            if s == 1:
                 tile2(2, True, False)
         tile2(0, False, False)
         tile2(1, False, True)
-        fill(4)
-        tt(T.a3[:], bank(3, 0, 128), T.km[:, 0:128], A.add, "ps3 km", "a3")
+        fill(9)
+        tt(T.a3[:], bank(3, 0, 128), T.km[:], A.add, "ps3 km", "a3")
         ts(T.f2[:], bank(3, 0, 128), 64.5, A.is_le, "ps3", "f2")
         wrap_scan(T.w3, T.a3, 128, "a3", "w3")
         scan(T.p2[:], T.f2[:], T.f2[:], 0.0, A.add, A.max, "f2", "p2")
@@ -350,63 +371,61 @@ def rank_program(g, core, T, topo):
         send(t, [(lra[:], ra[:, 0:K])], "ra%d" % t, "ar%d" % (3 * t + 1), "lra")
 
         tt(T.a3[:, 0:K], ra[:, 0:K], T.km[:, 0:K], A.add, "ra%d km" % t, "a3")
-        cp(ht[:].indirect(T.or2[:]), T.col[:], "col.0 col.1 or2", "ht%d" % t)
-        send(t, [(lh[:], ht[:, 0:K])], "ht%d" % t, "ar%d" % (3 * t + 2), "lh")
-        if t == 0:
-            clear_table(1, "lh")
         wrap_scan(T.w3, T.a3, K, "a3", "w3")
         ts(T.ora[:], T.w3[:, 15:K:16], -1.0, A.add, "w3", "ora")
         cp(T.kt[:].indirect(T.ora[:]), T.iof[:, 0:K], "iof ora", "kt")
         tt(T.a3[:, 0:K], T.kt[:], T.km[:, 0:K], A.add, "kt km", "a3")
         tt(T.a3[:, K::2], T.kt[:, 1::2], T.km[:, 0:K:2], A.add, "kt km", "a3.1")
         tt(T.a3[:, K + 1::2], T.kt[:, 0::2], T.km[:, 1:K:2], A.add, "kt km", "a3.2")
-        cp(T.at[:].indirect(T.ora[:]), ht[:, 0:K], "ht%d ora" % t, "at")
         wrap_scan(T.w3, T.a3, 128, "a3 a3.1 a3.2", "w3")
-        fill(1)
         cp(T.ok[:], T.w3[:, 15::16], "w3", "ok")
-        fill(9)
+        cp(ht[:].indirect(T.or2[:]), T.col[:], "col.0 col.1 or2", "ht%d" % t)
+        send(t, [(lh[:], ht[:, 0:K])], "ht%d" % t, "ar%d" % (3 * t + 2), "lh")
+        if t == 0:
+            clear_table(1, "lh")
+        act(T.xh[:], xs[t][:], F.Copy, "X0.0 X0.1" if t == 0 else
+            " ".join("X1.%d.%d" % (h, b) for h in range(2) for b in range(4)), "xh", scale=0.5)
+
+        sx, sm = T.w4[:, 15:K:16], T.sm
+        tt(T.a4[:], lra[:].indirect(T.ok[:]), T.ksg[:], A.mult, "lra ok ksg", "a4")
+        cp(T.at[:].indirect(T.ora[:]), ht[:, 0:K], "ht%d ora" % t, "at")
+        scan(T.w4[:], T.r01[:], T.a4[:], 0.0, A.mult, A.add, "r01 a4", "w4")
         for c in range(28):
             act(T.jv[:, K * c:K * c + K], T.at[:], F.Sign, "at thr", "va.%d" % c, scale=-1.0,
                 bias=T.thr[:, c:c + 1], accum_out=T.vacc[:, c:c + 1])
         act(T.bm[:, 0:K], lh[:].indirect(T.ok[:, 0:4]), F.Identity, "lh ok", "bm.0", bias=-1.0)
         act(T.bm[:, K:], lh[:].indirect(T.ok[:, 0:4]), F.Identity, "lh ok", "bm.1", bias=1023.0)
-        act(T.xh[:], xs[t][:], F.Copy, "X0.0 X0.1" if t == 0 else
-            " ".join("X1.%d.%d" % (h, b) for h in range(2) for b in range(4)), "xh", scale=0.5)
-
-        def unpack():
-            for b in range(4):
-                mm(4 + b, C, T.ebq[:, 128 * b:128 * b + 128], T.ebs[:, 128 * b:128 * b + 128], lq[:], ls[:], "ebq lq")
-                act(T.dh[:, C * b:C * b + C], bank(4 + b, 0, C), F.Copy, "ps%d" % (4 + b), "dh.%d" % b, scale=0.5)
-
-        sx, sm = T.w4[:, 15:K:16], T.sm
-        tt(T.a4[:], lra[:].indirect(T.ok[:]), T.ksg[:], A.mult, "lra ok ksg", "a4")
-        scan(T.w4[:], T.r01[:], T.a4[:], 0.0, A.mult, A.add, "r01 a4", "w4")
         tt(sm[:, 0:4], sx, T.w4[:, K + 15::16], A.subtract, "w4", "sm.0")
         tt(sm[:, 4:8], T.bs[:, 4:8], sx, A.subtract, "w4 bs.1", "sm.1")
         tt(sm[:, 8:12], T.bs[:, 8:12], sx, A.add, "w4 bs.2", "sm.2")
+        tt(sm[:, 20:24], T.bs[:, 0:4], sx, A.add, "w4 bs.0", "sm.5")
         ts(sm[:, 12:16], sm[:, 0:4], 1.0, A.is_equal, "sm.0", "sm.3", float(TB), A.mult)
         ts(sm[:, 16:20], sm[:, 0:4], 1.5, A.is_le, "sm.0", "sm.4", float(2 * TB), A.mult)
-        tt(sm[:, 20:24], T.bs[:, 0:4], sx, A.add, "w4 bs.0", "sm.5")
+        ts(sm[:, 32:36], sm[:, 0:4], 1.0, A.is_equal, "sm.0", "sm.7")
+        ts(T.oe[:, 0:4], sm[:, 20:24], float(S), A.add, "sm.5", "oe.0")
         tt(sm[:, 24:32], sm[:, 4:12], sm[:, 12:20], A.add, "sm.1 sm.2 sm.3 sm.4", "sm.6")
+        tt(sm[:, 36:40], sm[:, 32:36], sm[:, 4:8], A.add, "sm.7 sm.1", "sm.8")
         cp(T.od[:], sm[:, 20:32], "sm.5 sm.6", "od")
+        ts(T.oe[:, 4:8], sm[:, 36:40], float(S), A.add, "sm.8", "oe.1")
         cp(tb[:].indirect(T.od[:]), T.sv[:], "od sv.0 sv.1 tb%d" % t, "tb%d" % t)
-        side = {
-            0: lambda: ts(sm[:, 32:36], sm[:, 0:4], 1.0, A.is_equal, "sm.0", "sm.7"),
-            1: lambda: ts(T.oe[:, 0:4], sm[:, 20:24], float(S), A.add, "sm.5", "oe.0"),
-            2: lambda: tt(sm[:, 36:40], sm[:, 32:36], sm[:, 4:8], A.add, "sm.7 sm.1", "sm.8"),
-            4: lambda: ts(T.oe[:, 4:8], sm[:, 36:40], float(S), A.add, "sm.8", "oe.1"),
-            20: lambda: ts(T.ov[:], T.vacc[:], 0.5, A.mult, " ".join("va.%d" % c for c in range(28)), "ov",
-                           32.0, A.add),
-            22: lambda: tt(T.dl[:], T.bm[:, K:], T.at[:], A.subtract, "bm.1 at", "dl"),
-        }
-        if t == 0:
-            quant(T.ebq[:], T.ebs[:], T.eb[:], "eb.0 eb.1 eb.2 eb.3", "ebq")
-        unpack()
+
+        def unpack(b):
+            v = slice(128 * b, 128 * b + 128)
+            if t == 0:
+                quant(T.ebq[:, v], T.ebs[:, v], T.eb[:, 512 * b:512 * b + 512], "eb.%d" % b, "ebq.%d" % b)
+            mm(4 + b, C, T.ebq[:, v], T.ebs[:, v], lq[:], ls[:], "ebq.%d lq" % b)
+            act(T.dh[:, C * b:C * b + C], bank(4 + b, 0, C), F.Copy, "ps%d" % (4 + b), "dh.%d" % b, scale=0.5)
         for k in range(32):
             scan(T.ft[:, S * (k + 1):S * (k + 2)], tb[:, S * k:S * (k + 1)], T.ft[:, S * k:S * (k + 1)], 0.0,
                  A.add, A.max, "tb%d ft.%d" % (t, k), "ft.%d" % (k + 1))
-            if k in side:
-                side[k]()
+            if k < 4:
+                unpack(k)
+            if k == 4 and t == 0:
+                quant(T.vq[:], T.vs[:], T.vin[:], "vin", "vq")
+            if k == 24:
+                ts(T.ov[:], T.vacc[:], 0.5, A.mult, " ".join("va.%d" % c for c in range(28)), "ov", 32.0, A.add)
+            if k == 26:
+                tt(T.dl[:], T.bm[:, K:], T.at[:], A.subtract, "bm.1 at", "dl")
 
         fts = " ".join("ft.%d" % k for k in range(33))
         tt(T.lr[:], T.ft[:].indirect(T.oe[:]), T.wt[:], A.mult, fts + " oe.0 oe.1 wt", "lr")
@@ -415,16 +434,16 @@ def rank_program(g, core, T, topo):
         scan(T.pm[:, 1:], T.key[:], T.key[:], T.pm[:, 0:1], A.max, A.max, "key pm.0", "pm.1")
         cc = T.cc
         tt(cc[:, 0:K], T.pm[:, 1:], T.pm[:, 0:K], A.is_gt, "pm.0 pm.1", "cc.0")
-        tt(cc[:, K:2 * K], T.pm[:, 1:], T.pm[:, 0:K], A.is_le, "pm.0 pm.1", "cc.1")
-        tt(cc[:, 2 * K:3 * K], cc[:, 0:K], T.dl[:], A.mult, "cc.0 dl", "cc.2")
-        tt(cc[:, 3 * K:], cc[:, 0:K], T.bm[:, 0:K], A.mult, "cc.0 bm.0", "cc.3")
-        scan(T.zz[:, 1:65], cc[:, 2 * K - 1:K - 1:-1], cc[:, 3 * K - 1:2 * K - 1:-1], 0.0, A.mult, A.add,
-             "cc.1 cc.2", "zz.0")
-        scan(T.ut[:, K - 1::-1], cc[:, 2 * K - 1:K - 1:-1], cc[:, 4 * K - 1:3 * K - 1:-1], float(C - 1), A.mult, A.add,
-             "cc.1 cc.3", "ut")
-        scan(T.zz[:, 65:], cc[:, K:2 * K], cc[:, 2 * K:3 * K], T.zz[:, 64:65], A.mult, A.add, "cc.1 cc.2 zz.0", "zz.1")
+        tt(cc[:, 2 * K - 1:K - 1:-1], T.pm[:, 1:], T.pm[:, 0:K], A.is_le, "pm.0 pm.1", "cc.1")
+        act(cc[:, 2 * K:3 * K], cc[:, 0:K], F.Identity, "cc.0", "cc.2", scale=-1.0, bias=1.0)
+        tt(cc[:, 5 * K:], cc[:, 0:K], T.bm[:, 0:K], A.mult, "cc.0 bm.0", "cc.5")
+        tt(cc[:, 4 * K - 1:3 * K - 1:-1], cc[:, 0:K], T.dl[:], A.mult, "cc.0 dl", "cc.3")
+        tt(cc[:, 4 * K:5 * K], cc[:, 0:K], T.dl[:], A.mult, "cc.0 dl", "cc.4")
+        scan(T.ut[:, K - 1::-1], cc[:, K:2 * K], cc[:, 6 * K - 1:5 * K - 1:-1], float(C - 1), A.mult, A.add,
+             "cc.1 cc.5", "ut")
+        scan(T.zz[:, 1:], cc[:, K:3 * K], cc[:, 3 * K:5 * K], 0.0, A.mult, A.add, "cc.1 cc.2 cc.3 cc.4", "zz")
         act(T.ug[:], T.ut[:].indirect(T.ov[:]), F.Copy, "ut ut.e ov", "ug")
-        tt(T.fw[:], T.zz[:, 64:].indirect(T.ov[:]), T.pw[:], A.subtract, "zz.0 zz.1 ov pw", "fw")
+        tt(T.fw[:], T.zz[:, 64:].indirect(T.ov[:]), T.pw[:], A.subtract, "zz ov pw", "fw")
         scan(T.qs[:], T.fw[:], T.ug[:], 0.0, A.max, A.min, "fw ug", "qs")
         cp(T.oqo[:], T.qs[:, 15::16], "qs", "oqo")
         qr = T["qr%d" % t]
@@ -432,11 +451,13 @@ def rank_program(g, core, T, topo):
         dma("s", T.oq[:, C * t:C * t + C], qr[0:128:16, :], r="qr%d" % t)
 
         xn = xs[t + 1]
-        for h in range(2):
-            for b in range(4):
-                v = slice(4 * H * h + b, 4 * H * (h + 1), 4)
-                tt(T.gt[:, v], T.dh[:, C * b:C * b + C].indirect(T.oqo[:, 14 * h:14 * h + 14]), T.xh[:, v], A.add,
-                   "dh.%d oqo xh" % b, "gt.%d.%d" % (h, b))
+
+        def mid(h, b):
+            v = slice(4 * H * h + b, 4 * H * (h + 1), 4)
+            tt(T.gt[:, v], T.dh[:, C * b:C * b + C].indirect(T.oqo[:, 14 * h:14 * h + 14]), T.xh[:, v], A.add,
+               "dh.%d oqo xh" % b, "gt.%d.%d" % (h, b))
+
+        def layer(h):
             quant(T.gq[:, H * h:H * h + H], T.gs[:, H * h:H * h + H], T.gt[:, 4 * H * h:4 * H * (h + 1)],
                   " ".join("gt.%d.%d" % (h, b) for b in range(4)), "gq.%d" % h)
             for b in range(4):
@@ -444,13 +465,13 @@ def rank_program(g, core, T, topo):
                    T.gq[:, H * h:H * h + H], T.gs[:, H * h:H * h + H], "wq wsc gq.%d" % h)
                 act(T.rl[:, C * b + H * h:C * b + H * h + H], bank(4 * h + b, 0, H), F.Relu, "ps%d" % (4 * h + b),
                     "rl.%d.%d" % (h, b), scale=0.015625)
-        for h in range(2):
-            for b in range(4):
-                v = slice(4 * H * h + b, 4 * H * (h + 1), 4)
-                tt(xn[:, v], T.gt[:, v], T.rl[:, C * b + H * h:C * b + H * h + H], A.add,
-                   "gt.%d.%d rl.%d.%d" % (h, b, h, b), "X%d.%d.%d" % (t + 1, h, b))
-            if t == 1 and h == 0:
-                quant(T.vq[:], T.vs[:], T.vin[:], "vin", "vq")
+
+        def last(h, b):
+            v = slice(4 * H * h + b, 4 * H * (h + 1), 4)
+            tt(xn[:, v], T.gt[:, v], T.rl[:, C * b + H * h:C * b + H * h + H], A.add,
+               "gt.%d.%d rl.%d.%d" % (h, b, h, b), "X%d.%d.%d" % (t + 1, h, b))
+
+        def done(h):
             quant_state(t + 1, h)
             if t == 0:
                 score(1, h)
@@ -460,6 +481,21 @@ def rank_program(g, core, T, topo):
                 dma("s", T.oc[:, 4 * lo:4 * hi], T.tq2[:, lo:hi].bitcast(dt.uint8), r="tq2.%d" % h)
                 act(T.ysb[:, lo:hi], bank(h, 0, H), F.Copy, "ps%d" % h, "ysb.%d" % h)
                 dma("a", T.y[:, lo:hi], T.ysb[:, lo:hi], r="ysb.%d" % h)
+        for b in range(4):
+            mid(0, b)
+        mid(1, 0)
+        layer(0)
+        for b in range(1, 4):
+            mid(1, b)
+        last(0, 0)
+        layer(1)
+        for b in range(1, 4):
+            last(0, b)
+        last(1, 0)
+        done(0)
+        for b in range(1, 4):
+            last(1, b)
+        done(1)
     for k in range(4):
         dma("s", T.osc[4 * k:4 * k + 4, :], T.ts2[32 * k:32 * k + 4, :], r="tq2.0 tq2.1")
 

@@ -1,8 +1,8 @@
 from concourse.mybir import dt, AluOpType, ActivationFunctionType
 
 C, H, K = 448, 224, 64
-S = 130
-TB = 32 * S
+S, NB = 256, 22
+TB = NB * S
 BIG = 1.0e29
 F32, BF, I32, U16, X4, U8 = "float32", "bfloat16", "int32", "uint16", "float8_e4m3fn_x4", "uint8"
 
@@ -22,23 +22,23 @@ SCRATCH = {
     "eks": _sb(128, U8),
     "ct": _sb(16 * H, BF), "cq": _sb(4 * H, X4), "cs": _sb(4 * H, U8), "sg": _sb(6 * H, BF),
     "et": _sb(12 * 128, BF), "eq": _sb(3 * 128, X4), "es": _sb(3 * 128, U8), "sg2": _sb(4 * 128, BF),
-    "iw": _sb(C, I32), "pw": _sb(C, I32), "km": _sb(128, F32), "k2": _sb(H, F32), "r32": _sb(H, F32),
-    "rp": _sb(H, F32), "r16": _sb(128, F32), "r01": _sb(128, F32),
+    "iw": _sb(C, I32), "pw": _sb(C, I32), "km": _sb(192, F32), "k2": _sb(H, F32), "r32": _sb(H, F32),
+    "rp": _sb(H, F32), "r16": _sb(192, F32),
     "iof": _sb(C, F32), "isml": _sb(32, I32), "blk": _sb(8, F32), "ones": _sb(64, BF),
     "oul": _sb(8, U16), "pc": _sb(8, F32),
-    "thr": _sb(28, F32), "bex": _sb(4, F32), "bs": _sb(12, F32), "ksg": _sb(128, F32), "wt": _sb(128, F32),
-    "sv": _sb(192, BF), "zt": _sb(4 * S, BF),
+    "thr": _sb(28, F32), "kc": _sb(80, F32), "om": _sb(12, U16), "wt": _sb(K, F32),
+    "sv": _sb(192, BF), "zt": _sb(TB // 8, BF),
     "mx": _sb(C, F32), "am": _sb(C, F32), "wm": _sb(C, F32), "se": _sb(H, F32), "so": _sb(H, F32),
     "f1": _sb(H, BF), "p1": _sb(H, BF), "cb": _sb(384, BF), "cn": _sb(384, BF), "jk": _sb(384, BF),
     "jv": _sb(28 * K, BF), "acc": _sb(2, F32), "oa": _sb(4, U16), "cd": _sb(128, F32), "col": _sb(128, F32),
-    "a2": _sb(128, F32), "w2": _sb(128, F32), "f2": _sb(128, BF), "p2": _sb(128, BF), "a3": _sb(128, F32),
-    "w3": _sb(128, F32), "or2": _sb(8, U16),
+    "a2": _sb(128, F32), "w2": _sb(128, F32), "f2": _sb(128, BF), "p2": _sb(128, BF), "a3": _sb(192, F32),
+    "w3": _sb(192, F32), "or2": _sb(8, U16),
     "ra0": _sb(128, BF), "ra1": _sb(128, BF), "ht0": _sb(128, F32), "ht1": _sb(128, F32),
     "lr0": _sb(K, BF), "lr1": _sb(K, BF), "lh0": _sb(K, F32), "lh1": _sb(K, F32),
-    "ora": _sb(4, U16), "kt": _sb(K, F32), "at": _sb(K, F32), "ok": _sb(8, U16), "vacc": _sb(28, F32),
+    "ora": _sb(4, U16), "kt": _sb(K, F32), "at": _sb(K, F32), "ok": _sb(12, U16), "vacc": _sb(28, F32),
     "ov": _sb(28, U16),
-    "a4": _sb(128, F32), "w4": _sb(128, F32), "sm": _sb(40, F32), "od": _sb(12, U16),
-    "oe": _sb(8, U16), "tb0": _sb(3 * TB + 16, BF), "tb1": _sb(3 * TB + 16, BF), "ft": _sb(33 * S, BF),
+    "a4": _sb(192, F32), "w4": _sb(192, F32), "sm": _sb(96, F32), "od": _sb(16, U16),
+    "oe": _sb(8, U16), "tb0": _sb(3 * TB + 16, BF), "tb1": _sb(3 * TB + 16, BF), "ft": _sb((NB + 1) * S, BF),
     "lr": _sb(128, F32), "key": _sb(K, F32), "pm": _sb(K + 1, F32), "cc": _sb(6 * K, F32), "bm": _sb(2 * K, F32),
     "dl": _sb(K, F32), "zz": _sb(129, F32), "ut": _sb(K + 1, F32), "fw": _sb(C, F32), "ug": _sb(C, F32),
     "qs": _sb(C, F32), "oqo": _sb(28, U16), "qr0": _sb(C, F32), "qr1": _sb(C, F32),
@@ -104,7 +104,7 @@ def rank_program(g, core, T, topo):
 
     def clear_table(t, after):
         for j in range(8):
-            issue("s", lambda: g.sync.dma_start(T["tb%d" % t][:, 4 * S * j:4 * S * (j + 1)], T.zt[:]),
+            issue("s", lambda: g.sync.dma_start(T["tb%d" % t][:, TB // 8 * j:TB // 8 * (j + 1)], T.zt[:]),
                   ["zt", after], ["tb%d" % t] if j == 7 else [], "z%d" % t, 16)
 
     def send(t, pairs, r, arr, land):
@@ -162,66 +162,82 @@ def rank_program(g, core, T, topo):
         scan(out[:, 0:n], T.r16[:, 0:n], a[:, 0:n], -BIG, A.min, A.max, r + " r16", w)
 
     dma("s", T.xin[:, 0:4 * H], T.x[:, 0:4 * H], w="X0.0")
+    dma("a", T.uin[:], T.u[:], w="uin")
     dma("a", T.xin[:, 4 * H:], T.x[:, 4 * H:], w="X0.1")
-    dma("s", T.uin[:], T.u[:], w="uin")
     dma("s", T.wq[:].bitcast(dt.uint8), T.wc[:], w="wq")
     dma("s", T.wsc[:], T.ws[:], w="wsc")
     dma("s", T.vin[:], T.v[:], w="vin")
 
-    iul, iblk, ibs, ip, ipa = T.isml[:, 0:8], T.isml[:, 8:16], T.isml[:, 16:24], T.isml[:, 24:25], T.isml[:, 26:28]
+    iul, iblk, ibs, ip, ipa = T.isml[:, 0:8], T.isml[:, 8:16], T.isml[:, 16:24], T.isml[:, 24:25], T.isml[:, 26:27]
     iota(iul, [[16, 8]], 0, 0, "iul")
     iota(iblk, [[-16, 8]], 0, 1, "iblk")
     iota(T.iw[:], [[1023, C]], 1023, -1024, "iw")
     iota(ip, [[0, 1]], 0, 1, "ip")
     iota(T.iof[:], [[1, C]], 0, 0, "iof", True)
-    iota(T.bex[:], [[8 * S, 4]], 0, 0, "bex", True)
     ms(T.ones[:], 1.0, "ones")
     ms(T.r32[:], BIG, "r32")
     ms(T.zt[:], 0.0, "zt")
     cp(T.oul[:], iul, "iul", "oul")
     ts(ibs, iblk, 4, A.arith_shift_right, "iblk", "ibs")
     ms(T.r32[:, 0::32], -BIG, "r32")
-    ms(T.zt[:, 64::S], -1000.0, "zt")
-    ts(T.blk[:], ibs, 0.0, A.is_equal, "ibs", "blk")
     ms(T.rp[:, 0::2], -BIG, "rp.0")
+    ts(T.blk[:], ibs, 0.0, A.is_equal, "ibs", "blk")
     ms(T.rp[:, 1::2], BIG, "rp.1")
     ms(T.ct[:, 12 * H + 3::4], 0.0, "ct.15")
     ms(T.r16[:], BIG, "r16")
-    ms(T.r01[:], 1.0, "r01")
     ts(T.pw[:], T.iw[:], 16383, A.bitwise_and, "iw", "pw")
-    ts(T.isml[:, 26:27], ip, 15, A.bitwise_and, "ip", "ipa.0")
-    ts(T.isml[:, 27:28], ip, 1, A.bitwise_and, "ip", "ipa.1")
+    ts(ipa, ip, 15, A.bitwise_and, "ip", "ipa.0")
+    ms(T.r16[:, 0::16], -BIG, "r16")
     for e in range(2):
         ts(T.k2[:, e::2], T.pw[:, 0:112], 1024.0, A.is_ge, "pw", "k2.%d" % e, -BIG, A.mult)
-    cp(T.pc[:, 0:2], ipa, "ipa.0 ipa.1", "pc.0")
+    cp(T.pc[:, 0:1], ipa, "ipa.0", "pc.0")
     for j in range(8):
         act(T.ek[:, 64 * j:64 * j + 64], T.ones[:], F.Copy, "ones blk", "ek.%d" % j, scale=T.blk[:, j:j + 1])
-    quant(T.uq[:], T.us[:], T.uin[:], "uin", "uq")
     quant(T.ekq[:], T.eks[:], T.ek[:], " ".join("ek.%d" % j for j in range(8)), "ekq")
+    ts(T.km[:], T.pw[:, 0:192], 1024.0, A.is_ge, "pw", "km", -BIG, A.mult)
+    quant(T.uq[:], T.us[:], T.uin[:], "uin", "uq")
+    ts(T.thr[:], T.iof[:, 0::16], T.pc[:, 0:1], A.add, "iof pc.0", "thr", 0.5, A.add)
     cp(T.ur[:].bitcast(dt.uint32), T.uq[:].bitcast(dt.uint32).indirect(T.oul[:]), "uq oul", "ur")
     act(T.urs[:], T.us[:].indirect(T.oul[:]), F.Copy, "uq oul", "urs")
 
+    def kc(i, n=1):
+        return T.kc[:, 4 * i:4 * i + 4 * n]
+    th, vi, mi = T.thr[:, 0:4], T.isml[:, 0:4], T.isml[:, 4:8]
     later = [
-        lambda: ts(T.thr[:], T.iof[:, 0::16], T.pc[:, 0:1], A.add, "iof pc.0", "thr", 0.5, A.add),
-        lambda: ts(T.km[:], T.pw[:, 0:128], 1024.0, A.is_ge, "pw", "km", -BIG, A.mult),
-        lambda: ms(T.r16[:, 0::16], -BIG, "r16"),
+        lambda: ts(vi, th, 21846.0, A.mult, "thr", "iul", -10923.0, A.add),
+        lambda: ms(T.sv[:, K:], -1.0, "sv.1"),
+        lambda: ts(mi, vi, 16, A.arith_shift_right, "iul", "mi"),
+        lambda: ts(kc(0), th, 63.0, A.is_lt, "thr", "nl"),
         lambda: ms(T.et[:, 1024:], 0.0, "et.z"),
-        lambda: ts(T.pc[:, 2:3], T.pc[:, 1:2], -2.0, A.mult, "pc.0", "pc.2", 1.0, A.add),
-        lambda: ts(T.pc[:, 3:4], T.pc[:, 1:2], float(TB + S // 2), A.mult, "pc.0", "pc.3", -1.0, A.add),
-        lambda: ms(T.r01[:, 0::16], 0.0, "r01"),
-        lambda: ts(T.pc[:, 4:5], T.pc[:, 0:1], float(S // 2), A.mult, "pc.0 pc.2", "pc.4", T.pc[:, 2:3], A.mult),
-        lambda: ms(T.ft[:, 0:S], 0.0, "ft.0"),
-        lambda: ms(T.wt[:], 1.0, "wt"),
-        lambda: tt(T.pc[:, 5:6], T.pc[:, 4:5], T.pc[:, 3:4], A.add, "pc.3 pc.4", "pc.5"),
-        lambda: ts(T.ksg[:], T.pw[:, 0:128], 1024.0, A.is_lt, "pw pc.2", "ksg", T.pc[:, 2:3], A.mult),
-        lambda: ms(T.sv[:, 0:128], 1.0, "sv.0"),
-        lambda: ts(T.bs[:, 0:4], T.bex[:], T.pc[:, 2:3], A.mult, "bex pc.2 pc.5", "bs.0", T.pc[:, 5:6], A.add),
-        lambda: ms(T.wt[:, 0:K:2], 129.0 / 128.0, "wt"),
-        lambda: ms(T.sv[:, 128:], -1.0, "sv.1"),
-        lambda: ts(T.bs[:, 4:8], T.bs[:, 0:4], -1.0, A.mult, "bs.0", "bs.1", float(TB - 2), A.add),
-        lambda: ts(T.bs[:, 8:12], T.bs[:, 0:4], -1.0, A.add, "bs.0", "bs.2"),
+        lambda: ts(kc(1), mi, -3.0, A.mult, "mi", "k1", -0.5, A.add),
+        lambda: ts(kc(2), mi, float(S), A.mult, "mi", "bF", -1.0, A.add),
+        lambda: ts(kc(3), mi, -float(S), A.mult, "mi", "bB", float(TB + 1), A.add),
+        lambda: tt(kc(4), kc(1), th, A.add, "k1 thr", "rho"),
+        lambda: ts(kc(5), kc(4), 0.0, A.is_equal, "rho", "e0"),
+        lambda: ts(kc(6), kc(4), 2.0, A.is_equal, "rho", "e2"),
+        lambda: ts(kc(7), kc(6), -3.0, A.mult, "e2", "k7", 0.5, A.add),
+        lambda: ts(kc(8), kc(5), 3.0, A.mult, "e0", "k8", -1.5, A.add),
+        lambda: tt(kc(7), kc(7), th, A.add, "k7 thr", "k7"),
+        lambda: tt(kc(8), kc(8), th, A.add, "k8 thr", "k8"),
+        lambda: ts(T.om[:, 0:4], th, -0.5, A.add, "thr", "om.0"),
+        lambda: ts(kc(9), kc(5), 2.0, A.mult, "e0", "sz", -1.0, A.add),
+        lambda: ts(T.om[:, 4:12], kc(7, 2), 63.0, A.min, "k7 k8", "om.1"),
+        lambda: ts(kc(10), kc(6), -2.0, A.mult, "e2", "sy", 1.0, A.add),
+        lambda: ts(kc(11), mi, float(S), A.mult, "mi", "hm", -float(TB // 2 + 1), A.add),
+        lambda: tt(kc(9), kc(9), kc(0), A.mult, "sz nl", "sz"),
+        lambda: tt(kc(10), kc(10), kc(0), A.mult, "sy nl", "sy"),
+        lambda: ts(kc(12), kc(0), -float(5 * TB // 2 + 1), A.mult, "nl", "k12", float(3 * TB), A.add),
+        lambda: ts(kc(13), kc(0), -float(5 * TB // 2 + 2), A.mult, "nl", "k13", float(3 * TB + 1), A.add),
+        lambda: tt(kc(14), kc(9), kc(11), A.mult, "sz hm", "k14"),
+        lambda: tt(kc(15), kc(10), kc(11), A.mult, "sy hm", "k15"),
+        lambda: ms(T.ft[:, 0:S], 0.0, "ft.0.0 ft.0.1"),
+        lambda: tt(kc(14, 2), kc(14, 2), kc(12, 2), A.add, "k12 k13 k14 k15", "k14 k15"),
+        lambda: ts(kc(16, 2), kc(5, 2), -float(S), A.mult, "e0 e2", "ex", float(S), A.add),
+        lambda: ms(T.sv[:, 0:K], 1.0, "sv.0"),
+        lambda: ms(T.wt[:, 0::3], 129.0 / 128.0, "wt.0"),
+        lambda: ms(T.wt[:, 1::3], 0.0, "wt.1"),
+        lambda: ms(T.wt[:, 2::3], 1.0, "wt.2"),
         lambda: ms(T.ut[:, K:K + 1], float(C - 1), "ut.e"),
-        lambda: ms(T.wt[:, K + 1::2], 129.0 / 128.0, "wt"),
     ]
 
     def fill(n):
@@ -238,6 +254,9 @@ def rank_program(g, core, T, topo):
     def score(t, h):
         mm(h, H, T.ur[:], T.urs[:], T["tq%d" % t][:, H * h:H * h + H], T["ts%d" % t][:, H * h:H * h + H],
            "ur urs tq%d.%d" % (t, h))
+
+    def masked(h):
+        tt(T.am[:, H * h:H * h + H], bank(h, 0, H), T.k2[:], A.add, "ps%d k2.0 k2.1" % h, "am.%d" % h)
 
     def compare(src, step, n, w, wname, sname, tile, tname, tmp, tmpname, acols, eqslot):
         def view(buf, lo, hi):
@@ -280,6 +299,8 @@ def rank_program(g, core, T, topo):
     for h in range(2):
         quant_state(0, h)
         score(0, h)
+    fill(2)
+    masked(0)
 
     for t in range(2):
         tq, tsc, lq, ls = T["tq%d" % t], T["ts%d" % t], T["lq%d" % t], T["ls%d" % t]
@@ -295,7 +316,8 @@ def rank_program(g, core, T, topo):
 
         for h in range(2):
             v = slice(H * h, H * h + H)
-            tt(T.am[:, v], bank(h, 0, H), T.k2[:], A.add, "ps%d k2.0 k2.1" % h, "am.%d" % h)
+            if h:
+                masked(h)
             scan(T.mx[:, v], T.rp[:], bank(h, 0, H), -BIG, A.min, A.max, "ps%d rp.0 rp.1" % h, "mx.%d" % h)
             scan(T.wm[:, v], T.r32[:], T.am[:, v], -BIG, A.min, A.max, "am.%d r32" % h, "wm.%d" % h)
         fill(2)
@@ -339,8 +361,8 @@ def rank_program(g, core, T, topo):
 
         act(T.cd[:, 0::2], T.se[:].indirect(T.oa[:]), F.Copy, "se.0 se.1 oa.0 oa.1", "cd.0")
         act(T.cd[:, 1::2], T.so[:].indirect(T.oa[:]), F.Copy, "so.0 so.1 oa.0 oa.1", "cd.1")
-        tt(T.a2[:, 0::2], T.se[:].indirect(T.oa[:]), T.km[:, 0::2], A.add, "se.0 se.1 oa.0 oa.1 km", "a2.0")
-        tt(T.a2[:, 1::2], T.so[:].indirect(T.oa[:]), T.km[:, 1::2], A.add, "so.0 so.1 oa.0 oa.1 km", "a2.1")
+        tt(T.a2[:, 0::2], T.se[:].indirect(T.oa[:]), T.km[:, 0:128:2], A.add, "se.0 se.1 oa.0 oa.1 km", "a2.0")
+        tt(T.a2[:, 1::2], T.so[:].indirect(T.oa[:]), T.km[:, 1:128:2], A.add, "so.0 so.1 oa.0 oa.1 km", "a2.1")
         fill(2)
         wrap_scan(T.w2, T.a2, 128, "a2.0 a2.1", "w2")
         fill(2)
@@ -355,59 +377,78 @@ def rank_program(g, core, T, topo):
             mm(3, 128, T.ekq[:], T.eks[:], T.eq[:, 128 * q:128 * q + 128], T.es[:, 128 * q:128 * q + 128],
                "ekq eq.%d" % q, first, last)
         eqs()
-        for s, c in [(0, 7), (1, 3), (2, 4), (3, 2), (7, 5)]:
+        for s, c in [(7, 5), (0, 7), (1, 3), (2, 4), (3, 2)]:
             vcol(s, c)
-            if s == 1:
-                tile2(2, True, False)
-        tile2(0, False, False)
-        tile2(1, False, True)
-        fill(9)
-        tt(T.a3[:], bank(3, 0, 128), T.km[:], A.add, "ps3 km", "a3")
-        ts(T.f2[:], bank(3, 0, 128), 64.5, A.is_le, "ps3", "f2")
+        tile2(2, True, False)
+        tile2(1, False, False)
+        tile2(0, False, True)
+        fill(4)
+        tt(T.a3[:, 0:128], bank(3, 0, 128), T.km[:, 0:128], A.add, "ps3 km", "a3")
+        ts(T.f2[:], bank(3, 0, 128), 64.5, A.is_le, "ps3", "f2", 2.0, A.mult)
         wrap_scan(T.w3, T.a3, 128, "a3", "w3")
         scan(T.p2[:], T.f2[:], T.f2[:], 0.0, A.add, A.max, "f2", "p2")
-        ts(T.or2[:], T.w3[:, 15::16], -1.0, A.add, "w3", "or2")
+        ts(T.or2[:], T.w3[:, 15:128:16], -1.0, A.add, "w3", "or2")
         cp(ra[:].indirect(T.or2[:]), T.p2[:], "p2 or2", "ra%d" % t)
         send(t, [(lra[:], ra[:, 0:K])], "ra%d" % t, "ar%d" % (3 * t + 1), "lra")
 
+        cp(ht[:].indirect(T.or2[:, 0:4]), T.col[:, 0:K], "col.0 col.1 or2", "ht%d" % t)
         tt(T.a3[:, 0:K], ra[:, 0:K], T.km[:, 0:K], A.add, "ra%d km" % t, "a3")
-        wrap_scan(T.w3, T.a3, K, "a3", "w3")
-        ts(T.ora[:], T.w3[:, 15:K:16], -1.0, A.add, "w3", "ora")
-        cp(T.kt[:].indirect(T.ora[:]), T.iof[:, 0:K], "iof ora", "kt")
-        tt(T.a3[:, 0:K], T.kt[:], T.km[:, 0:K], A.add, "kt km", "a3")
-        tt(T.a3[:, K::2], T.kt[:, 1::2], T.km[:, 0:K:2], A.add, "kt km", "a3.1")
-        tt(T.a3[:, K + 1::2], T.kt[:, 0::2], T.km[:, 1:K:2], A.add, "kt km", "a3.2")
-        wrap_scan(T.w3, T.a3, 128, "a3 a3.1 a3.2", "w3")
-        cp(T.ok[:], T.w3[:, 15::16], "w3", "ok")
-        cp(ht[:].indirect(T.or2[:]), T.col[:], "col.0 col.1 or2", "ht%d" % t)
+        cp(ht[:].indirect(T.or2[:, 4:8]), T.col[:, K:], "col.0 col.1 or2", "ht%d" % t)
         send(t, [(lh[:], ht[:, 0:K])], "ht%d" % t, "ar%d" % (3 * t + 2), "lh")
         if t == 0:
             clear_table(1, "lh")
-        act(T.xh[:], xs[t][:], F.Copy, "X0.0 X0.1" if t == 0 else
-            " ".join("X1.%d.%d" % (h, b) for h in range(2) for b in range(4)), "xh", scale=0.5)
-
-        sx, sm = T.w4[:, 15:K:16], T.sm
-        tt(T.a4[:], lra[:].indirect(T.ok[:]), T.ksg[:], A.mult, "lra ok ksg", "a4")
+        wrap_scan(T.w3, T.a3, K, "a3", "w3")
+        fill(2)
+        ts(T.ora[:], T.w3[:, 15:K:16], 0.5, A.mult, "w3", "ora", -1.0, A.add)
+        fill(2)
+        cp(T.kt[:].indirect(T.ora[:]), T.iof[:, 0:K], "iof ora", "kt")
+        fill(2)
+        tt(T.a3[:], T.kt[:].indirect(T.om[:]), T.km[:], A.add, "kt km om.0 om.1", "a3")
+        fill(2)
+        wrap_scan(T.w3, T.a3, 192, "a3", "w3")
+        fill(2)
+        cp(T.ok[:], T.w3[:, 15::16], "w3", "ok")
         cp(T.at[:].indirect(T.ora[:]), ht[:, 0:K], "ht%d ora" % t, "at")
-        scan(T.w4[:], T.r01[:], T.a4[:], 0.0, A.mult, A.add, "r01 a4", "w4")
         for c in range(28):
             act(T.jv[:, K * c:K * c + K], T.at[:], F.Sign, "at thr", "va.%d" % c, scale=-1.0,
                 bias=T.thr[:, c:c + 1], accum_out=T.vacc[:, c:c + 1])
         act(T.bm[:, 0:K], lh[:].indirect(T.ok[:, 0:4]), F.Identity, "lh ok", "bm.0", bias=-1.0)
         act(T.bm[:, K:], lh[:].indirect(T.ok[:, 0:4]), F.Identity, "lh ok", "bm.1", bias=1023.0)
-        tt(sm[:, 0:4], sx, T.w4[:, K + 15::16], A.subtract, "w4", "sm.0")
-        tt(sm[:, 4:8], T.bs[:, 4:8], sx, A.subtract, "w4 bs.1", "sm.1")
-        tt(sm[:, 8:12], T.bs[:, 8:12], sx, A.add, "w4 bs.2", "sm.2")
-        tt(sm[:, 20:24], T.bs[:, 0:4], sx, A.add, "w4 bs.0", "sm.5")
-        ts(sm[:, 12:16], sm[:, 0:4], 1.0, A.is_equal, "sm.0", "sm.3", float(TB), A.mult)
-        ts(sm[:, 16:20], sm[:, 0:4], 1.5, A.is_le, "sm.0", "sm.4", float(2 * TB), A.mult)
-        ts(sm[:, 32:36], sm[:, 0:4], 1.0, A.is_equal, "sm.0", "sm.7")
-        ts(T.oe[:, 0:4], sm[:, 20:24], float(S), A.add, "sm.5", "oe.0")
-        tt(sm[:, 24:32], sm[:, 4:12], sm[:, 12:20], A.add, "sm.1 sm.2 sm.3 sm.4", "sm.6")
-        tt(sm[:, 36:40], sm[:, 32:36], sm[:, 4:8], A.add, "sm.7 sm.1", "sm.8")
-        cp(T.od[:], sm[:, 20:32], "sm.5 sm.6", "od")
-        ts(T.oe[:, 4:8], sm[:, 36:40], float(S), A.add, "sm.8", "oe.1")
-        cp(tb[:].indirect(T.od[:]), T.sv[:], "od sv.0 sv.1 tb%d" % t, "tb%d" % t)
+        act(T.xh[:], xs[t][:], F.Copy, "X0.0 X0.1" if t == 0 else
+            " ".join("X1.%d.%d" % (h, b) for h in range(2) for b in range(4)), "xh", scale=0.5)
+
+        x, y, z = T.w4[:, 15:K:16], T.w4[:, K + 15:2 * K:16], T.w4[:, 2 * K + 15::16]
+
+        def sm(i, n=1):
+            return T.sm[:, 4 * i:4 * i + 4 * n]
+        tbn = "tb%d" % t
+        tt(T.a4[:], lra[:].indirect(T.ok[:]), T.km[:], A.add, "lra ok km", "a4")
+        fill(2)
+        wrap_scan(T.w4, T.a4, 192, "a4", "w4")
+        fill(9)
+        tt(sm(0), x, y, A.subtract, "w4", "s0")
+        tt(sm(1), x, z, A.subtract, "w4", "s1")
+        tt(sm(2), z, y, A.subtract, "w4", "s2")
+        tt(sm(3), y, z, A.subtract, "w4", "s3")
+        tt(sm(7), sm(0), kc(10), A.mult, "s0 sy", "s7")
+        tt(sm(6), sm(1), kc(9), A.mult, "s1 sz", "s6")
+        tt(sm(16), kc(2), x, A.add, "w4 bF", "s16")
+        tt(sm(8, 2), sm(0, 2), sm(2, 2), A.mult, "s0 s1 s2 s3", "s8")
+        tt(sm(17), kc(3), x, A.subtract, "w4 bB", "s17")
+        tt(sm(4), x, kc(9), A.mult, "w4 sz", "s4")
+        tt(sm(5), x, kc(10), A.mult, "w4 sy", "s5")
+        tt(sm(12, 2), sm(6, 2), sm(8, 2), A.min, "s6 s7 s8", "s12")
+        cp(T.od[:, 0:8], sm(16, 2), "s16 s17", "od.0")
+        tt(sm(10, 2), sm(4, 2), kc(14, 2), A.add, "s4 s5 k14 k15", "s10")
+        ts(sm(14), sm(12), 0.0, A.is_lt, "s12", "s14", float(TB), A.mult)
+        ts(sm(15), sm(13), 0.0, A.is_lt, "s12", "s15", float(2 * TB), A.mult)
+        cp(tb[:].indirect(T.od[:, 0:4]), T.sv[:, 0:K], "od.0 sv.0 " + tbn, tbn)
+        tt(sm(18, 2), sm(10, 2), sm(14, 2), A.add, "s10 s14 s15", "s18")
+        tt(sm(20, 2), sm(16, 2), kc(16, 2), A.add, "s16 s17 ex", "s20")
+        cp(tb[:].indirect(T.od[:, 4:8]), T.sv[:, 0:K], "od.0 sv.0 " + tbn, tbn)
+        cp(T.od[:, 8:16], sm(18, 2), "s18", "od.1")
+        cp(T.oe[:], sm(20, 2), "s20", "oe")
+        cp(tb[:].indirect(T.od[:, 8:16]), T.sv[:, K:], "od.1 sv.1 " + tbn, tbn)
 
         def unpack(b):
             v = slice(128 * b, 128 * b + 128)
@@ -415,22 +456,26 @@ def rank_program(g, core, T, topo):
                 quant(T.ebq[:, v], T.ebs[:, v], T.eb[:, 512 * b:512 * b + 512], "eb.%d" % b, "ebq.%d" % b)
             mm(4 + b, C, T.ebq[:, v], T.ebs[:, v], lq[:], ls[:], "ebq.%d lq" % b)
             act(T.dh[:, C * b:C * b + C], bank(4 + b, 0, C), F.Copy, "ps%d" % (4 + b), "dh.%d" % b, scale=0.5)
-        for k in range(32):
-            scan(T.ft[:, S * (k + 1):S * (k + 2)], tb[:, S * k:S * (k + 1)], T.ft[:, S * k:S * (k + 1)], 0.0,
-                 A.add, A.max, "tb%d ft.%d" % (t, k), "ft.%d" % (k + 1))
-            if k < 4:
-                unpack(k)
+        unpack(0)
+        for k in range(NB):
+            for e in range(2):
+                lo = S * k + 128 * e
+                scan(T.ft[:, lo + S:lo + S + 128], tb[:, lo:lo + 128], T.ft[:, lo:lo + 128], 0.0,
+                     A.add, A.max, "%s ft.%d.%d" % (tbn, k, e), "ft.%d.%d" % (k + 1, e))
+            if k < 3:
+                unpack(k + 1)
             if k == 4 and t == 0:
                 quant(T.vq[:], T.vs[:], T.vin[:], "vin", "vq")
-            if k == 24:
+            if k == 18:
                 ts(T.ov[:], T.vacc[:], 0.5, A.mult, " ".join("va.%d" % c for c in range(28)), "ov", 32.0, A.add)
-            if k == 26:
+            if k == NB - 1:
                 tt(T.dl[:], T.bm[:, K:], T.at[:], A.subtract, "bm.1 at", "dl")
 
-        fts = " ".join("ft.%d" % k for k in range(33))
-        tt(T.lr[:], T.ft[:].indirect(T.oe[:]), T.wt[:], A.mult, fts + " oe.0 oe.1 wt", "lr")
-        ts(T.pm[:, 0:1], T.ft[:, 32 * S + 63:32 * S + 64], 1.0, A.add, "ft.32", "pm.0")
-        tt(T.key[:], T.lr[:, 0:K], T.lr[:, K:], A.add, "lr", "key")
+        fts = " ".join("ft.%d.%d" % (k, e) for k in range(NB + 1) for e in range(2))
+        ts(T.lr[:, 0:K], T.ft[:].indirect(T.oe[:, 0:4]), 129.0 / 128.0, A.mult, fts + " oe", "lr.0")
+        tt(T.lr[:, K:], T.ft[:].indirect(T.oe[:, 4:8]), T.wt[:], A.add, fts + " oe wt.0 wt.1 wt.2", "lr.1")
+        ts(T.pm[:, 0:1], T.ft[:, NB * S + 127:NB * S + 128], 1.0, A.add, fts, "pm.0")
+        tt(T.key[:], T.lr[:, 0:K], T.lr[:, K:], A.add, "lr.0 lr.1", "key")
         scan(T.pm[:, 1:], T.key[:], T.key[:], T.pm[:, 0:1], A.max, A.max, "key pm.0", "pm.1")
         cc = T.cc
         tt(cc[:, 0:K], T.pm[:, 1:], T.pm[:, 0:K], A.is_gt, "pm.0 pm.1", "cc.0")
@@ -442,12 +487,16 @@ def rank_program(g, core, T, topo):
         scan(T.ut[:, K - 1::-1], cc[:, K:2 * K], cc[:, 6 * K - 1:5 * K - 1:-1], float(C - 1), A.mult, A.add,
              "cc.1 cc.5", "ut")
         scan(T.zz[:, 1:], cc[:, K:3 * K], cc[:, 3 * K:5 * K], 0.0, A.mult, A.add, "cc.1 cc.2 cc.3 cc.4", "zz")
-        act(T.ug[:], T.ut[:].indirect(T.ov[:]), F.Copy, "ut ut.e ov", "ug")
-        tt(T.fw[:], T.zz[:, 64:].indirect(T.ov[:]), T.pw[:], A.subtract, "zz ov pw", "fw")
-        scan(T.qs[:], T.fw[:], T.ug[:], 0.0, A.max, A.min, "fw ug", "qs")
-        cp(T.oqo[:], T.qs[:, 15::16], "qs", "oqo")
+        halves = [(slice(H * h, H * h + H), slice(14 * h, 14 * h + 14), h) for h in range(2)]
+        for v, o, h in halves:
+            act(T.ug[:, v], T.ut[:].indirect(T.ov[:, o]), F.Copy, "ut ut.e ov", "ug.%d" % h)
+            tt(T.fw[:, v], T.zz[:, 64:].indirect(T.ov[:, o]), T.pw[:, v], A.subtract, "zz ov pw", "fw.%d" % h)
+        for v, o, h in halves:
+            scan(T.qs[:, v], T.fw[:, v], T.ug[:, v], 0.0, A.max, A.min, "fw.%d ug.%d" % (h, h), "qs.%d" % h)
+        for v, o, h in halves:
+            cp(T.oqo[:, o], T.qs[:, H * h + 15:H * h + H:16], "qs.%d" % h, "oqo.%d" % h)
         qr = T["qr%d" % t]
-        act(qr[:], T.iof[:].indirect(T.oqo[:]), F.Copy, "iof oqo", "qr%d" % t)
+        act(qr[:], T.iof[:].indirect(T.oqo[:]), F.Copy, "iof oqo.0 oqo.1", "qr%d" % t)
         dma("s", T.oq[:, C * t:C * t + C], qr[0:128:16, :], r="qr%d" % t)
 
         xn = xs[t + 1]
@@ -455,7 +504,7 @@ def rank_program(g, core, T, topo):
         def mid(h, b):
             v = slice(4 * H * h + b, 4 * H * (h + 1), 4)
             tt(T.gt[:, v], T.dh[:, C * b:C * b + C].indirect(T.oqo[:, 14 * h:14 * h + 14]), T.xh[:, v], A.add,
-               "dh.%d oqo xh" % b, "gt.%d.%d" % (h, b))
+               "dh.%d oqo.%d xh" % (b, h), "gt.%d.%d" % (h, b))
 
         def layer(h):
             quant(T.gq[:, H * h:H * h + H], T.gs[:, H * h:H * h + H], T.gt[:, 4 * H * h:4 * H * (h + 1)],
@@ -495,6 +544,8 @@ def rank_program(g, core, T, topo):
         done(0)
         for b in range(1, 4):
             last(1, b)
+        if t == 0:
+            masked(0)
         done(1)
     for k in range(4):
         dma("s", T.osc[4 * k:4 * k + 4, :], T.ts2[32 * k:32 * k + 4, :], r="tq2.0 tq2.1")

@@ -1,9 +1,11 @@
 from concourse.mybir import dt, AluOpType, ActivationFunctionType
 
 C, H, K = 448, 224, 64
-S, NB = 256, 22
+S, NB, MID = 128, 22, 10
 TB = NB * S
 BIG = 1.0e29
+FAR = 2.0 ** 90
+U = 2.0 ** -17
 F32, BF, I32, U16, X4, U8 = "float32", "bfloat16", "int32", "uint16", "float8_e4m3fn_x4", "uint8"
 
 
@@ -22,29 +24,29 @@ SCRATCH = {
     "eks": _sb(128, U8),
     "ct": _sb(16 * H, BF), "cq": _sb(4 * H, X4), "cs": _sb(4 * H, U8), "sg": _sb(6 * H, BF),
     "et": _sb(12 * 128, BF), "eq": _sb(3 * 128, X4), "es": _sb(3 * 128, U8), "sg2": _sb(4 * 128, BF),
-    "iw": _sb(C, I32), "pw": _sb(C, I32), "km": _sb(192, F32), "k2": _sb(H, F32), "r32": _sb(H, F32),
-    "rp": _sb(H, F32), "r16": _sb(192, F32),
-    "iof": _sb(C, F32), "isml": _sb(32, I32), "blk": _sb(8, F32), "ones": _sb(64, BF),
-    "oul": _sb(8, U16), "pc": _sb(8, F32),
-    "thr": _sb(28, F32), "kc": _sb(80, F32), "om": _sb(12, U16), "wt": _sb(K, F32),
-    "sv": _sb(192, BF), "zt": _sb(TB // 8, BF),
-    "mx": _sb(C, F32), "am": _sb(C, F32), "wm": _sb(C, F32), "se": _sb(H, F32), "so": _sb(H, F32),
+    "jm": _sb(256, F32), "pws": _sb(C, F32), "pw": _sb(C, F32), "km": _sb(128, F32), "k2": _sb(H, F32),
+    "r32": _sb(H, BF), "r16": _sb(128, BF), "iof": _sb(C, F32), "isml": _sb(32, I32), "blk": _sb(32, F32),
+    "ones": _sb(K, BF), "oul": _sb(8, U16), "pc": _sb(8, F32), "thr": _sb(28, F32), "zt": _sb(TB // 4, BF),
+    "nb": _sb(66, F32), "nr": _sb(66, F32), "kb": _sb(K, F32), "kp": _sb(K, F32), "ce": _sb(8, F32),
+    "c2v": _sb(K, F32),
+    "mx": _sb(H, F32), "am": _sb(C, F32), "wm": _sb(C, F32), "se": _sb(H, F32), "so": _sb(H, F32),
     "f1": _sb(H, BF), "p1": _sb(H, BF), "cb": _sb(384, BF), "cn": _sb(384, BF), "jk": _sb(384, BF),
-    "jv": _sb(28 * K, BF), "acc": _sb(2, F32), "oa": _sb(4, U16), "cd": _sb(128, F32), "col": _sb(128, F32),
-    "a2": _sb(128, F32), "w2": _sb(128, F32), "f2": _sb(128, BF), "p2": _sb(128, BF), "a3": _sb(192, F32),
-    "w3": _sb(192, F32), "or2": _sb(8, U16),
-    "ra0": _sb(128, BF), "ra1": _sb(128, BF), "ht0": _sb(128, F32), "ht1": _sb(128, F32),
-    "lr0": _sb(K, BF), "lr1": _sb(K, BF), "lh0": _sb(K, F32), "lh1": _sb(K, F32),
-    "ora": _sb(4, U16), "kt": _sb(K, F32), "at": _sb(K, F32), "ok": _sb(12, U16), "vacc": _sb(28, F32),
-    "ov": _sb(28, U16),
-    "a4": _sb(192, F32), "w4": _sb(192, F32), "sm": _sb(96, F32), "od": _sb(16, U16),
-    "oe": _sb(8, U16), "tb0": _sb(3 * TB + 16, BF), "tb1": _sb(3 * TB + 16, BF), "ft": _sb((NB + 1) * S, BF),
-    "lr": _sb(128, F32), "key": _sb(K, F32), "pm": _sb(K + 1, F32), "cc": _sb(6 * K, F32), "bm": _sb(2 * K, F32),
-    "dl": _sb(K, F32), "zz": _sb(129, F32), "ut": _sb(K + 1, F32), "fw": _sb(C, F32), "ug": _sb(C, F32),
+    "jv": _sb(28 * K, BF), "acc": _sb(2, F32), "oa": _sb(4, U16), "cd": _sb(128, F32), "col": _sb(129, F32),
+    "dc": _sb(128, F32), "a2": _sb(128, F32), "w2": _sb(128, F32), "f2": _sb(128, BF), "p2": _sb(128, F32),
+    "a3": _sb(128, F32), "w3": _sb(128, F32), "or2": _sb(8, U16),
+    "ra0": _sb(128, F32), "ra1": _sb(128, F32), "lr0": _sb(K, F32), "lr1": _sb(K, F32),
+    "ora": _sb(4, U16), "av": _sb(K, F32), "af": _sb(K, F32), "vacc": _sb(28, F32), "ov": _sb(28, U16),
+    "bv": _sb(K, F32), "a4": _sb(K, F32), "w4": _sb(K, F32), "sm": _sb(4 * 32, BF), "od": _sb(8, U16),
+    "vf": _sb(K, BF), "vb": _sb(K, BF), "oes": _sb(8, F32), "oe": _sb(8, U16),
+    "tf0": _sb(TB, BF), "tb0": _sb(TB, BF), "tf1": _sb(TB, BF), "tb1": _sb(TB, BF),
+    "ff": _sb(TB + S, BF), "fb": _sb(TB + S, BF),
+    "bi": _sb(K, I32), "sf": _sb(7 * K, F32), "gr": _sb(2 * K, F32), "m1": _sb(2 * K, F32), "m0": _sb(K + 1, F32),
+    "dq": _sb(K + 1, F32), "xu": _sb(K, F32),
+    "ut": _sb(K + 1, F32), "fw": _sb(C, F32), "ug": _sb(C, F32),
     "qs": _sb(C, F32), "oqo": _sb(28, U16), "qr0": _sb(C, F32), "qr1": _sb(C, F32),
     "ps": ("psum", [128, 4096], F32),
 }
-SEMAPHORES = (["ev", "ea", "ep", "eg", "loc", "z0", "z1"] + ["ar%d" % i for i in range(6)]
+SEMAPHORES = (["ev", "ea", "ep", "eg", "loc", "z0", "z1"] + ["ar%d" % i for i in range(4)]
               + ["dm%d" % i for i in range(24)])
 
 
@@ -102,10 +104,11 @@ def rank_program(g, core, T, topo):
         ndma[0] += 1
         issue(q, lambda: queue[q].dma_start(out, in_), r.split(), w.split(), "dm%d" % (ndma[0] - 1), 16)
 
-    def clear_table(t, after):
+    def clear_tables(t, after):
         for j in range(8):
-            issue("s", lambda: g.sync.dma_start(T["tb%d" % t][:, TB // 8 * j:TB // 8 * (j + 1)], T.zt[:]),
-                  ["zt", after], ["tb%d" % t] if j == 7 else [], "z%d" % t, 16)
+            tab = T["t%s%d" % ("fb"[j // 4], t)]
+            issue("s", lambda: g.sync.dma_start(tab[:, TB // 4 * (j % 4):TB // 4 * (j % 4 + 1)], T.zt[:]),
+                  ["zt", after], ["tz%d" % t] if j == 7 else [], "z%d" % t, 16)
 
     def send(t, pairs, r, arr, land):
         peer = T.cores[rank ^ (1 << t)]
@@ -152,7 +155,7 @@ def rank_program(g, core, T, topo):
     def bank(b, lo, hi, step=1):
         return T.ps[:, 512 * b + lo:512 * b + hi:step]
 
-    def iota(out, pat, base, cm, w, small=False):
+    def iota(out, pat, base, cm, w, small=True):
         if small:
             op("g", lambda: g.iota(out, pat, base, cm, allow_small_or_imprecise_dtypes=True), "", w)
         else:
@@ -161,83 +164,58 @@ def rank_program(g, core, T, topo):
     def wrap_scan(out, a, n, r, w):
         scan(out[:, 0:n], T.r16[:, 0:n], a[:, 0:n], -BIG, A.min, A.max, r + " r16", w)
 
-    dma("s", T.xin[:, 0:4 * H], T.x[:, 0:4 * H], w="X0.0")
     dma("a", T.uin[:], T.u[:], w="uin")
-    dma("a", T.xin[:, 4 * H:], T.x[:, 4 * H:], w="X0.1")
-    dma("s", T.wq[:].bitcast(dt.uint8), T.wc[:], w="wq")
+    dma("s", T.xin[:, 0:4 * H], T.x[:, 0:4 * H], w="X0.0")
+    dma("s", T.xin[:, 4 * H:], T.x[:, 4 * H:], w="X0.1")
+    dma("s", T.wq[:].bitcast(dt.uint8), T.wc[:], r="X0.0 X0.1", w="wq")
     dma("s", T.wsc[:], T.ws[:], w="wsc")
     dma("s", T.vin[:], T.v[:], w="vin")
 
-    iul, iblk, ibs, ip, ipa = T.isml[:, 0:8], T.isml[:, 8:16], T.isml[:, 16:24], T.isml[:, 24:25], T.isml[:, 26:27]
-    iota(iul, [[16, 8]], 0, 0, "iul")
-    iota(iblk, [[-16, 8]], 0, 1, "iblk")
-    iota(T.iw[:], [[1023, C]], 1023, -1024, "iw")
-    iota(ip, [[0, 1]], 0, 1, "ip")
-    iota(T.iof[:], [[1, C]], 0, 0, "iof", True)
-    ms(T.ones[:], 1.0, "ones")
+    iul, ip, ipa = T.isml[:, 0:8], T.isml[:, 24:25], T.isml[:, 26:27]
+    iota(ip, [[0, 1]], 0, 1, "ip", False)
+    iota(iul, [[16, 8]], 0, 0, "iul", False)
+    iota(T.jm[:], [[0, 8], [1, 16], [0, 2]], 0, 0, "jm")
+    iota(T.blk[:, 0:8], [[-16, 8]], 0, 1, "blk.0")
+    iota(T.iof[:], [[1, C]], 0, 0, "iof")
     ms(T.r32[:], BIG, "r32")
-    ms(T.zt[:], 0.0, "zt")
+    ts(ipa, ip, 15, A.bitwise_and, "ip", "ipa")
     cp(T.oul[:], iul, "iul", "oul")
-    ts(ibs, iblk, 4, A.arith_shift_right, "iblk", "ibs")
     ms(T.r32[:, 0::32], -BIG, "r32")
-    ms(T.rp[:, 0::2], -BIG, "rp.0")
-    ts(T.blk[:], ibs, 0.0, A.is_equal, "ibs", "blk")
-    ms(T.rp[:, 1::2], BIG, "rp.1")
+    ts(T.pc[:, 0:1], ipa, -FAR, A.mult, "ipa", "pc.0")
     ms(T.ct[:, 12 * H + 3::4], 0.0, "ct.15")
+    ts(T.pc[:, 1:2], ipa, 0.5, A.add, "ipa", "pc.1")
+    ts(T.pc[:, 2:3], ipa, -2048.0 * U, A.mult, "ipa", "pc.2")
     ms(T.r16[:], BIG, "r16")
-    ts(T.pw[:], T.iw[:], 16383, A.bitwise_and, "iw", "pw")
-    ts(ipa, ip, 15, A.bitwise_and, "ip", "ipa.0")
+    ms(T.zt[:], 0.0, "zt")
     ms(T.r16[:, 0::16], -BIG, "r16")
-    for e in range(2):
-        ts(T.k2[:, e::2], T.pw[:, 0:112], 1024.0, A.is_ge, "pw", "k2.%d" % e, -BIG, A.mult)
-    cp(T.pc[:, 0:1], ipa, "ipa.0", "pc.0")
-    for j in range(8):
-        act(T.ek[:, 64 * j:64 * j + 64], T.ones[:], F.Copy, "ones blk", "ek.%d" % j, scale=T.blk[:, j:j + 1])
-    quant(T.ekq[:], T.eks[:], T.ek[:], " ".join("ek.%d" % j for j in range(8)), "ekq")
-    ts(T.km[:], T.pw[:, 0:192], 1024.0, A.is_ge, "pw", "km", -BIG, A.mult)
     quant(T.uq[:], T.us[:], T.uin[:], "uin", "uq")
-    ts(T.thr[:], T.iof[:, 0::16], T.pc[:, 0:1], A.add, "iof pc.0", "thr", 0.5, A.add)
+    ms(T.et[:, 1024:1280], 0.0, "et.z0")
     cp(T.ur[:].bitcast(dt.uint32), T.uq[:].bitcast(dt.uint32).indirect(T.oul[:]), "uq oul", "ur")
+    act(T.k2[:], T.jm[:, 0:H], F.Abs, "jm pc.0", "k2", scale=FAR, bias=T.pc[:, 0:1])
+    act(T.blk[:, 8:16], T.blk[:, 0:8], F.Abs, "blk.0", "blk.1", bias=-7.5)
+    act(T.km[:], T.jm[:, 0::2], F.Abs, "jm pc.0", "km", scale=FAR, bias=T.pc[:, 0:1])
+    act(T.blk[:, 16:24], T.blk[:, 8:16], F.Sign, "blk.1", "blk.2", scale=-1.0, bias=8.0)
     act(T.urs[:], T.us[:].indirect(T.oul[:]), F.Copy, "uq oul", "urs")
+    act(T.blk[:, 24:32], T.blk[:, 16:24], F.Relu, "blk.2", "blk.3")
+    for j in range(8):
+        act(T.ek[:, 64 * j:64 * j + 64], T.jm[:, 0:64], F.Identity, "jm blk.3", "ek.%d" % j, scale=0.0,
+            bias=T.blk[:, 24 + j:25 + j])
+    act(T.thr[:], T.iof[:, 0::16], F.Identity, "iof pc.1", "thr", bias=T.pc[:, 1:2])
 
-    def kc(i, n=1):
-        return T.kc[:, 4 * i:4 * i + 4 * n]
-    th, vi, mi = T.thr[:, 0:4], T.isml[:, 0:4], T.isml[:, 4:8]
     later = [
-        lambda: ts(vi, th, 21846.0, A.mult, "thr", "iul", -10923.0, A.add),
-        lambda: ms(T.sv[:, K:], -1.0, "sv.1"),
-        lambda: ts(mi, vi, 16, A.arith_shift_right, "iul", "mi"),
-        lambda: ts(kc(0), th, 63.0, A.is_lt, "thr", "nl"),
-        lambda: ms(T.et[:, 1024:], 0.0, "et.z"),
-        lambda: ts(kc(1), mi, -3.0, A.mult, "mi", "k1", -0.5, A.add),
-        lambda: ts(kc(2), mi, float(S), A.mult, "mi", "bF", -1.0, A.add),
-        lambda: ts(kc(3), mi, -float(S), A.mult, "mi", "bB", float(TB + 1), A.add),
-        lambda: tt(kc(4), kc(1), th, A.add, "k1 thr", "rho"),
-        lambda: ts(kc(5), kc(4), 0.0, A.is_equal, "rho", "e0"),
-        lambda: ts(kc(6), kc(4), 2.0, A.is_equal, "rho", "e2"),
-        lambda: ts(kc(7), kc(6), -3.0, A.mult, "e2", "k7", 0.5, A.add),
-        lambda: ts(kc(8), kc(5), 3.0, A.mult, "e0", "k8", -1.5, A.add),
-        lambda: tt(kc(7), kc(7), th, A.add, "k7 thr", "k7"),
-        lambda: tt(kc(8), kc(8), th, A.add, "k8 thr", "k8"),
-        lambda: ts(T.om[:, 0:4], th, -0.5, A.add, "thr", "om.0"),
-        lambda: ts(kc(9), kc(5), 2.0, A.mult, "e0", "sz", -1.0, A.add),
-        lambda: ts(T.om[:, 4:12], kc(7, 2), 63.0, A.min, "k7 k8", "om.1"),
-        lambda: ts(kc(10), kc(6), -2.0, A.mult, "e2", "sy", 1.0, A.add),
-        lambda: ts(kc(11), mi, float(S), A.mult, "mi", "hm", -float(TB // 2 + 1), A.add),
-        lambda: tt(kc(9), kc(9), kc(0), A.mult, "sz nl", "sz"),
-        lambda: tt(kc(10), kc(10), kc(0), A.mult, "sy nl", "sy"),
-        lambda: ts(kc(12), kc(0), -float(5 * TB // 2 + 1), A.mult, "nl", "k12", float(3 * TB), A.add),
-        lambda: ts(kc(13), kc(0), -float(5 * TB // 2 + 2), A.mult, "nl", "k13", float(3 * TB + 1), A.add),
-        lambda: tt(kc(14), kc(9), kc(11), A.mult, "sz hm", "k14"),
-        lambda: tt(kc(15), kc(10), kc(11), A.mult, "sy hm", "k15"),
-        lambda: ms(T.ft[:, 0:S], 0.0, "ft.0.0 ft.0.1"),
-        lambda: tt(kc(14, 2), kc(14, 2), kc(12, 2), A.add, "k12 k13 k14 k15", "k14 k15"),
-        lambda: ts(kc(16, 2), kc(5, 2), -float(S), A.mult, "e0 e2", "ex", float(S), A.add),
-        lambda: ms(T.sv[:, 0:K], 1.0, "sv.0"),
-        lambda: ms(T.wt[:, 0::3], 129.0 / 128.0, "wt.0"),
-        lambda: ms(T.wt[:, 1::3], 0.0, "wt.1"),
-        lambda: ms(T.wt[:, 2::3], 1.0, "wt.2"),
-        lambda: ms(T.ut[:, K:K + 1], float(C - 1), "ut.e"),
+        lambda: ms(T.et[:, 1280:], 0.0, "et.z1"),
+        lambda: ms(T.col[:, 0:1], 0.0, "col.z"),
+        lambda: ms(T.dc[:, 1::2], 1.0 / 1024.0, "dc.1"),
+        lambda: ms(T.ones[:], 1.0, "ones"),
+        lambda: ms(T.vf[:, 0::3], -1.0, "vf.0"),
+        lambda: ms(T.vf[:, 2::3], 0.0, "vf.2"),
+        lambda: ms(T.vb[:, 0::3], 0.0, "vb.0"),
+        lambda: ms(T.vb[:, 2::3], -1.0, "vb.2"),
+        lambda: ms(T.ff[:, 0:S], 0.0, "ff.0"),
+        lambda: ms(T.fb[:, TB:], 0.0, "fb.%d" % NB),
+        lambda: ms(T.ut[:, K:K + 1], (C - 1) * U, "ut.e"),
+        lambda: tt(T.kb[:], T.km[:, 0:K], T.nr[:, 0:K], A.subtract, "km nr.0 nr.1 nr.2", "kb"),
+        lambda: tt(T.kp[:], T.km[:, 0:K], T.nr[:, 0:K], A.add, "km nr.0 nr.1 nr.2", "kp"),
     ]
 
     def fill(n):
@@ -246,22 +224,36 @@ def rank_program(g, core, T, topo):
 
     xs = [T.xin, T.x1, T.x2]
 
+    def xnames(t, h):
+        return "X0.%d" % h if t == 0 else " ".join("X%d.%d.%d" % (t, h, b) for b in range(4))
+
     def quant_state(t, h):
         quant(T["tq%d" % t][:, H * h:H * h + H], T["ts%d" % t][:, H * h:H * h + H],
-              xs[t][:, 4 * H * h:4 * H * (h + 1)], "X%d.%d" % (t, h) if t == 0 else
-              " ".join("X%d.%d.%d" % (t, h, b) for b in range(4)), "tq%d.%d" % (t, h))
+              xs[t][:, 4 * H * h:4 * H * (h + 1)], xnames(t, h), "tq%d.%d" % (t, h))
 
     def score(t, h):
-        mm(h, H, T.ur[:], T.urs[:], T["tq%d" % t][:, H * h:H * h + H], T["ts%d" % t][:, H * h:H * h + H],
-           "ur urs tq%d.%d" % (t, h))
+        for e in range(2):
+            mm(2 * h + e, H, T.ur[:], T.urs[:], T["tq%d" % t][:, H * h:H * h + H], T["ts%d" % t][:, H * h:H * h + H],
+               "ur urs tq%d.%d" % (t, h))
+        act(T.so[:, 112 * h:112 * h + 112], bank(2 * h + 1, 1, H, 2), F.Copy, "ps%d" % (2 * h + 1), "so.%d" % h)
+        act(T.se[:, 112 * h:112 * h + 112], bank(2 * h + 1, 0, H, 2), F.Copy, "ps%d" % (2 * h + 1), "se.%d" % h)
 
     def masked(h):
-        tt(T.am[:, H * h:H * h + H], bank(h, 0, H), T.k2[:], A.add, "ps%d k2.0 k2.1" % h, "am.%d" % h)
+        tt(T.am[:, H * h:H * h + H], bank(2 * h, 0, H), T.k2[:], A.subtract, "ps%d k2" % (2 * h), "am.%d" % h)
+
+    def larger(h):
+        tt(T.mx[:, 112 * h:112 * h + 112], bank(2 * h, 0, H, 2), T.so[:, 112 * h:112 * h + 112], A.max,
+           "ps%d so.%d" % (2 * h, h), "mx.%d" % h)
+
+    def wrapped(h):
+        v = slice(H * h, H * h + H)
+        scan(T.wm[:, v], T.r32[:], T.am[:, v], -BIG, A.min, A.max, "am.%d r32" % h, "wm.%d" % h)
+
+    def half_x(t, j):
+        v = slice(C * j, C * j + C)
+        act(T.xh[:, v], xs[t][:, v], F.Copy, xnames(t, j // 2), "xh.%d" % j, scale=0.5)
 
     def compare(src, step, n, w, wname, sname, tile, tname, tmp, tmpname, acols, eqslot):
-        def view(buf, lo, hi):
-            return buf[:, step * lo + step - 1:step * hi:step]
-
         def slot(s, lo, hi):
             o = 4 * n * (s // 4)
             return tile[:, o + s % 4 + 4 * lo:o + 4 * hi:4]
@@ -275,7 +267,7 @@ def rank_program(g, core, T, topo):
                     "%s.%d.1" % (tname, s), bias=1.0)
         for k, (s, c) in enumerate(acols):
             e = step * (16 * c + 16)
-            act(tmp[:, n * k:n * k + n], view(src, 0, n), F.Sign, sname + " " + wname, "%s.%d" % (tmpname, k),
+            act(tmp[:, n * k:n * k + n], src[:, 0:n], F.Sign, sname + " " + wname, "%s.%d" % (tmpname, k),
                 scale=-1.0, bias=w[:, e - 1:e])
             if k:
                 second(k - 1)
@@ -284,12 +276,12 @@ def rank_program(g, core, T, topo):
         def vcol(s, c):
             m = 16 * c + 16
             sc = w[:, step * m - 1:step * m]
-            ts(slot(s, 0, m), view(src, 0, m), sc, A.is_lt, sname + " " + wname, "%s.%d.0" % (tname, s))
+            ts(slot(s, 0, m), src[:, 0:m], sc, A.is_lt, sname + " " + wname, "%s.%d.0" % (tname, s))
             if m < n:
-                ts(slot(s, m, n), view(src, m, n), sc, A.is_le, sname + " " + wname, "%s.%d.1" % (tname, s))
+                ts(slot(s, m, n), src[:, m:n], sc, A.is_le, sname + " " + wname, "%s.%d.1" % (tname, s))
 
         def eqs():
-            tt(slot(eqslot, 0, n), view(src, 0, n), view(w, 0, n), A.is_equal, sname + " " + wname,
+            tt(slot(eqslot, 0, n), src[:, 0:n], w[:, step - 1:step * n:step], A.is_equal, sname + " " + wname,
                "%s.%d.0" % (tname, eqslot))
         return vcol, eqs
 
@@ -301,36 +293,41 @@ def rank_program(g, core, T, topo):
         score(0, h)
     fill(2)
     masked(0)
+    quant(T.ekq[:], T.eks[:], T.ek[:], " ".join("ek.%d" % j for j in range(8)), "ekq")
+    wrapped(0)
+    larger(0)
 
     for t in range(2):
         tq, tsc, lq, ls = T["tq%d" % t], T["ts%d" % t], T["lq%d" % t], T["ls%d" % t]
-        ra, ht, lra, lh, tb = T["ra%d" % t], T["ht%d" % t], T["lr%d" % t], T["lh%d" % t], T["tb%d" % t]
+        ra, lra, tf, tb = T["ra%d" % t], T["lr%d" % t], T["tf%d" % t], T["tb%d" % t]
         send(t, [(lq[:].bitcast(dt.uint8), tq[:].bitcast(dt.uint8)), (ls[:], tsc[:])],
-             "tq%d.0 tq%d.1" % (t, t), "ar%d" % (3 * t), "lq")
+             "tq%d.0 tq%d.1" % (t, t), "ar%d" % (2 * t), "lq")
         if t == 0:
-            clear_table(0, "lq")
-            iota(T.eb[:], [[0, 2048]], 0, 0, "eb", True)
+            clear_tables(0, "lq")
+            iota(T.nb[:], [[S, NB], [0, 3]], 0, 0, "nb")
+            iota(T.nr[:, 0:33], [[S, 11], [0, 3]], 0, 0, "nr.0")
+            iota(T.nr[:, 32:33], [[0, 1]], 0, 0, "nr.0 nr.1")
+            iota(T.nr[:, 33:], [[S, 11], [0, 3]], S, 0, "nr.2")
+            iota(T.pws[:], [[-16, 28], [2047, 16]], 512, 0, "pws")
+            iota(T.eb[:], [[0, 2048]], 0, 0, "eb")
             for b in range(4):
                 v = T.eb[:, 512 * b + b:512 * b + 512:4]
                 op("g", lambda: g.affine_select(v, v, [[-1, 128]], A.not_equal, 1.0, 0, 1), "eb", "eb.%d" % b)
 
-        for h in range(2):
-            v = slice(H * h, H * h + H)
-            if h:
-                masked(h)
-            scan(T.mx[:, v], T.rp[:], bank(h, 0, H), -BIG, A.min, A.max, "ps%d rp.0 rp.1" % h, "mx.%d" % h)
-            scan(T.wm[:, v], T.r32[:], T.am[:, v], -BIG, A.min, A.max, "am.%d r32" % h, "wm.%d" % h)
-        fill(2)
+        masked(1)
+        fill(1)
+        wrapped(1)
+        larger(1)
+        fill(1)
         vcol, eqs = compare(T.mx, 2, H, T.wm, "wm.0 wm.1", "mx.0 mx.1", T.ct, "ct", T.sg, "sg",
                             [(8 + i, c) for i, c in enumerate([0, 1, 2, 10, 11, 12])], 14)
-        for h in range(2):
-            act(T.se[:, 112 * h:112 * h + 112], bank(h, 0, H, 2), F.Copy, "ps%d" % h, "se.%d" % h)
-            act(T.so[:, 112 * h:112 * h + 112], bank(h, 1, H, 2), F.Copy, "ps%d" % h, "so.%d" % h)
+        half_x(t, 0)
+        half_x(t, 1)
 
         def tile1(q):
             quant(T.cq[:, H * q:H * q + H], T.cs[:, H * q:H * q + H], T.ct[:, 4 * H * q:4 * H * (q + 1)],
                   names("ct", q) + " ct.15", "cq.%d" % q)
-            mm(2, H, T.ekq[:], T.eks[:], T.cq[:, H * q:H * q + H], T.cs[:, H * q:H * q + H], "ekq cq.%d" % q,
+            mm(4, H, T.ekq[:], T.eks[:], T.cq[:, H * q:H * q + H], T.cs[:, H * q:H * q + H], "ekq cq.%d" % q,
                q == 0, q == 3)
         for s, c in enumerate([3, 4, 5, 6, 7, 8, 9, 13]):
             vcol(s, c)
@@ -340,12 +337,12 @@ def rank_program(g, core, T, topo):
         tile1(1)
         tile1(2)
         tile1(3)
-        fill(5)
+        fill(4)
 
-        ts(T.f1[:], bank(2, 0, H), 64.5, A.is_le, "ps2", "f1")
-        fill(2)
+        ts(T.f1[:], bank(4, 0, H), 64.5, A.is_le, "ps4", "f1")
+        fill(1)
         scan(T.p1[:], T.f1[:], T.f1[:], 0.0, A.add, A.max, "f1", "p1")
-        fill(2)
+        fill(1)
         for c in range(2):
             act(T.jk[:, 192 * c:192 * c + 192], T.p1[:, 0:192], F.Sign, "p1 thr", "acc.%d" % c, scale=-1.0,
                 bias=T.thr[:, c:c + 1], accum_out=T.acc[:, c:c + 1])
@@ -357,24 +354,30 @@ def rank_program(g, core, T, topo):
             scan(T.cn[:, 192 * c:192 * c + 192], v, v, 32.0, A.add, A.max, "cb.%d" % c, "cn.%d" % c)
         ts(T.oa[:, 0:2], T.acc[:], 0.5, A.mult, "acc.0 acc.1", "oa.0", 96.0, A.add)
         cp(T.oa[:, 2:4], T.cn[:, 191::192], "cn.0 cn.1", "oa.1")
-        fill(2)
+        fill(1)
 
         act(T.cd[:, 0::2], T.se[:].indirect(T.oa[:]), F.Copy, "se.0 se.1 oa.0 oa.1", "cd.0")
         act(T.cd[:, 1::2], T.so[:].indirect(T.oa[:]), F.Copy, "so.0 so.1 oa.0 oa.1", "cd.1")
-        tt(T.a2[:, 0::2], T.se[:].indirect(T.oa[:]), T.km[:, 0:128:2], A.add, "se.0 se.1 oa.0 oa.1 km", "a2.0")
-        tt(T.a2[:, 1::2], T.so[:].indirect(T.oa[:]), T.km[:, 1:128:2], A.add, "so.0 so.1 oa.0 oa.1 km", "a2.1")
-        fill(2)
+        tt(T.a2[:, 0::2], T.se[:].indirect(T.oa[:]), T.km[:, 0:128:2], A.subtract, "se.0 se.1 oa.0 oa.1 km", "a2.0")
+        tt(T.a2[:, 1::2], T.so[:].indirect(T.oa[:]), T.km[:, 1:128:2], A.subtract, "so.0 so.1 oa.0 oa.1 km", "a2.1")
+        fill(1)
         wrap_scan(T.w2, T.a2, 128, "a2.0 a2.1", "w2")
-        fill(2)
+        fill(1)
+        act(T.col[:, 1::2], T.iof[:].indirect(T.oa[:]), F.Identity, "iof oa.0 oa.1", "col.0", scale=2.0 / 1024.0)
+        act(T.col[:, 2::2], T.iof[:].indirect(T.oa[:]), F.Identity, "iof oa.0 oa.1", "col.1", scale=2.0 / 1024.0,
+            bias=1.0 / 1024.0)
         vcol, eqs = compare(T.cd, 1, 128, T.w2, "w2", "cd.0 cd.1", T.et, "et", T.sg2, "sh",
                             [(4, 0), (5, 1), (6, 6)], 8)
-        act(T.col[:, 0::2], T.iof[:].indirect(T.oa[:]), F.Identity, "iof oa.0 oa.1", "col.0", scale=2.0)
-        act(T.col[:, 1::2], T.iof[:].indirect(T.oa[:]), F.Identity, "iof oa.0 oa.1", "col.1", scale=2.0, bias=1.0)
+        half_x(t, 2)
+        half_x(t, 3)
+        if t == 0:
+            act(T.c2v[:], T.iof[:, 0:K], F.Identity, "iof", "c2v", scale=2.0, bias=2.0)
+            act(T.pw[:], T.pws[:], F.Abs, "pws pc.2", "pw", scale=U, bias=T.pc[:, 2:3])
 
         def tile2(q, first, last):
             quant(T.eq[:, 128 * q:128 * q + 128], T.es[:, 128 * q:128 * q + 128], T.et[:, 512 * q:512 * q + 512],
-                  names("et", q) + " et.z", "eq.%d" % q)
-            mm(3, 128, T.ekq[:], T.eks[:], T.eq[:, 128 * q:128 * q + 128], T.es[:, 128 * q:128 * q + 128],
+                  names("et", q) + " et.z0 et.z1", "eq.%d" % q)
+            mm(5, 128, T.ekq[:], T.eks[:], T.eq[:, 128 * q:128 * q + 128], T.es[:, 128 * q:128 * q + 128],
                "ekq eq.%d" % q, first, last)
         eqs()
         for s, c in [(7, 5), (0, 7), (1, 3), (2, 4), (3, 2)]:
@@ -382,119 +385,122 @@ def rank_program(g, core, T, topo):
         tile2(2, True, False)
         tile2(1, False, False)
         tile2(0, False, True)
-        fill(4)
-        tt(T.a3[:, 0:128], bank(3, 0, 128), T.km[:, 0:128], A.add, "ps3 km", "a3")
-        ts(T.f2[:], bank(3, 0, 128), 64.5, A.is_le, "ps3", "f2", 2.0, A.mult)
-        wrap_scan(T.w3, T.a3, 128, "a3", "w3")
-        scan(T.p2[:], T.f2[:], T.f2[:], 0.0, A.add, A.max, "f2", "p2")
+        tt(T.dc[:, 0::2], T.col[:, 1::2], T.col[:, 0:128:2], A.subtract, "col.z col.0 col.1", "dc.0")
+        fill(2)
+        tt(T.a3[:], bank(5, 0, 128), T.km[:], A.subtract, "ps5 km", "a3.0 a3.1")
+        ts(T.f2[:], bank(5, 0, 128), 64.5, A.is_le, "ps5", "f2", 2.0, A.mult)
+        wrap_scan(T.w3, T.a3, 128, "a3.0 a3.1", "w3")
+        scan(T.p2[:], T.f2[:], T.dc[:], 0.0, A.add, A.add, "f2 dc.0 dc.1", "p2")
         ts(T.or2[:], T.w3[:, 15:128:16], -1.0, A.add, "w3", "or2")
+        fill(1)
         cp(ra[:].indirect(T.or2[:]), T.p2[:], "p2 or2", "ra%d" % t)
-        send(t, [(lra[:], ra[:, 0:K])], "ra%d" % t, "ar%d" % (3 * t + 1), "lra")
-
-        cp(ht[:].indirect(T.or2[:, 0:4]), T.col[:, 0:K], "col.0 col.1 or2", "ht%d" % t)
-        tt(T.a3[:, 0:K], ra[:, 0:K], T.km[:, 0:K], A.add, "ra%d km" % t, "a3")
-        cp(ht[:].indirect(T.or2[:, 4:8]), T.col[:, K:], "col.0 col.1 or2", "ht%d" % t)
-        send(t, [(lh[:], ht[:, 0:K])], "ht%d" % t, "ar%d" % (3 * t + 2), "lh")
+        send(t, [(lra[:], ra[:, 0:K])], "ra%d" % t, "ar%d" % (2 * t + 1), "lra")
         if t == 0:
-            clear_table(1, "lh")
-        wrap_scan(T.w3, T.a3, K, "a3", "w3")
-        fill(2)
-        ts(T.ora[:], T.w3[:, 15:K:16], 0.5, A.mult, "w3", "ora", -1.0, A.add)
-        fill(2)
-        cp(T.kt[:].indirect(T.ora[:]), T.iof[:, 0:K], "iof ora", "kt")
-        fill(2)
-        tt(T.a3[:], T.kt[:].indirect(T.om[:]), T.km[:], A.add, "kt km om.0 om.1", "a3")
-        fill(2)
-        wrap_scan(T.w3, T.a3, 192, "a3", "w3")
-        fill(2)
-        cp(T.ok[:], T.w3[:, 15::16], "w3", "ok")
-        cp(T.at[:].indirect(T.ora[:]), ht[:, 0:K], "ht%d ora" % t, "at")
-        for c in range(28):
-            act(T.jv[:, K * c:K * c + K], T.at[:], F.Sign, "at thr", "va.%d" % c, scale=-1.0,
-                bias=T.thr[:, c:c + 1], accum_out=T.vacc[:, c:c + 1])
-        act(T.bm[:, 0:K], lh[:].indirect(T.ok[:, 0:4]), F.Identity, "lh ok", "bm.0", bias=-1.0)
-        act(T.bm[:, K:], lh[:].indirect(T.ok[:, 0:4]), F.Identity, "lh ok", "bm.1", bias=1023.0)
-        act(T.xh[:], xs[t][:], F.Copy, "X0.0 X0.1" if t == 0 else
-            " ".join("X1.%d.%d" % (h, b) for h in range(2) for b in range(4)), "xh", scale=0.5)
+            clear_tables(1, "lra")
 
-        x, y, z = T.w4[:, 15:K:16], T.w4[:, K + 15:2 * K:16], T.w4[:, 2 * K + 15::16]
-
-        def sm(i, n=1):
-            return T.sm[:, 4 * i:4 * i + 4 * n]
-        tbn = "tb%d" % t
-        tt(T.a4[:], lra[:].indirect(T.ok[:]), T.km[:], A.add, "lra ok km", "a4")
         fill(2)
-        wrap_scan(T.w4, T.a4, 192, "a4", "w4")
+        tt(T.a3[:, 0:K], ra[:, 0:K], T.km[:, 0:K], A.subtract, "ra%d km" % t, "a3.0")
+        fill(2)
+        wrap_scan(T.w3, T.a3, K, "a3.0", "w3")
         fill(9)
-        tt(sm(0), x, y, A.subtract, "w4", "s0")
-        tt(sm(1), x, z, A.subtract, "w4", "s1")
-        tt(sm(2), z, y, A.subtract, "w4", "s2")
-        tt(sm(3), y, z, A.subtract, "w4", "s3")
-        tt(sm(7), sm(0), kc(10), A.mult, "s0 sy", "s7")
-        tt(sm(6), sm(1), kc(9), A.mult, "s1 sz", "s6")
-        tt(sm(16), kc(2), x, A.add, "w4 bF", "s16")
-        tt(sm(8, 2), sm(0, 2), sm(2, 2), A.mult, "s0 s1 s2 s3", "s8")
-        tt(sm(17), kc(3), x, A.subtract, "w4 bB", "s17")
-        tt(sm(4), x, kc(9), A.mult, "w4 sz", "s4")
-        tt(sm(5), x, kc(10), A.mult, "w4 sy", "s5")
-        tt(sm(12, 2), sm(6, 2), sm(8, 2), A.min, "s6 s7 s8", "s12")
-        cp(T.od[:, 0:8], sm(16, 2), "s16 s17", "od.0")
-        tt(sm(10, 2), sm(4, 2), kc(14, 2), A.add, "s4 s5 k14 k15", "s10")
-        ts(sm(14), sm(12), 0.0, A.is_lt, "s12", "s14", float(TB), A.mult)
-        ts(sm(15), sm(13), 0.0, A.is_lt, "s12", "s15", float(2 * TB), A.mult)
-        cp(tb[:].indirect(T.od[:, 0:4]), T.sv[:, 0:K], "od.0 sv.0 " + tbn, tbn)
-        tt(sm(18, 2), sm(10, 2), sm(14, 2), A.add, "s10 s14 s15", "s18")
-        tt(sm(20, 2), sm(16, 2), kc(16, 2), A.add, "s16 s17 ex", "s20")
-        cp(tb[:].indirect(T.od[:, 4:8]), T.sv[:, 0:K], "od.0 sv.0 " + tbn, tbn)
-        cp(T.od[:, 8:16], sm(18, 2), "s18", "od.1")
-        cp(T.oe[:], sm(20, 2), "s20", "oe")
-        cp(tb[:].indirect(T.od[:, 8:16]), T.sv[:, K:], "od.1 sv.1 " + tbn, tbn)
+        ts(T.ora[:], T.w3[:, 15:K:16], 0.5, A.mult, "w3", "ora", -1.0, A.add)
+        if t == 0:
+            tt(T.a3[:, 0:K], T.nb[:, 2:66], T.kp[:], A.subtract, "nb kp", "a3.0")
+            tt(T.a3[:, K:], T.nb[:, 1:65], T.kp[:], A.subtract, "nb kp", "a3.1")
+        cp(T.av[:].indirect(T.ora[:]), ra[:, 0:K], "ra%d ora" % t, "av")
+        if t == 0:
+            wrap_scan(T.w3, T.a3, 128, "a3.0 a3.1", "w3")
+        tt(T.af[:], T.av[:], T.c2v[:], A.subtract, "av c2v", "af")
+        if t == 0:
+            ts(T.ce[:, 0:4], T.w3[:, 15:K:16], -2.0, A.add, "w3", "ce.0")
+            ts(T.ce[:, 4:8], T.w3[:, K + 15::16], -1.0, A.add, "w3", "ce.1")
+        for c in range(28):
+            act(T.jv[:, K * c:K * c + K], T.af[:], F.Sign, "af thr", "va.%d" % c, scale=-1024.0,
+                bias=T.thr[:, c:c + 1], accum_out=T.vacc[:, c:c + 1])
+
+        bv, x = T.bv, T.w4[:, 15::16]
+        bf, t1, dl, b2, gl, k0, kq = [T.sf[:, K * i:K * i + K] for i in range(7)]
+
+        def sm(i):
+            return T.sm[:, 32 * i:32 * i + 21]
+
+        def put(d, what, h):
+            tab = (tf, tb)[d][:, S * MID * h:S * (MID + 1) if h == 0 else TB]
+            odd = d if what else 1 - d
+            vals, vn = ((T.vf, "vf.0 vf.1 vf.2"), (T.vb, "vb.0 vb.1 vb.2"))[d] if what else (T.ones, "ones")
+            n = "t%d.%d" % (d, h)
+            cp(tab.indirect(T.od[:, 4 * odd + 2 * h:4 * odd + 2 * h + 2]), vals[:, 32 * h:32 * h + 32],
+               "od.%d tz%d t%d.%d %s" % (odd, t, d, 1 - h, vn), n)
+        cp(bv[:].indirect(T.ora[:]), lra[:], "lra ora", "bv")
+        tt(T.a4[:], bv[:], T.kb[:], A.subtract, "bv kb", "a4")
+        tt(sm(0), bv[:, 0:63:3], bv[:, 1:63:3], A.is_lt, "bv", "s0")
+        tt(sm(1), bv[:, 1:63:3], bv[:, 2:63:3], A.is_gt, "bv", "s1")
+        wrap_scan(T.w4, T.a4, K, "a4", "w4")
+        tt(sm(2), bv[:, 2:63:3], bv[:, 0:63:3], A.is_gt, "bv", "s2")
+        tt(sm(3), sm(0), sm(1), A.subtract, "s0 s1", "s3")
+        ts(T.od[:, 4:8], x, -1.0, A.add, "w4", "od.1")
+        ts(T.od[:, 0:4], x, -2.0, A.add, "w4", "od.0")
+        tt(T.vf[:, 1:63:3], sm(3), sm(2), A.subtract, "s2 s3", "vf.1")
+        tt(T.vb[:, 1:63:3], sm(3), sm(2), A.subtract, "s2 s3", "vb.1")
+        put(0, 0, 0)
+        put(1, 0, 1)
+        put(0, 1, 0)
+        put(1, 1, 1)
 
         def unpack(b):
             v = slice(128 * b, 128 * b + 128)
             if t == 0:
                 quant(T.ebq[:, v], T.ebs[:, v], T.eb[:, 512 * b:512 * b + 512], "eb.%d" % b, "ebq.%d" % b)
-            mm(4 + b, C, T.ebq[:, v], T.ebs[:, v], lq[:], ls[:], "ebq.%d lq" % b)
-            act(T.dh[:, C * b:C * b + C], bank(4 + b, 0, C), F.Copy, "ps%d" % (4 + b), "dh.%d" % b, scale=0.5)
-        unpack(0)
-        for k in range(NB):
-            for e in range(2):
-                lo = S * k + 128 * e
-                scan(T.ft[:, lo + S:lo + S + 128], tb[:, lo:lo + 128], T.ft[:, lo:lo + 128], 0.0,
-                     A.add, A.max, "%s ft.%d.%d" % (tbn, k, e), "ft.%d.%d" % (k + 1, e))
-            if k < 3:
-                unpack(k + 1)
-            if k == 4 and t == 0:
-                quant(T.vq[:], T.vs[:], T.vin[:], "vin", "vq")
-            if k == 18:
-                ts(T.ov[:], T.vacc[:], 0.5, A.mult, " ".join("va.%d" % c for c in range(28)), "ov", 32.0, A.add)
-            if k == NB - 1:
-                tt(T.dl[:], T.bm[:, K:], T.at[:], A.subtract, "bm.1 at", "dl")
+            mm(b, C, T.ebq[:, v], T.ebs[:, v], lq[:], ls[:], "ebq.%d lq" % b)
+            act(T.dh[:, C * b:C * b + C], bank(b, 0, C), F.Copy, "ps%d" % b, "dh.%d" % b, scale=0.5)
+        inside = [
+            lambda: put(0, 0, 1), lambda: put(1, 0, 0), lambda: put(0, 1, 1), lambda: put(1, 1, 0),
+            lambda: unpack(0), lambda: unpack(1), lambda: unpack(2), lambda: unpack(3),
+            lambda: tt(T.oes[:, 0:4], x, T.ce[:, 0:4], A.add, "w4 ce.0", "oes.0"),
+            lambda: tt(T.oes[:, 4:8], x, T.ce[:, 4:8], A.add, "w4 ce.1", "oes.1"),
+            lambda: cp(T.bi[:], bv[:], "bv", "bi"),
+            lambda: cp(T.oe[:], T.oes[:], "oes.0 oes.1", "oe"),
+            lambda: tt(bf, bv[:], T.bi[:], A.subtract, "bv bi", "bf"),
+            lambda: tt(t1, bf, T.af[:], A.subtract, "bf af", "t1"),
+            lambda: ts(b2, bf, 1024.0 * U, A.mult, "bf", "b2", 1023.0 * U, A.add),
+            lambda: ts(dl, t1, 1024.0 * U, A.mult, "t1", "dl", 512.0 * U, A.add),
+            lambda: ts(T.ov[:], T.vacc[:], 0.5, A.mult, " ".join("va.%d" % c for c in range(28)), "ov", 32.0, A.add),
+        ]
+        if t == 0:
+            inside.append(lambda: quant(T.vq[:], T.vs[:], T.vin[:], "vin", "vq"))
 
-        fts = " ".join("ft.%d.%d" % (k, e) for k in range(NB + 1) for e in range(2))
-        ts(T.lr[:, 0:K], T.ft[:].indirect(T.oe[:, 0:4]), 129.0 / 128.0, A.mult, fts + " oe", "lr.0")
-        tt(T.lr[:, K:], T.ft[:].indirect(T.oe[:, 4:8]), T.wt[:], A.add, fts + " oe wt.0 wt.1 wt.2", "lr.1")
-        ts(T.pm[:, 0:1], T.ft[:, NB * S + 127:NB * S + 128], 1.0, A.add, fts, "pm.0")
-        tt(T.key[:], T.lr[:, 0:K], T.lr[:, K:], A.add, "lr.0 lr.1", "key")
-        scan(T.pm[:, 1:], T.key[:], T.key[:], T.pm[:, 0:1], A.max, A.max, "key pm.0", "pm.1")
-        cc = T.cc
-        tt(cc[:, 0:K], T.pm[:, 1:], T.pm[:, 0:K], A.is_gt, "pm.0 pm.1", "cc.0")
-        tt(cc[:, 2 * K - 1:K - 1:-1], T.pm[:, 1:], T.pm[:, 0:K], A.is_le, "pm.0 pm.1", "cc.1")
-        act(cc[:, 2 * K:3 * K], cc[:, 0:K], F.Identity, "cc.0", "cc.2", scale=-1.0, bias=1.0)
-        tt(cc[:, 5 * K:], cc[:, 0:K], T.bm[:, 0:K], A.mult, "cc.0 bm.0", "cc.5")
-        tt(cc[:, 4 * K - 1:3 * K - 1:-1], cc[:, 0:K], T.dl[:], A.mult, "cc.0 dl", "cc.3")
-        tt(cc[:, 4 * K:5 * K], cc[:, 0:K], T.dl[:], A.mult, "cc.0 dl", "cc.4")
-        scan(T.ut[:, K - 1::-1], cc[:, K:2 * K], cc[:, 6 * K - 1:5 * K - 1:-1], float(C - 1), A.mult, A.add,
-             "cc.1 cc.5", "ut")
-        scan(T.zz[:, 1:], cc[:, K:3 * K], cc[:, 3 * K:5 * K], 0.0, A.mult, A.add, "cc.1 cc.2 cc.3 cc.4", "zz")
+        def back(buf, m):
+            return buf[:, S * m + S - 1:S * m - 1 if m else None:-1]
+        for k in range(NB):
+            m = NB - 1 - k
+            scan(T.ff[:, S * k + S:S * k + 2 * S], tf[:, S * k:S * k + S], T.ff[:, S * k:S * k + S], 0.0, A.add, A.max,
+                 "ff.%d t0.0" % k + (" t0.1" if k >= MID else ""), "ff.%d" % (k + 1))
+            scan(back(T.fb, m), back(tb, m), back(T.fb, m + 1), 0.0, A.add, A.max,
+                 "fb.%d t1.1" % (m + 1) + (" t1.0" if m <= MID else ""), "fb.%d" % m)
+            if inside:
+                inside.pop(0)()
+
+        ffs = " ".join("ff.%d" % k for k in range(NB + 1))
+        fbs = " ".join("fb.%d" % k for k in range(NB + 1))
+        act(gl, T.ff[:].indirect(T.oe[:, 0:4]), F.Copy, ffs + " oe", "gl", scale=129.0 / 128.0)
+        ts(T.m0[:, 0:1], T.ff[:, TB + S - 1:], -1.0, A.add, ffs, "m0.0")
+        tt(T.gr[:, 0:K], T.fb[:].indirect(T.oe[:, 4:8]), dl, A.add, fbs + " oe dl", "gr.0")
+        tt(k0, T.fb[:].indirect(T.oe[:, 4:8]), gl, A.add, fbs + " oe gl", "k0")
+        tt(T.gr[:, K:], T.gr[:, 0:K], gl, A.add, "gr.0 gl", "gr.1")
+        scan(T.m0[:, 1:], k0, k0, T.m0[:, 0:1], A.max, A.max, "k0 m0.0", "m0.1")
+        tt(kq, k0, b2, A.subtract, "k0 b2", "kq")
+        scan(T.m1[:], T.gr[:], T.gr[:], 0.0, A.max, A.max, "gr.0 gr.1", "m1")
+        tt(T.xu[:], T.m0[:, 0:K], kq, A.subtract, "m0.0 m0.1 kq", "xu")
+        tt(T.dq[:], T.m1[:, K - 1:], T.m0[:], A.subtract, "m1 m0.0 m0.1", "dq")
+        scan(T.ut[:, K - 1::-1], T.xu[:, ::-1], T.xu[:, ::-1], (C - 1) * U, A.min, A.min, "xu", "ut")
         halves = [(slice(H * h, H * h + H), slice(14 * h, 14 * h + 14), h) for h in range(2)]
         for v, o, h in halves:
             act(T.ug[:, v], T.ut[:].indirect(T.ov[:, o]), F.Copy, "ut ut.e ov", "ug.%d" % h)
-            tt(T.fw[:, v], T.zz[:, 64:].indirect(T.ov[:, o]), T.pw[:, v], A.subtract, "zz ov pw", "fw.%d" % h)
+            tt(T.fw[:, v], T.dq[:].indirect(T.ov[:, o]), T.pw[:, v], A.subtract, "dq ov pw", "fw.%d" % h)
         for v, o, h in halves:
             scan(T.qs[:, v], T.fw[:, v], T.ug[:, v], 0.0, A.max, A.min, "fw.%d ug.%d" % (h, h), "qs.%d" % h)
         for v, o, h in halves:
-            cp(T.oqo[:, o], T.qs[:, H * h + 15:H * h + H:16], "qs.%d" % h, "oqo.%d" % h)
+            ts(T.oqo[:, o], T.qs[:, H * h + 15:H * h + H:16], 1.0 / U, A.mult, "qs.%d" % h, "oqo.%d" % h)
         qr = T["qr%d" % t]
         act(qr[:], T.iof[:].indirect(T.oqo[:]), F.Copy, "iof oqo.0 oqo.1", "qr%d" % t)
         dma("s", T.oq[:, C * t:C * t + C], qr[0:128:16, :], r="qr%d" % t)
@@ -504,7 +510,7 @@ def rank_program(g, core, T, topo):
         def mid(h, b):
             v = slice(4 * H * h + b, 4 * H * (h + 1), 4)
             tt(T.gt[:, v], T.dh[:, C * b:C * b + C].indirect(T.oqo[:, 14 * h:14 * h + 14]), T.xh[:, v], A.add,
-               "dh.%d oqo.%d xh" % (b, h), "gt.%d.%d" % (h, b))
+               "dh.%d oqo.%d xh.%d xh.%d" % (b, h, 2 * h, 2 * h + 1), "gt.%d.%d" % (h, b))
 
         def layer(h):
             quant(T.gq[:, H * h:H * h + H], T.gs[:, H * h:H * h + H], T.gt[:, 4 * H * h:4 * H * (h + 1)],
@@ -547,6 +553,9 @@ def rank_program(g, core, T, topo):
         if t == 0:
             masked(0)
         done(1)
+        if t == 0:
+            wrapped(0)
+            larger(0)
     for k in range(4):
         dma("s", T.osc[4 * k:4 * k + 4, :], T.ts2[32 * k:32 * k + 4, :], r="tq2.0 tq2.1")
 

@@ -1,8 +1,11 @@
 from concourse.mybir import dt, AluOpType, ActivationFunctionType
 
-C, H, K = 448, 224, 64
+C, H, P, K = 448, 224, 112, 64
+W = H - K + 16
 S, NB, MID = 128, 22, 10
 TB = NB * S
+CUT = (H, 256)
+NA = 4
 BIG = 1.0e29
 FAR = 2.0 ** 90
 U = 2.0 ** -17
@@ -14,7 +17,7 @@ def _sb(n, d):
 
 
 SCRATCH = {
-    "xin": _sb(4 * C, BF), "x1": _sb(4 * C, BF), "x2": _sb(4 * C, BF), "xh": _sb(4 * C, BF), "gt": _sb(4 * C, BF),
+    "xin": _sb(4 * C, BF), "x1": _sb(4 * C, BF), "x2": _sb(4 * C, BF), "xh": _sb(4 * C, BF), "yt": _sb(4 * C, BF),
     "dh": _sb(4 * C, BF), "rl": _sb(4 * C, F32), "ysb": _sb(C, F32),
     "uin": _sb(512, BF), "vin": _sb(512, BF), "uq": _sb(128, X4), "us": _sb(128, U8), "ur": _sb(128, X4),
     "urs": _sb(128, U8), "vq": _sb(128, X4), "vs": _sb(128, U8), "wq": _sb(512, X4), "wsc": _sb(512, U8),
@@ -22,28 +25,28 @@ SCRATCH = {
     "lq0": _sb(C, X4), "lq1": _sb(C, X4), "ls0": _sb(C, U8), "ls1": _sb(C, U8), "gq": _sb(C, X4), "gs": _sb(C, U8),
     "eb": _sb(2048, BF), "ebq": _sb(512, X4), "ebs": _sb(512, U8), "ek": _sb(512, BF), "ekq": _sb(128, X4),
     "eks": _sb(128, U8),
-    "ct": _sb(16 * H, BF), "cq": _sb(4 * H, X4), "cs": _sb(4 * H, U8), "sg": _sb(6 * H, BF),
+    "ct": _sb(4 * 960, BF), "cq": _sb(1024, X4), "cs": _sb(1024, U8), "sg": _sb(16 * P, BF),
     "et": _sb(12 * 128, BF), "eq": _sb(3 * 128, X4), "es": _sb(3 * 128, U8), "sg2": _sb(4 * 128, BF),
     "jm": _sb(256, F32), "pws": _sb(C, F32), "pw": _sb(C, F32), "km": _sb(128, F32), "k2": _sb(H, F32),
     "r32": _sb(H, BF), "r16": _sb(128, BF), "iof": _sb(C, F32), "isml": _sb(32, I32), "blk": _sb(32, F32),
     "ones": _sb(K, BF), "oul": _sb(8, U16), "pc": _sb(8, F32), "thr": _sb(28, F32), "zt": _sb(TB // 4, BF),
-    "nb": _sb(66, F32), "nr": _sb(66, F32), "kb": _sb(K, F32), "kp": _sb(K, F32), "ce": _sb(8, F32),
-    "c2v": _sb(K, F32),
-    "mx": _sb(H, F32), "am": _sb(C, F32), "wm": _sb(C, F32), "se": _sb(H, F32), "so": _sb(H, F32),
-    "f1": _sb(H, BF), "p1": _sb(H, BF), "cb": _sb(384, BF), "cn": _sb(384, BF), "jk": _sb(384, BF),
+    "nb": _sb(66, F32), "nr": _sb(66, F32), "kc": _sb(4 * K, F32), "ce": _sb(8, F32), "rz": _sb(128, BF),
+    "cw": _sb(1024, BF), "ec": _sb(128, BF),
+    "mx": _sb(P + H, F32), "rp": _sb(H, BF), "am": _sb(C, F32), "wm": _sb(C, F32), "se": _sb(H, F32), "so": _sb(H, F32),
+    "f1": _sb(H, BF), "p1": _sb(H, BF), "cb": _sb(2 * W, BF), "cn": _sb(2 * W, BF), "jk": _sb(2 * W, BF),
     "jv": _sb(28 * K, BF), "acc": _sb(2, F32), "oa": _sb(4, U16), "cd": _sb(128, F32), "col": _sb(129, F32),
     "dc": _sb(128, F32), "a2": _sb(128, F32), "w2": _sb(128, F32), "f2": _sb(128, BF), "p2": _sb(128, F32),
     "a3": _sb(128, F32), "w3": _sb(128, F32), "or2": _sb(8, U16),
     "ra0": _sb(128, F32), "ra1": _sb(128, F32), "lr0": _sb(K, F32), "lr1": _sb(K, F32),
-    "ora": _sb(4, U16), "av": _sb(K, F32), "af": _sb(K, F32), "vacc": _sb(28, F32), "ov": _sb(28, U16),
+    "ora": _sb(4, U16), "av": _sb(K, F32), "vacc": _sb(28, F32), "ov": _sb(28, U16),
     "bv": _sb(K, F32), "a4": _sb(K, F32), "w4": _sb(K, F32), "sm": _sb(4 * 32, BF), "od": _sb(8, U16),
     "vf": _sb(K, BF), "vb": _sb(K, BF), "oes": _sb(8, F32), "oe": _sb(8, U16),
     "tf0": _sb(TB, BF), "tb0": _sb(TB, BF), "tf1": _sb(TB, BF), "tb1": _sb(TB, BF),
-    "ff": _sb(TB + S, BF), "fb": _sb(TB + S, BF),
+    "ff": _sb(TB, BF), "fb": _sb(TB, BF),
     "bi": _sb(K, I32), "sf": _sb(7 * K, F32), "gr": _sb(2 * K, F32), "m1": _sb(2 * K, F32), "m0": _sb(K + 1, F32),
     "dq": _sb(K + 1, F32), "xu": _sb(K, F32),
     "ut": _sb(K + 1, F32), "fw": _sb(C, F32), "ug": _sb(C, F32),
-    "qs": _sb(C, F32), "oqo": _sb(28, U16), "qr0": _sb(C, F32), "qr1": _sb(C, F32),
+    "qs": _sb(C, F32), "oqo": _sb(28, U16), "qr": _sb(2 * C, F32),
     "ps": ("psum", [128, 4096], F32),
 }
 SEMAPHORES = (["ev", "ea", "ep", "eg", "loc", "z0", "z1"] + ["ar%d" % i for i in range(4)]
@@ -177,12 +180,22 @@ def rank_program(g, core, T, topo):
     iota(T.jm[:], [[0, 8], [1, 16], [0, 2]], 0, 0, "jm")
     iota(T.blk[:, 0:8], [[-16, 8]], 0, 1, "blk.0")
     iota(T.iof[:], [[1, C]], 0, 0, "iof")
+    iota(T.nb[:], [[S, NB], [0, 3]], 0, 0, "nb")
+    iota(T.nr[:, 0:33], [[S, 11], [0, 3]], 0, 0, "nr.0")
+    iota(T.nr[:, 33:], [[S, 11], [0, 3]], S, 0, "nr.2")
+    iota(T.nr[:, 32:33], [[0, 1]], 0, 0, "nr.0 nr.1")
+    iota(T.pws[:], [[-16, 28], [2047, 16]], 512, 0, "pws")
     ms(T.r32[:], BIG, "r32")
     ts(ipa, ip, 15, A.bitwise_and, "ip", "ipa")
     cp(T.oul[:], iul, "iul", "oul")
     ms(T.r32[:, 0::32], -BIG, "r32")
     ts(T.pc[:, 0:1], ipa, -FAR, A.mult, "ipa", "pc.0")
-    ms(T.ct[:, 12 * H + 3::4], 0.0, "ct.15")
+    ms(T.ct[:, 2 * 960 + 3:2 * 960 + 4 * P:4], 0.0, "ct.11.0.0")
+    ms(T.ct[:, 2 * 960 + 514:3 * 960:4], 0.0, "ct.10.1.0")
+    for q in range(4):
+        ms(T.ct[:, 960 * q + 4 * P:960 * q + 512], 0.0, "ct.z%d" % q)
+    ms(T.rp[:, 0::2], -BIG, "rp.0")
+    ms(T.rp[:, 1::2], BIG, "rp.1")
     ts(T.pc[:, 1:2], ipa, 0.5, A.add, "ipa", "pc.1")
     ts(T.pc[:, 2:3], ipa, -2048.0 * U, A.mult, "ipa", "pc.2")
     ms(T.r16[:], BIG, "r16")
@@ -201,10 +214,14 @@ def rank_program(g, core, T, topo):
         act(T.ek[:, 64 * j:64 * j + 64], T.jm[:, 0:64], F.Identity, "jm blk.3", "ek.%d" % j, scale=0.0,
             bias=T.blk[:, 24 + j:25 + j])
     act(T.thr[:], T.iof[:, 0::16], F.Identity, "iof pc.1", "thr", bias=T.pc[:, 1:2])
+    for b in range(4):
+        dma("s", T.eb[:, 512 * b:512 * b + 512], T.zt[:, 0:512], r="zt", w="eb.%d" % b)
 
     later = [
         lambda: ms(T.et[:, 1280:], 0.0, "et.z1"),
+        lambda: ms(T.rz[:], 1.0, "rz"),
         lambda: ms(T.col[:, 0:1], 0.0, "col.z"),
+        lambda: ms(T.rz[:, 0::16], 0.0, "rz"),
         lambda: ms(T.dc[:, 1::2], 1.0 / 1024.0, "dc.1"),
         lambda: ms(T.ones[:], 1.0, "ones"),
         lambda: ms(T.vf[:, 0::3], -1.0, "vf.0"),
@@ -212,11 +229,11 @@ def rank_program(g, core, T, topo):
         lambda: ms(T.vb[:, 0::3], 0.0, "vb.0"),
         lambda: ms(T.vb[:, 2::3], -1.0, "vb.2"),
         lambda: ms(T.ff[:, 0:S], 0.0, "ff.0"),
-        lambda: ms(T.fb[:, TB:], 0.0, "fb.%d" % NB),
         lambda: ms(T.ut[:, K:K + 1], (C - 1) * U, "ut.e"),
-        lambda: tt(T.kb[:], T.km[:, 0:K], T.nr[:, 0:K], A.subtract, "km nr.0 nr.1 nr.2", "kb"),
-        lambda: tt(T.kp[:], T.km[:, 0:K], T.nr[:, 0:K], A.add, "km nr.0 nr.1 nr.2", "kp"),
+        lambda: tt(kb, T.km[:, 0:K], T.nr[:, 0:K], A.subtract, "km nr.0 nr.1 nr.2", "kb"),
+        lambda: tt(kp, T.km[:, 0:K], T.nr[:, 0:K], A.add, "km nr.0 nr.1 nr.2", "kp"),
     ]
+    kb, kp, c2v, af = [T.kc[:, K * i:K * i + K] for i in range(4)]
 
     def fill(n):
         for _ in range(min(n, len(later))):
@@ -232,18 +249,71 @@ def rank_program(g, core, T, topo):
               xs[t][:, 4 * H * h:4 * H * (h + 1)], xnames(t, h), "tq%d.%d" % (t, h))
 
     def score(t, h):
-        for e in range(2):
-            mm(2 * h + e, H, T.ur[:], T.urs[:], T["tq%d" % t][:, H * h:H * h + H], T["ts%d" % t][:, H * h:H * h + H],
-               "ur urs tq%d.%d" % (t, h))
-        act(T.so[:, 112 * h:112 * h + 112], bank(2 * h + 1, 1, H, 2), F.Copy, "ps%d" % (2 * h + 1), "so.%d" % h)
-        act(T.se[:, 112 * h:112 * h + 112], bank(2 * h + 1, 0, H, 2), F.Copy, "ps%d" % (2 * h + 1), "se.%d" % h)
+        for e in range(2 - h):
+            mm(2 * h + e, H, T.ur[:], T.urs[:], T["tq%d" % t][:, H * h:H * h + H],
+               T["ts%d" % t][:, H * h:H * h + H], "ur urs tq%d.%d" % (t, h))
+        if h == 0:
+            apart(0)
+
+    def apart(h):
+        act(T.so[:, P * h:P * h + P], bank(h + 1, 1, H, 2), F.Copy, "ps%d" % (h + 1), "so.%d" % h)
+        act(T.se[:, P * h:P * h + P], bank(h + 1, 0, H, 2), F.Copy, "ps%d" % (h + 1), "se.%d" % h)
 
     def masked(h):
         tt(T.am[:, H * h:H * h + H], bank(2 * h, 0, H), T.k2[:], A.subtract, "ps%d k2" % (2 * h), "am.%d" % h)
 
     def larger(h):
-        tt(T.mx[:, 112 * h:112 * h + 112], bank(2 * h, 0, H, 2), T.so[:, 112 * h:112 * h + 112], A.max,
-           "ps%d so.%d" % (2 * h, h), "mx.%d" % h)
+        if h == 0:
+            tt(T.mx[:, 0:P], bank(0, 0, H, 2), T.so[:, 0:P], A.max, "ps0 so.0", "mx.0")
+        else:
+            scan(T.mx[:, P:], T.rp[:], bank(2, 0, H), -BIG, A.min, A.max, "ps2 rp.0 rp.1", "mx.1")
+
+    def mxv(b, lo, hi):
+        return T.mx[:, P + 1 + 2 * lo:P + 2 * hi:2] if b else T.mx[:, lo:hi]
+
+    def slot1(s, b, lo, hi):
+        o = 960 * (s // 4) + 512 * b
+        return T.ct[:, o + s % 4 + 4 * lo:o + 4 * hi:4]
+
+    def tile1(q, b):
+        o, v = 960 * q + 4 * P * b, slice(256 * q + 128 * b, 256 * q + 128 * b + 128)
+        quant(T.cq[:, v], T.cs[:, v], T.ct[:, o:o + 512],
+              " ".join("ct.%d.%d.%d" % (s, b, i) for s in range(4 * q, 4 * q + 4) for i in range(2)) + " ct.z%d" % q,
+              "cq.%d.%d" % (q, b))
+        mm(4 + 2 * b, 128, T.ekq[:], T.eks[:], T.cq[:, v], T.cs[:, v], "ekq cq.%d.%d" % (q, b), q == 1 - b, q == 3)
+
+    def vblock(c, b, s):
+        m = min(max(16 * c + 16 - P * b, 0), P)
+        for i, (lo, hi, o) in enumerate([(0, m, A.is_lt), (m, P, A.is_le)]):
+            if lo < hi:
+                ts(slot1(s, b, lo, hi), mxv(b, lo, hi), T.wm[:, 32 * c + 31:32 * c + 32], o,
+                   "mx.%d wm.%d" % (b, c // 7), "ct.%d.%d.%d" % (s, b, i))
+
+    def veq(b, s):
+        tt(slot1(s, b, 0, P), mxv(b, 0, P), T.wm[:, H * b + 1:H * b + H:2], A.is_equal, "mx.%d wm.%d" % (b, b),
+           "ct.%d.%d.0" % (s, b))
+
+    def ablocks(blocks, k0):
+        def second(k):
+            c, b, s = blocks[k]
+            m, o = min(max(16 * c + 16 - P * b, 0), P), P * (k0 + k)
+            if m:
+                act(slot1(s, b, 0, m), T.sg[:, o:o + m], F.Relu, "sg.%d" % (k0 + k), "ct.%d.%d.0" % (s, b))
+            if m < P:
+                act(slot1(s, b, m, P), T.sg[:, o + m:o + P], F.Sign, "sg.%d" % (k0 + k), "ct.%d.%d.1" % (s, b),
+                    bias=1.0)
+        for k in range(len(blocks) + 2):
+            if k < len(blocks):
+                c, b, s = blocks[k]
+                act(T.sg[:, P * (k0 + k):P * (k0 + k + 1)], mxv(b, 0, P), F.Sign, "mx.%d wm.%d" % (b, c // 7),
+                    "sg.%d" % (k0 + k), scale=-1.0, bias=T.wm[:, 32 * c + 31:32 * c + 32])
+            if k >= 2:
+                second(k - 2)
+
+    def early():
+        veq(0, 0)
+        for c in range(3):
+            vblock(c, 0, 1 + c)
 
     def wrapped(h):
         v = slice(H * h, H * h + H)
@@ -296,6 +366,7 @@ def rank_program(g, core, T, topo):
     quant(T.ekq[:], T.eks[:], T.ek[:], " ".join("ek.%d" % j for j in range(8)), "ekq")
     wrapped(0)
     larger(0)
+    masked(1)
 
     for t in range(2):
         tq, tsc, lq, ls = T["tq%d" % t], T["ts%d" % t], T["lq%d" % t], T["ls%d" % t]
@@ -304,74 +375,81 @@ def rank_program(g, core, T, topo):
              "tq%d.0 tq%d.1" % (t, t), "ar%d" % (2 * t), "lq")
         if t == 0:
             clear_tables(0, "lq")
-            iota(T.nb[:], [[S, NB], [0, 3]], 0, 0, "nb")
-            iota(T.nr[:, 0:33], [[S, 11], [0, 3]], 0, 0, "nr.0")
-            iota(T.nr[:, 32:33], [[0, 1]], 0, 0, "nr.0 nr.1")
-            iota(T.nr[:, 33:], [[S, 11], [0, 3]], S, 0, "nr.2")
-            iota(T.pws[:], [[-16, 28], [2047, 16]], 512, 0, "pws")
-            iota(T.eb[:], [[0, 2048]], 0, 0, "eb")
             for b in range(4):
                 v = T.eb[:, 512 * b + b:512 * b + 512:4]
-                op("g", lambda: g.affine_select(v, v, [[-1, 128]], A.not_equal, 1.0, 0, 1), "eb", "eb.%d" % b)
+                op("g", lambda: g.affine_select(v, v, [[-1, 128]], A.not_equal, 1.0, 0, 1), "", "eb.%d" % b)
 
-        masked(1)
-        fill(1)
-        wrapped(1)
+        ablocks([(c, 0, 1 + c) for c in range(3, 7)], 0)
+        if t:
+            early()
+            masked(1)
         larger(1)
-        fill(1)
-        vcol, eqs = compare(T.mx, 2, H, T.wm, "wm.0 wm.1", "mx.0 mx.1", T.ct, "ct", T.sg, "sg",
-                            [(8 + i, c) for i, c in enumerate([0, 1, 2, 10, 11, 12])], 14)
+        wrapped(1)
+        if t == 0:
+            early()
+        tile1(1, 0)
+        vblock(6, 1, 7)
+        ablocks([(c, 1, 4 + c) for c in range(3)] + [(c, 0, 5 + c) for c in range(7, 11)]
+                + [(c, 1, 9 + c) for c in range(3, 6)] + [(13, 1, 15)], 4)
+        apart(1)
         half_x(t, 0)
         half_x(t, 1)
+        tile1(0, 0)
+        for c in range(11, 14):
+            vblock(c, 0, c - 3)
+        for c in range(7, 11):
+            vblock(c, 1, c - 7)
+        tile1(2, 0)
+        vblock(11, 1, 8)
+        tile1(0, 1)
+        veq(1, 11)
+        tile1(1, 1)
+        vblock(12, 1, 9)
+        tile1(3, 0)
+        fill(1)
+        tile1(2, 1)
+        fill(1)
+        tile1(3, 1)
 
-        def tile1(q):
-            quant(T.cq[:, H * q:H * q + H], T.cs[:, H * q:H * q + H], T.ct[:, 4 * H * q:4 * H * (q + 1)],
-                  names("ct", q) + " ct.15", "cq.%d" % q)
-            mm(4, H, T.ekq[:], T.eks[:], T.cq[:, H * q:H * q + H], T.cs[:, H * q:H * q + H], "ekq cq.%d" % q,
-               q == 0, q == 3)
-        for s, c in enumerate([3, 4, 5, 6, 7, 8, 9, 13]):
-            vcol(s, c)
-            if s == 4:
-                tile1(0)
-        eqs()
-        tile1(1)
-        tile1(2)
-        tile1(3)
-        fill(4)
-
-        ts(T.f1[:], bank(4, 0, H), 64.5, A.is_le, "ps4", "f1")
+        ts(T.f1[:, 0:P], bank(4, 0, P), 64.5, A.is_le, "ps4", "f1.0")
+        fill(3)
+        scan(T.p1[:, 0:P], T.f1[:, 0:P], T.f1[:, 0:P], 0.0, A.add, A.max, "f1.0", "p1.0")
         fill(1)
-        scan(T.p1[:], T.f1[:], T.f1[:], 0.0, A.add, A.max, "f1", "p1")
+        ts(T.f1[:, P:], bank(6, 16, 128), 64.5, A.is_le, "ps6", "f1.1")
+        fill(2)
+        scan(T.p1[:, P:], T.f1[:, P:], T.f1[:, P:], T.p1[:, P - 1:P], A.add, A.max, "f1.1 p1.0", "p1.1")
+        fill(2)
+        for c in range(2):
+            act(T.jk[:, W * c:W * c + W], T.p1[:, 16 * c:16 * c + W], F.Sign, "p1.0 p1.1 thr", "acc.%d" % c,
+                scale=-1.0, bias=T.thr[:, c:c + 1], accum_out=T.acc[:, c:c + 1])
+        for c in range(2, 4):
+            ts(T.cb[:, W * c - 2 * W:W * c - W], T.p1[:, 16 * c:16 * c + W], T.thr[:, c:c + 1], A.is_lt,
+               "p1.0 p1.1 thr", "cb.%d" % c)
         fill(1)
+        for c in range(2, 4):
+            v = T.cb[:, W * c - 2 * W:W * c - W]
+            scan(T.cn[:, W * c - 2 * W:W * c - W], v, v, 16.0 * c, A.add, A.max, "cb.%d" % c, "cn.%d" % c)
         for c in range(2):
-            act(T.jk[:, 192 * c:192 * c + 192], T.p1[:, 0:192], F.Sign, "p1 thr", "acc.%d" % c, scale=-1.0,
-                bias=T.thr[:, c:c + 1], accum_out=T.acc[:, c:c + 1])
-        for c in range(2):
-            ts(T.cb[:, 192 * c:192 * c + 192], T.p1[:, 32:H], T.thr[:, 2 + c:3 + c], A.is_lt, "p1 thr", "cb.%d" % c)
-        fill(1)
-        for c in range(2):
-            v = T.cb[:, 192 * c:192 * c + 192]
-            scan(T.cn[:, 192 * c:192 * c + 192], v, v, 32.0, A.add, A.max, "cb.%d" % c, "cn.%d" % c)
-        ts(T.oa[:, 0:2], T.acc[:], 0.5, A.mult, "acc.0 acc.1", "oa.0", 96.0, A.add)
-        cp(T.oa[:, 2:4], T.cn[:, 191::192], "cn.0 cn.1", "oa.1")
+            ts(T.oa[:, c:c + 1], T.acc[:, c:c + 1], 0.5, A.mult, "acc.%d" % c, "oa.%d" % c, W / 2 + 16.0 * c, A.add)
+        cp(T.oa[:, 2:4], T.cn[:, W - 1::W], "cn.2 cn.3", "oa.2")
         fill(1)
 
-        act(T.cd[:, 0::2], T.se[:].indirect(T.oa[:]), F.Copy, "se.0 se.1 oa.0 oa.1", "cd.0")
-        act(T.cd[:, 1::2], T.so[:].indirect(T.oa[:]), F.Copy, "so.0 so.1 oa.0 oa.1", "cd.1")
-        tt(T.a2[:, 0::2], T.se[:].indirect(T.oa[:]), T.km[:, 0:128:2], A.subtract, "se.0 se.1 oa.0 oa.1 km", "a2.0")
-        tt(T.a2[:, 1::2], T.so[:].indirect(T.oa[:]), T.km[:, 1:128:2], A.subtract, "so.0 so.1 oa.0 oa.1 km", "a2.1")
+        oa = " oa.0 oa.1 oa.2"
+        act(T.cd[:, 0::2], T.se[:].indirect(T.oa[:]), F.Copy, "se.0 se.1" + oa, "cd.0")
+        act(T.cd[:, 1::2], T.so[:].indirect(T.oa[:]), F.Copy, "so.0 so.1" + oa, "cd.1")
+        tt(T.a2[:, 0::2], T.se[:].indirect(T.oa[:]), T.km[:, 0:128:2], A.subtract, "se.0 se.1 km" + oa, "a2.0")
+        tt(T.a2[:, 1::2], T.so[:].indirect(T.oa[:]), T.km[:, 1:128:2], A.subtract, "so.0 so.1 km" + oa, "a2.1")
         fill(1)
         wrap_scan(T.w2, T.a2, 128, "a2.0 a2.1", "w2")
         fill(1)
-        act(T.col[:, 1::2], T.iof[:].indirect(T.oa[:]), F.Identity, "iof oa.0 oa.1", "col.0", scale=2.0 / 1024.0)
-        act(T.col[:, 2::2], T.iof[:].indirect(T.oa[:]), F.Identity, "iof oa.0 oa.1", "col.1", scale=2.0 / 1024.0,
-            bias=1.0 / 1024.0)
+        act(T.col[:, 1::2], T.iof[:].indirect(T.oa[:]), F.Identity, "iof" + oa, "col.0", scale=2.0 / 1024.0)
         vcol, eqs = compare(T.cd, 1, 128, T.w2, "w2", "cd.0 cd.1", T.et, "et", T.sg2, "sh",
                             [(4, 0), (5, 1), (6, 6)], 8)
+        act(T.col[:, 2::2], T.col[:, 1::2], F.Identity, "col.0", "col.1", bias=1.0 / 1024.0)
         half_x(t, 2)
         half_x(t, 3)
         if t == 0:
-            act(T.c2v[:], T.iof[:, 0:K], F.Identity, "iof", "c2v", scale=2.0, bias=2.0)
+            act(c2v, T.iof[:, 0:K], F.Identity, "iof", "c2v", scale=2.0, bias=2.0)
             act(T.pw[:], T.pws[:], F.Abs, "pws pc.2", "pw", scale=U, bias=T.pc[:, 2:3])
 
         def tile2(q, first, last):
@@ -379,44 +457,48 @@ def rank_program(g, core, T, topo):
                   names("et", q) + " et.z0 et.z1", "eq.%d" % q)
             mm(5, 128, T.ekq[:], T.eks[:], T.eq[:, 128 * q:128 * q + 128], T.es[:, 128 * q:128 * q + 128],
                "ekq eq.%d" % q, first, last)
+        slots = [(0, 7), (1, 3), (2, 4), (3, 2), (7, 5), (4, 0), (5, 1), (6, 6)]
+
+        def beaten(s, c):
+            v = T.et[:, 512 * (s // 4) + s % 4:512 * (s // 4) + 512:4]
+            scan(T.cw[:, 128 * c:128 * c + 128], v, v, T.ec[:, 16 * c + 15:16 * c + 16], A.add, A.max,
+                 "et.%d.0 et.%d.1 ec" % (s, s), "cw.%d" % c)
         eqs()
-        for s, c in [(7, 5), (0, 7), (1, 3), (2, 4), (3, 2)]:
-            vcol(s, c)
+        vcol(*slots[0])
+        vcol(*slots[1])
         tile2(2, True, False)
-        tile2(1, False, False)
-        tile2(0, False, True)
+        scan(T.ec[:], T.rz[:], T.et[:, 1024::4], 0.0, A.mult, A.add, "rz et.8.0", "ec")
+        for s, c in slots[2:5]:
+            vcol(s, c)
+        beaten(*slots[0])
+        tile2(0, False, False)
+        beaten(*slots[1])
+        tile2(1, False, True)
+        for s, c in slots[2:]:
+            beaten(s, c)
         tt(T.dc[:, 0::2], T.col[:, 1::2], T.col[:, 0:128:2], A.subtract, "col.z col.0 col.1", "dc.0")
-        fill(2)
-        tt(T.a3[:], bank(5, 0, 128), T.km[:], A.subtract, "ps5 km", "a3.0 a3.1")
         ts(T.f2[:], bank(5, 0, 128), 64.5, A.is_le, "ps5", "f2", 2.0, A.mult)
-        wrap_scan(T.w3, T.a3, 128, "a3.0 a3.1", "w3")
-        scan(T.p2[:], T.f2[:], T.dc[:], 0.0, A.add, A.add, "f2 dc.0 dc.1", "p2")
-        ts(T.or2[:], T.w3[:, 15:128:16], -1.0, A.add, "w3", "or2")
+        ts(T.or2[:], T.cw[:, 127::128], -1.0, A.mult, " ".join("cw.%d" % c for c in range(8)), "or2", 128.0, A.add)
         fill(1)
+        scan(T.p2[:], T.f2[:], T.dc[:], 0.0, A.add, A.add, "f2 dc.0 dc.1", "p2")
+        fill(2)
         cp(ra[:].indirect(T.or2[:]), T.p2[:], "p2 or2", "ra%d" % t)
         send(t, [(lra[:], ra[:, 0:K])], "ra%d" % t, "ar%d" % (2 * t + 1), "lra")
         if t == 0:
             clear_tables(1, "lra")
 
-        fill(2)
-        tt(T.a3[:, 0:K], ra[:, 0:K], T.km[:, 0:K], A.subtract, "ra%d km" % t, "a3.0")
-        fill(2)
-        wrap_scan(T.w3, T.a3, K, "a3.0", "w3")
         fill(9)
+        if t == 1:
+            quant(T.vq[:], T.vs[:], T.vin[:], "vin", "vq")
+        tt(T.a3[:, 0:K], ra[:, 0:K], T.km[:, 0:K], A.subtract, "ra%d km" % t, "a3.0")
+        wrap_scan(T.w3, T.a3, K, "a3.0", "w3")
         ts(T.ora[:], T.w3[:, 15:K:16], 0.5, A.mult, "w3", "ora", -1.0, A.add)
         if t == 0:
-            tt(T.a3[:, 0:K], T.nb[:, 2:66], T.kp[:], A.subtract, "nb kp", "a3.0")
-            tt(T.a3[:, K:], T.nb[:, 1:65], T.kp[:], A.subtract, "nb kp", "a3.1")
+            tt(T.a3[:, 0:K], T.nb[:, 2:66], kp, A.subtract, "nb kp", "a3.0")
+            tt(T.a3[:, K:], T.nb[:, 1:65], kp, A.subtract, "nb kp", "a3.1")
         cp(T.av[:].indirect(T.ora[:]), ra[:, 0:K], "ra%d ora" % t, "av")
         if t == 0:
             wrap_scan(T.w3, T.a3, 128, "a3.0 a3.1", "w3")
-        tt(T.af[:], T.av[:], T.c2v[:], A.subtract, "av c2v", "af")
-        if t == 0:
-            ts(T.ce[:, 0:4], T.w3[:, 15:K:16], -2.0, A.add, "w3", "ce.0")
-            ts(T.ce[:, 4:8], T.w3[:, K + 15::16], -1.0, A.add, "w3", "ce.1")
-        for c in range(28):
-            act(T.jv[:, K * c:K * c + K], T.af[:], F.Sign, "af thr", "va.%d" % c, scale=-1024.0,
-                bias=T.thr[:, c:c + 1], accum_out=T.vacc[:, c:c + 1])
 
         bv, x = T.bv, T.w4[:, 15::16]
         bf, t1, dl, b2, gl, k0, kq = [T.sf[:, K * i:K * i + K] for i in range(7)]
@@ -432,7 +514,11 @@ def rank_program(g, core, T, topo):
             cp(tab.indirect(T.od[:, 4 * odd + 2 * h:4 * odd + 2 * h + 2]), vals[:, 32 * h:32 * h + 32],
                "od.%d tz%d t%d.%d %s" % (odd, t, d, 1 - h, vn), n)
         cp(bv[:].indirect(T.ora[:]), lra[:], "lra ora", "bv")
-        tt(T.a4[:], bv[:], T.kb[:], A.subtract, "bv kb", "a4")
+        tt(af, T.av[:], c2v, A.subtract, "av c2v", "af")
+        for c in range(28):
+            act(T.jv[:, K * c:K * c + K], af, F.Sign, "af thr", "va.%d" % c, scale=-1024.0,
+                bias=T.thr[:, c:c + 1], accum_out=T.vacc[:, c:c + 1])
+        tt(T.a4[:], bv[:], kb, A.subtract, "bv kb", "a4")
         tt(sm(0), bv[:, 0:63:3], bv[:, 1:63:3], A.is_lt, "bv", "s0")
         tt(sm(1), bv[:, 1:63:3], bv[:, 2:63:3], A.is_gt, "bv", "s1")
         wrap_scan(T.w4, T.a4, K, "a4", "w4")
@@ -444,6 +530,7 @@ def rank_program(g, core, T, topo):
         tt(T.vb[:, 1:63:3], sm(3), sm(2), A.subtract, "s2 s3", "vb.1")
         put(0, 0, 0)
         put(1, 0, 1)
+        ts(T.fb[:, TB - S:TB], T.iof[:, 2:S + 2], bv[:, K - 1:K], A.is_le, "iof bv", "fb.%d" % (NB - 1))
         put(0, 1, 0)
         put(1, 1, 1)
 
@@ -461,18 +548,19 @@ def rank_program(g, core, T, topo):
             lambda: cp(T.bi[:], bv[:], "bv", "bi"),
             lambda: cp(T.oe[:], T.oes[:], "oes.0 oes.1", "oe"),
             lambda: tt(bf, bv[:], T.bi[:], A.subtract, "bv bi", "bf"),
-            lambda: tt(t1, bf, T.af[:], A.subtract, "bf af", "t1"),
+            lambda: tt(t1, bf, af, A.subtract, "bf af", "t1"),
             lambda: ts(b2, bf, 1024.0 * U, A.mult, "bf", "b2", 1023.0 * U, A.add),
             lambda: ts(dl, t1, 1024.0 * U, A.mult, "t1", "dl", 512.0 * U, A.add),
             lambda: ts(T.ov[:], T.vacc[:], 0.5, A.mult, " ".join("va.%d" % c for c in range(28)), "ov", 32.0, A.add),
         ]
         if t == 0:
-            inside.append(lambda: quant(T.vq[:], T.vs[:], T.vin[:], "vin", "vq"))
+            inside[4:4] = [lambda: ts(T.ce[:, 0:4], T.w3[:, 15:K:16], -2.0, A.add, "w3", "ce.0"),
+                           lambda: ts(T.ce[:, 4:8], T.w3[:, K + 15::16], -1.0, A.add, "w3", "ce.1")]
 
         def back(buf, m):
             return buf[:, S * m + S - 1:S * m - 1 if m else None:-1]
-        for k in range(NB):
-            m = NB - 1 - k
+        for k in range(NB - 1):
+            m = NB - 2 - k
             scan(T.ff[:, S * k + S:S * k + 2 * S], tf[:, S * k:S * k + S], T.ff[:, S * k:S * k + S], 0.0, A.add, A.max,
                  "ff.%d t0.0" % k + (" t0.1" if k >= MID else ""), "ff.%d" % (k + 1))
             scan(back(T.fb, m), back(tb, m), back(T.fb, m + 1), 0.0, A.add, A.max,
@@ -480,11 +568,11 @@ def rank_program(g, core, T, topo):
             if inside:
                 inside.pop(0)()
 
-        ffs = " ".join("ff.%d" % k for k in range(NB + 1))
-        fbs = " ".join("fb.%d" % k for k in range(NB + 1))
+        ffs = " ".join("ff.%d" % k for k in range(NB))
+        fbs = " ".join("fb.%d" % k for k in range(NB))
         act(gl, T.ff[:].indirect(T.oe[:, 0:4]), F.Copy, ffs + " oe", "gl", scale=129.0 / 128.0)
-        ts(T.m0[:, 0:1], T.ff[:, TB + S - 1:], -1.0, A.add, ffs, "m0.0")
         tt(T.gr[:, 0:K], T.fb[:].indirect(T.oe[:, 4:8]), dl, A.add, fbs + " oe dl", "gr.0")
+        ts(T.m0[:, 0:1], T.fb[:, 0:1], -1.0, A.add, "fb.0", "m0.0")
         tt(k0, T.fb[:].indirect(T.oe[:, 4:8]), gl, A.add, fbs + " oe gl", "k0")
         tt(T.gr[:, K:], T.gr[:, 0:K], gl, A.add, "gr.0 gl", "gr.1")
         scan(T.m0[:, 1:], k0, k0, T.m0[:, 0:1], A.max, A.max, "k0 m0.0", "m0.1")
@@ -493,69 +581,91 @@ def rank_program(g, core, T, topo):
         tt(T.xu[:], T.m0[:, 0:K], kq, A.subtract, "m0.0 m0.1 kq", "xu")
         tt(T.dq[:], T.m1[:, K - 1:], T.m0[:], A.subtract, "m1 m0.0 m0.1", "dq")
         scan(T.ut[:, K - 1::-1], T.xu[:, ::-1], T.xu[:, ::-1], (C - 1) * U, A.min, A.min, "xu", "ut")
-        halves = [(slice(H * h, H * h + H), slice(14 * h, 14 * h + 14), h) for h in range(2)]
+        cut = (0, CUT[t], C)
+        halves = [(slice(cut[h], cut[h + 1]), slice(cut[h] // 16, cut[h + 1] // 16), h) for h in range(2)]
         for v, o, h in halves:
             act(T.ug[:, v], T.ut[:].indirect(T.ov[:, o]), F.Copy, "ut ut.e ov", "ug.%d" % h)
             tt(T.fw[:, v], T.dq[:].indirect(T.ov[:, o]), T.pw[:, v], A.subtract, "dq ov pw", "fw.%d" % h)
-        for v, o, h in halves:
+
+        def warp(v, o, h):
             scan(T.qs[:, v], T.fw[:, v], T.ug[:, v], 0.0, A.max, A.min, "fw.%d ug.%d" % (h, h), "qs.%d" % h)
-        for v, o, h in halves:
-            ts(T.oqo[:, o], T.qs[:, H * h + 15:H * h + H:16], 1.0 / U, A.mult, "qs.%d" % h, "oqo.%d" % h)
-        qr = T["qr%d" % t]
-        act(qr[:], T.iof[:].indirect(T.oqo[:]), F.Copy, "iof oqo.0 oqo.1", "qr%d" % t)
-        dma("s", T.oq[:, C * t:C * t + C], qr[0:128:16, :], r="qr%d" % t)
+
+        def offsets(v, o, h):
+            ts(T.oqo[:, o], T.qs[:, cut[h] + 15:cut[h + 1]:16], 1.0 / U, A.mult, "qs.%d" % h, "oqo.%d" % h)
+        warp(*halves[0])
+        offsets(*halves[0])
+        warp(*halves[1])
 
         xn = xs[t + 1]
+        xhs = " xh.0 xh.1 xh.2 xh.3"
+
+        def cols(h, b):
+            return slice(4 * cut[h] + b, 4 * cut[h + 1], 4)
+
+        def xname(h, b):
+            return "X%d.%d.%d" % (t + 1, h, b)
+
+        def picked(h, b):
+            return T.dh[:, C * b:C * b + C].indirect(T.oqo[:, halves[h][1]])
 
         def mid(h, b):
-            v = slice(4 * H * h + b, 4 * H * (h + 1), 4)
-            tt(T.gt[:, v], T.dh[:, C * b:C * b + C].indirect(T.oqo[:, 14 * h:14 * h + 14]), T.xh[:, v], A.add,
-               "dh.%d oqo.%d xh.%d xh.%d" % (b, h, 2 * h, 2 * h + 1), "gt.%d.%d" % (h, b))
+            tt(xn[:, cols(h, b)], picked(h, b), T.xh[:, cols(h, b)], A.add, "dh.%d oqo.%d" % (b, h) + xhs, xname(h, b))
+
+        def add(b):
+            tt(xn[:, cols(1, b)], T.yt[:, cols(1, b)], T.xh[:, cols(1, b)], A.add, "yt.%d" % b + xhs, xname(1, b))
 
         def layer(h):
-            quant(T.gq[:, H * h:H * h + H], T.gs[:, H * h:H * h + H], T.gt[:, 4 * H * h:4 * H * (h + 1)],
-                  " ".join("gt.%d.%d" % (h, b) for b in range(4)), "gq.%d" % h)
+            lo, hi = cut[h], cut[h + 1]
+            quant(T.gq[:, lo:hi], T.gs[:, lo:hi], xn[:, 4 * lo:4 * hi], xnames(t + 1, h), "gq.%d" % h)
             for b in range(4):
-                mm(4 * h + b, H, T.wq[:, 128 * b:128 * b + 128], T.wsc[:, 128 * b:128 * b + 128],
-                   T.gq[:, H * h:H * h + H], T.gs[:, H * h:H * h + H], "wq wsc gq.%d" % h)
-                act(T.rl[:, C * b + H * h:C * b + H * h + H], bank(4 * h + b, 0, H), F.Relu, "ps%d" % (4 * h + b),
-                    "rl.%d.%d" % (h, b), scale=0.015625)
+                k = 4 * h + b
+                mm(k, hi - lo, T.wq[:, 128 * b:128 * b + 128], T.wsc[:, 128 * b:128 * b + 128],
+                   T.gq[:, lo:hi], T.gs[:, lo:hi], "wq wsc gq.%d" % h)
+                act(T.rl[:, cols(h, b)], bank(k, 0, hi - lo), F.Relu, "ps%d" % k, "rl.%d.%d" % (h, b), scale=0.015625)
 
         def last(h, b):
-            v = slice(4 * H * h + b, 4 * H * (h + 1), 4)
-            tt(xn[:, v], T.gt[:, v], T.rl[:, C * b + H * h:C * b + H * h + H], A.add,
-               "gt.%d.%d rl.%d.%d" % (h, b, h, b), "X%d.%d.%d" % (t + 1, h, b))
+            v = cols(h, b)
+            tt(xn[:, v], xn[:, v], T.rl[:, v], A.add, "rl.%d.%d" % (h, b), xname(h, b))
 
         def done(h):
-            quant_state(t + 1, h)
             if t == 0:
+                quant_state(1, h)
                 score(1, h)
-            else:
-                lo, hi = H * h, H * h + H
-                mm(h, H, T.vq[:], T.vs[:], T.tq2[:, lo:hi], T.ts2[:, lo:hi], "vq tq2.%d" % h)
-                dma("s", T.oc[:, 4 * lo:4 * hi], T.tq2[:, lo:hi].bitcast(dt.uint8), r="tq2.%d" % h)
-                act(T.ysb[:, lo:hi], bank(h, 0, H), F.Copy, "ps%d" % h, "ysb.%d" % h)
-                dma("a", T.y[:, lo:hi], T.ysb[:, lo:hi], r="ysb.%d" % h)
-        for b in range(4):
+                return
+            lo, hi = cut[h], cut[h + 1]
+            quant(T.tq2[:, lo:hi], T.ts2[:, lo:hi], xn[:, 4 * lo:4 * hi], xnames(2, h), "tq2.%d" % h)
+            mm(h, hi - lo, T.vq[:], T.vs[:], T.tq2[:, lo:hi], T.ts2[:, lo:hi], "vq tq2.%d" % h)
+            dma("s", T.oc[:, 4 * lo:4 * hi], T.tq2[:, lo:hi].bitcast(dt.uint8), r="tq2.%d" % h)
+            act(T.ysb[:, lo:hi], bank(h, 0, hi - lo), F.Copy, "ps%d" % h, "ysb.%d" % h)
+            dma("a", T.y[:, lo:hi], T.ysb[:, lo:hi], r="ysb.%d" % h)
+        mid(0, 0)
+        offsets(*halves[1])
+        for b in range(NA):
+            act(T.yt[:, cols(1, b)], picked(1, b), F.Copy, "dh.%d oqo.1" % b, "yt.%d" % b)
+        for b in range(1, 4):
             mid(0, b)
-        mid(1, 0)
+        second = [lambda b=b: mid(1, b) for b in range(NA, 4)] + [lambda b=b: add(b) for b in range(NA)]
+        second[0]()
         layer(0)
-        for b in range(1, 4):
-            mid(1, b)
-        last(0, 0)
+        for f in second[1:]:
+            f()
         layer(1)
-        for b in range(1, 4):
+        qr = T.qr[:, C * t:C * t + C]
+        act(qr, T.iof[:].indirect(T.oqo[:]), F.Copy, "iof oqo.0 oqo.1", "qr%d" % t)
+        dma("s", T.oq[:, C * t:C * t + C], T.qr[0:128:16, C * t:C * t + C], r="qr%d" % t)
+        for b in range(4):
             last(0, b)
         last(1, 0)
         done(0)
-        for b in range(1, 4):
-            last(1, b)
+        last(1, 1)
+        last(1, 2)
         if t == 0:
             masked(0)
-        done(1)
+        last(1, 3)
         if t == 0:
             wrapped(0)
             larger(0)
+        done(1)
     for k in range(4):
         dma("s", T.osc[4 * k:4 * k + 4, :], T.ts2[32 * k:32 * k + 4, :], r="tq2.0 tq2.1")
 

from concourse.mybir import dt, AluOpType, ActivationFunctionType

C, H, P, K = 448, 224, 112, 64
W = H - K + 16
S, NB, MID = 128, 22, 10
TB = NB * S
CUT = (H, 256)
NA = 4
BIG = 1.0e29
FAR = 2.0 ** 90
U = 2.0 ** -17
F32, BF, I32, U16, X4, U8 = "float32", "bfloat16", "int32", "uint16", "float8_e4m3fn_x4", "uint8"


def _sb(n, d):
    return ("sbuf", [128, n], d)


SCRATCH = {
    "xin": _sb(4 * C, BF), "x1": _sb(4 * C, BF), "x2": _sb(4 * C, BF), "xh": _sb(4 * C, BF), "yt": _sb(4 * C, BF),
    "dh": _sb(4 * C, BF), "rl": _sb(4 * C, F32), "ysb": _sb(C, F32),
    "uin": _sb(512, BF), "vin": _sb(512, BF), "uq": _sb(128, X4), "us": _sb(128, U8), "ur": _sb(128, X4),
    "urs": _sb(128, U8), "vq": _sb(128, X4), "vs": _sb(128, U8), "wq": _sb(512, X4), "wsc": _sb(512, U8),
    "tq0": _sb(C, X4), "tq1": _sb(C, X4), "tq2": _sb(C, X4), "ts0": _sb(C, U8), "ts1": _sb(C, U8), "ts2": _sb(C, U8),
    "lq0": _sb(C, X4), "lq1": _sb(C, X4), "ls0": _sb(C, U8), "ls1": _sb(C, U8), "gq": _sb(C, X4), "gs": _sb(C, U8),
    "eb": _sb(2048, BF), "ebq": _sb(512, X4), "ebs": _sb(512, U8), "ek": _sb(512, BF), "ekq": _sb(128, X4),
    "eks": _sb(128, U8),
    "ct": _sb(4 * 960, BF), "cq": _sb(1024, X4), "cs": _sb(1024, U8), "sg": _sb(16 * P, BF),
    "et": _sb(12 * 128, BF), "eq": _sb(3 * 128, X4), "es": _sb(3 * 128, U8), "sg2": _sb(4 * 128, BF),
    "jm": _sb(256, F32), "pws": _sb(C, F32), "pw": _sb(C, F32), "km": _sb(128, F32), "k2": _sb(H, F32),
    "r32": _sb(H, BF), "r16": _sb(128, BF), "iof": _sb(C, F32), "isml": _sb(32, I32), "blk": _sb(32, F32),
    "ones": _sb(K, BF), "oul": _sb(8, U16), "pc": _sb(8, F32), "thr": _sb(28, F32), "zt": _sb(TB // 4, BF),
    "nb": _sb(66, F32), "nr": _sb(66, F32), "kc": _sb(4 * K, F32), "ce": _sb(8, F32), "rz": _sb(128, BF),
    "cw": _sb(1024, BF), "ec": _sb(128, BF),
    "mx": _sb(P + H, F32), "rp": _sb(H, BF), "am": _sb(C, F32), "wm": _sb(C, F32), "se": _sb(H, F32), "so": _sb(H, F32),
    "f1": _sb(H, BF), "p1": _sb(H, BF), "cb": _sb(2 * W, BF), "cn": _sb(2 * W, BF), "jk": _sb(2 * W, BF),
    "jv": _sb(28 * K, BF), "acc": _sb(2, F32), "oa": _sb(4, U16), "cd": _sb(128, F32), "col": _sb(129, F32),
    "dc": _sb(128, F32), "a2": _sb(128, F32), "w2": _sb(128, F32), "f2": _sb(128, BF), "p2": _sb(128, F32),
    "a3": _sb(128, F32), "w3": _sb(128, F32), "or2": _sb(8, U16),
    "ra0": _sb(128, F32), "ra1": _sb(128, F32), "lr0": _sb(K, F32), "lr1": _sb(K, F32),
    "ora": _sb(4, U16), "av": _sb(K, F32), "vacc": _sb(28, F32), "ov": _sb(28, U16),
    "bv": _sb(K, F32), "a4": _sb(K, F32), "w4": _sb(K, F32), "sm": _sb(4 * 32, BF), "od": _sb(8, U16),
    "vf": _sb(K, BF), "vb": _sb(K, BF), "oes": _sb(8, F32), "oe": _sb(8, U16),
    "tf0": _sb(TB, BF), "tb0": _sb(TB, BF), "tf1": _sb(TB, BF), "tb1": _sb(TB, BF),
    "ff": _sb(TB, BF), "fb": _sb(TB, BF),
    "bi": _sb(K, I32), "sf": _sb(7 * K, F32), "gr": _sb(2 * K, F32), "m1": _sb(2 * K, F32), "m0": _sb(K + 1, F32),
    "dq": _sb(K + 1, F32), "xu": _sb(K, F32),
    "ut": _sb(K + 1, F32), "fw": _sb(C, F32), "ug": _sb(C, F32),
    "qs": _sb(C, F32), "oqo": _sb(28, U16), "qr": _sb(2 * C, F32),
    "ps": ("psum", [128, 4096], F32),
}
SEMAPHORES = (["ev", "ea", "ep", "eg", "loc", "z0", "z1"] + ["ar%d" % i for i in range(4)]
              + ["dm%d" % i for i in range(24)])


def rank_program(g, core, T, topo):
    rank = T.rank_of(core)
    if rank is None:
        return
    A, F = AluOpType, ActivationFunctionType
    V, ACT, PE = g.vector, g.scalar, g.tensor
    queue = {"v": V, "a": ACT, "p": PE, "g": g, "s": g.sync}
    semof = {"v": "ev", "a": "ea", "p": "ep", "g": "eg"}
    total, waited = {}, {}
    clock = {q: {} for q in queue}
    wrote, readers = {}, {}
    ndma = [0]

    def need(q, toks):
        c = clock[q]
        best = {}
        for s, val, ck in toks:
            if c.get(s, 0) < val and best.get(s, (0, None))[0] < val:
                best[s] = (val, ck)
        for s in sorted(best, key=lambda n: -len(best[n][1])):
            val, ck = best[s]
            if c.get(s, 0) >= val:
                continue
            queue[q].wait_ge(T.sem[s], val)
            waited[s] = max(waited.get(s, 0), val)
            for n in ck:
                c[n] = max(c.get(n, 0), ck[n])
            c[s] = val

    def issue(q, fn, r, w, sem, inc):
        toks = [wrote[n] for n in list(r) + list(w) if n in wrote]
        for n in w:
            toks += readers.get(n, [])
        for n in r:
            if n.startswith("ps"):
                toks += [k for k in readers.get(n, []) if k[0] != sem]
        need(q, toks)
        ins = fn()
        if inc:
            ins.then_inc(T.sem[sem], inc)
            total[sem] = total.get(sem, 0) + inc
            tok = (sem, total[sem], dict(clock[q]))
            for n in r:
                readers.setdefault(n, []).append(tok)
            for n in w:
                wrote[n], readers[n] = tok, []

    def op(q, fn, r="", w=""):
        issue(q, fn, r.split(), w.split(), semof[q], 1)

    def dma(q, out, in_, r="", w=""):
        ndma[0] += 1
        issue(q, lambda: queue[q].dma_start(out, in_), r.split(), w.split(), "dm%d" % (ndma[0] - 1), 16)

    def clear_tables(t, after):
        for j in range(8):
            tab = T["t%s%d" % ("fb"[j // 4], t)]
            issue("s", lambda: g.sync.dma_start(tab[:, TB // 4 * (j % 4):TB // 4 * (j % 4 + 1)], T.zt[:]),
                  ["zt", after], ["tz%d" % t] if j == 7 else [], "z%d" % t, 16)

    def send(t, pairs, r, arr, land):
        peer = T.cores[rank ^ (1 << t)]
        rid, pid, _se = topo.addr(peer)
        back = len(topo.engines(peer, core))
        for out, in_ in pairs:
            issue("g", lambda: g.remote_dma(out, in_, T.sem[arr], T.sem.loc, pid, rid, topo.mask(core, peer)),
                  r.split(), [], None, 0)
            total["loc"] = total.get("loc", 0) + len(topo.engines(core, peer))
        total[arr] = back * len(pairs)
        wrote[land] = (arr, total[arr], {})

    def tt(out, a, b, o, r, w):
        op("v", lambda: V.tensor_tensor(out, a, b, o), r, w)

    def ts(out, a, s1, o1, r, w, s2=None, o2=None):
        if o2 is None:
            op("v", lambda: V.tensor_scalar(out, a, s1, None, o1), r, w)
        else:
            op("v", lambda: V.tensor_scalar(out, a, s1, s2, o1, o2), r, w)

    def cp(out, a, r, w):
        op("v", lambda: V.tensor_copy(out, a), r, w)

    def ms(out, val, w):
        op("v", lambda: V.memset(out, val), "", w)

    def scan(out, a, b, init, o0, o1, r, w):
        op("v", lambda: V.tensor_tensor_scan(out, a, b, init, o0, o1), r, w)

    def act(out, a, f, r, w, **kw):
        op("a", lambda: ACT.activation(out, a, f, **kw), r, w)

    def quant(q, s, a, r, w):
        op("v", lambda: V.quantize_mx(q, s, a), r, w)

    def mm(bank, n, lq, ls, rq, rs, r, start=True, stop=True):
        out = T.ps[:, 512 * bank:512 * bank + n]
        if stop:
            op("p", lambda: PE.matmul_mx(out, lq, ls, rq, rs, start, stop), r, "ps%d" % bank)
        else:
            issue("p", lambda: PE.matmul_mx(out, lq, ls, rq, rs, start, stop), r.split(), ["ps%d" % bank], None, 0)

    def bank(b, lo, hi, step=1):
        return T.ps[:, 512 * b + lo:512 * b + hi:step]

    def iota(out, pat, base, cm, w, small=True):
        if small:
            op("g", lambda: g.iota(out, pat, base, cm, allow_small_or_imprecise_dtypes=True), "", w)
        else:
            op("g", lambda: g.iota(out, pat, base, cm), "", w)

    def wrap_scan(out, a, n, r, w):
        scan(out[:, 0:n], T.r16[:, 0:n], a[:, 0:n], -BIG, A.min, A.max, r + " r16", w)

    dma("a", T.uin[:], T.u[:], w="uin")
    dma("s", T.xin[:, 0:4 * H], T.x[:, 0:4 * H], w="X0.0")
    dma("s", T.xin[:, 4 * H:], T.x[:, 4 * H:], w="X0.1")
    dma("s", T.wq[:].bitcast(dt.uint8), T.wc[:], r="X0.0 X0.1", w="wq")
    dma("s", T.wsc[:], T.ws[:], w="wsc")
    dma("s", T.vin[:], T.v[:], w="vin")

    iul, ip, ipa = T.isml[:, 0:8], T.isml[:, 24:25], T.isml[:, 26:27]
    iota(ip, [[0, 1]], 0, 1, "ip", False)
    iota(iul, [[16, 8]], 0, 0, "iul", False)
    iota(T.jm[:], [[0, 8], [1, 16], [0, 2]], 0, 0, "jm")
    iota(T.blk[:, 0:8], [[-16, 8]], 0, 1, "blk.0")
    iota(T.iof[:], [[1, C]], 0, 0, "iof")
    iota(T.nb[:], [[S, NB], [0, 3]], 0, 0, "nb")
    iota(T.nr[:, 0:33], [[S, 11], [0, 3]], 0, 0, "nr.0")
    iota(T.nr[:, 33:], [[S, 11], [0, 3]], S, 0, "nr.2")
    iota(T.nr[:, 32:33], [[0, 1]], 0, 0, "nr.0 nr.1")
    iota(T.pws[:], [[-16, 28], [2047, 16]], 512, 0, "pws")
    ms(T.r32[:], BIG, "r32")
    ts(ipa, ip, 15, A.bitwise_and, "ip", "ipa")
    cp(T.oul[:], iul, "iul", "oul")
    ms(T.r32[:, 0::32], -BIG, "r32")
    ts(T.pc[:, 0:1], ipa, -FAR, A.mult, "ipa", "pc.0")
    ms(T.ct[:, 2 * 960 + 3:2 * 960 + 4 * P:4], 0.0, "ct.11.0.0")
    ms(T.ct[:, 2 * 960 + 514:3 * 960:4], 0.0, "ct.10.1.0")
    for q in range(4):
        ms(T.ct[:, 960 * q + 4 * P:960 * q + 512], 0.0, "ct.z%d" % q)
    ms(T.rp[:, 0::2], -BIG, "rp.0")
    ms(T.rp[:, 1::2], BIG, "rp.1")
    ts(T.pc[:, 1:2], ipa, 0.5, A.add, "ipa", "pc.1")
    ts(T.pc[:, 2:3], ipa, -2048.0 * U, A.mult, "ipa", "pc.2")
    ms(T.r16[:], BIG, "r16")
    ms(T.zt[:], 0.0, "zt")
    ms(T.r16[:, 0::16], -BIG, "r16")
    quant(T.uq[:], T.us[:], T.uin[:], "uin", "uq")
    ms(T.et[:, 1024:1280], 0.0, "et.z0")
    cp(T.ur[:].bitcast(dt.uint32), T.uq[:].bitcast(dt.uint32).indirect(T.oul[:]), "uq oul", "ur")
    act(T.k2[:], T.jm[:, 0:H], F.Abs, "jm pc.0", "k2", scale=FAR, bias=T.pc[:, 0:1])
    act(T.blk[:, 8:16], T.blk[:, 0:8], F.Abs, "blk.0", "blk.1", bias=-7.5)
    act(T.km[:], T.jm[:, 0::2], F.Abs, "jm pc.0", "km", scale=FAR, bias=T.pc[:, 0:1])
    act(T.blk[:, 16:24], T.blk[:, 8:16], F.Sign, "blk.1", "blk.2", scale=-1.0, bias=8.0)
    act(T.urs[:], T.us[:].indirect(T.oul[:]), F.Copy, "uq oul", "urs")
    act(T.blk[:, 24:32], T.blk[:, 16:24], F.Relu, "blk.2", "blk.3")
    for j in range(8):
        act(T.ek[:, 64 * j:64 * j + 64], T.jm[:, 0:64], F.Identity, "jm blk.3", "ek.%d" % j, scale=0.0,
            bias=T.blk[:, 24 + j:25 + j])
    act(T.thr[:], T.iof[:, 0::16], F.Identity, "iof pc.1", "thr", bias=T.pc[:, 1:2])
    for b in range(4):
        dma("s", T.eb[:, 512 * b:512 * b + 512], T.zt[:, 0:512], r="zt", w="eb.%d" % b)

    later = [
        lambda: ms(T.et[:, 1280:], 0.0, "et.z1"),
        lambda: ms(T.rz[:], 1.0, "rz"),
        lambda: ms(T.col[:, 0:1], 0.0, "col.z"),
        lambda: ms(T.rz[:, 0::16], 0.0, "rz"),
        lambda: ms(T.dc[:, 1::2], 1.0 / 1024.0, "dc.1"),
        lambda: ms(T.ones[:], 1.0, "ones"),
        lambda: ms(T.vf[:, 0::3], -1.0, "vf.0"),
        lambda: ms(T.vf[:, 2::3], 0.0, "vf.2"),
        lambda: ms(T.vb[:, 0::3], 0.0, "vb.0"),
        lambda: ms(T.vb[:, 2::3], -1.0, "vb.2"),
        lambda: ms(T.ff[:, 0:S], 0.0, "ff.0"),
        lambda: ms(T.ut[:, K:K + 1], (C - 1) * U, "ut.e"),
        lambda: tt(kb, T.km[:, 0:K], T.nr[:, 0:K], A.subtract, "km nr.0 nr.1 nr.2", "kb"),
        lambda: tt(kp, T.km[:, 0:K], T.nr[:, 0:K], A.add, "km nr.0 nr.1 nr.2", "kp"),
    ]
    kb, kp, c2v, af = [T.kc[:, K * i:K * i + K] for i in range(4)]

    def fill(n):
        for _ in range(min(n, len(later))):
            later.pop(0)()

    xs = [T.xin, T.x1, T.x2]

    def xnames(t, h):
        return "X0.%d" % h if t == 0 else " ".join("X%d.%d.%d" % (t, h, b) for b in range(4))

    def quant_state(t, h):
        quant(T["tq%d" % t][:, H * h:H * h + H], T["ts%d" % t][:, H * h:H * h + H],
              xs[t][:, 4 * H * h:4 * H * (h + 1)], xnames(t, h), "tq%d.%d" % (t, h))

    def score(t, h):
        for e in range(2 - h):
            mm(2 * h + e, H, T.ur[:], T.urs[:], T["tq%d" % t][:, H * h:H * h + H],
               T["ts%d" % t][:, H * h:H * h + H], "ur urs tq%d.%d" % (t, h))
        if h == 0:
            apart(0)

    def apart(h):
        act(T.so[:, P * h:P * h + P], bank(h + 1, 1, H, 2), F.Copy, "ps%d" % (h + 1), "so.%d" % h)
        act(T.se[:, P * h:P * h + P], bank(h + 1, 0, H, 2), F.Copy, "ps%d" % (h + 1), "se.%d" % h)

    def masked(h):
        tt(T.am[:, H * h:H * h + H], bank(2 * h, 0, H), T.k2[:], A.subtract, "ps%d k2" % (2 * h), "am.%d" % h)

    def larger(h):
        if h == 0:
            tt(T.mx[:, 0:P], bank(0, 0, H, 2), T.so[:, 0:P], A.max, "ps0 so.0", "mx.0")
        else:
            scan(T.mx[:, P:], T.rp[:], bank(2, 0, H), -BIG, A.min, A.max, "ps2 rp.0 rp.1", "mx.1")

    def mxv(b, lo, hi):
        return T.mx[:, P + 1 + 2 * lo:P + 2 * hi:2] if b else T.mx[:, lo:hi]

    def slot1(s, b, lo, hi):
        o = 960 * (s // 4) + 512 * b
        return T.ct[:, o + s % 4 + 4 * lo:o + 4 * hi:4]

    def tile1(q, b):
        o, v = 960 * q + 4 * P * b, slice(256 * q + 128 * b, 256 * q + 128 * b + 128)
        quant(T.cq[:, v], T.cs[:, v], T.ct[:, o:o + 512],
              " ".join("ct.%d.%d.%d" % (s, b, i) for s in range(4 * q, 4 * q + 4) for i in range(2)) + " ct.z%d" % q,
              "cq.%d.%d" % (q, b))
        mm(4 + 2 * b, 128, T.ekq[:], T.eks[:], T.cq[:, v], T.cs[:, v], "ekq cq.%d.%d" % (q, b), q == 1 - b, q == 3)

    def vblock(c, b, s):
        m = min(max(16 * c + 16 - P * b, 0), P)
        for i, (lo, hi, o) in enumerate([(0, m, A.is_lt), (m, P, A.is_le)]):
            if lo < hi:
                ts(slot1(s, b, lo, hi), mxv(b, lo, hi), T.wm[:, 32 * c + 31:32 * c + 32], o,
                   "mx.%d wm.%d" % (b, c // 7), "ct.%d.%d.%d" % (s, b, i))

    def veq(b, s):
        tt(slot1(s, b, 0, P), mxv(b, 0, P), T.wm[:, H * b + 1:H * b + H:2], A.is_equal, "mx.%d wm.%d" % (b, b),
           "ct.%d.%d.0" % (s, b))

    def ablocks(blocks, k0):
        def second(k):
            c, b, s = blocks[k]
            m, o = min(max(16 * c + 16 - P * b, 0), P), P * (k0 + k)
            if m:
                act(slot1(s, b, 0, m), T.sg[:, o:o + m], F.Relu, "sg.%d" % (k0 + k), "ct.%d.%d.0" % (s, b))
            if m < P:
                act(slot1(s, b, m, P), T.sg[:, o + m:o + P], F.Sign, "sg.%d" % (k0 + k), "ct.%d.%d.1" % (s, b),
                    bias=1.0)
        for k in range(len(blocks) + 2):
            if k < len(blocks):
                c, b, s = blocks[k]
                act(T.sg[:, P * (k0 + k):P * (k0 + k + 1)], mxv(b, 0, P), F.Sign, "mx.%d wm.%d" % (b, c // 7),
                    "sg.%d" % (k0 + k), scale=-1.0, bias=T.wm[:, 32 * c + 31:32 * c + 32])
            if k >= 2:
                second(k - 2)

    def early():
        veq(0, 0)
        for c in range(3):
            vblock(c, 0, 1 + c)

    def wrapped(h):
        v = slice(H * h, H * h + H)
        scan(T.wm[:, v], T.r32[:], T.am[:, v], -BIG, A.min, A.max, "am.%d r32" % h, "wm.%d" % h)

    def half_x(t, j):
        v = slice(C * j, C * j + C)
        act(T.xh[:, v], xs[t][:, v], F.Copy, xnames(t, j // 2), "xh.%d" % j, scale=0.5)

    def compare(src, step, n, w, wname, sname, tile, tname, tmp, tmpname, acols, eqslot):
        def slot(s, lo, hi):
            o = 4 * n * (s // 4)
            return tile[:, o + s % 4 + 4 * lo:o + 4 * hi:4]

        def second(k):
            s, c = acols[k]
            m = 16 * c + 16
            act(slot(s, 0, m), tmp[:, n * k:n * k + m], F.Relu, "%s.%d" % (tmpname, k), "%s.%d.0" % (tname, s))
            if m < n:
                act(slot(s, m, n), tmp[:, n * k + m:n * k + n], F.Sign, "%s.%d" % (tmpname, k),
                    "%s.%d.1" % (tname, s), bias=1.0)
        for k, (s, c) in enumerate(acols):
            e = step * (16 * c + 16)
            act(tmp[:, n * k:n * k + n], src[:, 0:n], F.Sign, sname + " " + wname, "%s.%d" % (tmpname, k),
                scale=-1.0, bias=w[:, e - 1:e])
            if k:
                second(k - 1)
        second(len(acols) - 1)

        def vcol(s, c):
            m = 16 * c + 16
            sc = w[:, step * m - 1:step * m]
            ts(slot(s, 0, m), src[:, 0:m], sc, A.is_lt, sname + " " + wname, "%s.%d.0" % (tname, s))
            if m < n:
                ts(slot(s, m, n), src[:, m:n], sc, A.is_le, sname + " " + wname, "%s.%d.1" % (tname, s))

        def eqs():
            tt(slot(eqslot, 0, n), src[:, 0:n], w[:, step - 1:step * n:step], A.is_equal, sname + " " + wname,
               "%s.%d.0" % (tname, eqslot))
        return vcol, eqs

    def names(tname, q):
        return " ".join("%s.%d.%d" % (tname, s, i) for s in range(4 * q, 4 * q + 4) for i in range(2))

    for h in range(2):
        quant_state(0, h)
        score(0, h)
    fill(2)
    masked(0)
    quant(T.ekq[:], T.eks[:], T.ek[:], " ".join("ek.%d" % j for j in range(8)), "ekq")
    wrapped(0)
    larger(0)
    masked(1)

    for t in range(2):
        tq, tsc, lq, ls = T["tq%d" % t], T["ts%d" % t], T["lq%d" % t], T["ls%d" % t]
        ra, lra, tf, tb = T["ra%d" % t], T["lr%d" % t], T["tf%d" % t], T["tb%d" % t]
        send(t, [(lq[:].bitcast(dt.uint8), tq[:].bitcast(dt.uint8)), (ls[:], tsc[:])],
             "tq%d.0 tq%d.1" % (t, t), "ar%d" % (2 * t), "lq")
        if t == 0:
            clear_tables(0, "lq")
            for b in range(4):
                v = T.eb[:, 512 * b + b:512 * b + 512:4]
                op("g", lambda: g.affine_select(v, v, [[-1, 128]], A.not_equal, 1.0, 0, 1), "", "eb.%d" % b)

        ablocks([(c, 0, 1 + c) for c in range(3, 7)], 0)
        if t:
            early()
            masked(1)
        larger(1)
        wrapped(1)
        if t == 0:
            early()
        tile1(1, 0)
        vblock(6, 1, 7)
        ablocks([(c, 1, 4 + c) for c in range(3)] + [(c, 0, 5 + c) for c in range(7, 11)]
                + [(c, 1, 9 + c) for c in range(3, 6)] + [(13, 1, 15)], 4)
        apart(1)
        half_x(t, 0)
        half_x(t, 1)
        tile1(0, 0)
        for c in range(11, 14):
            vblock(c, 0, c - 3)
        for c in range(7, 11):
            vblock(c, 1, c - 7)
        tile1(2, 0)
        vblock(11, 1, 8)
        tile1(0, 1)
        veq(1, 11)
        tile1(1, 1)
        vblock(12, 1, 9)
        tile1(3, 0)
        fill(1)
        tile1(2, 1)
        fill(1)
        tile1(3, 1)

        ts(T.f1[:, 0:P], bank(4, 0, P), 64.5, A.is_le, "ps4", "f1.0")
        fill(3)
        scan(T.p1[:, 0:P], T.f1[:, 0:P], T.f1[:, 0:P], 0.0, A.add, A.max, "f1.0", "p1.0")
        fill(1)
        ts(T.f1[:, P:], bank(6, 16, 128), 64.5, A.is_le, "ps6", "f1.1")
        fill(2)
        scan(T.p1[:, P:], T.f1[:, P:], T.f1[:, P:], T.p1[:, P - 1:P], A.add, A.max, "f1.1 p1.0", "p1.1")
        fill(2)
        for c in range(2):
            act(T.jk[:, W * c:W * c + W], T.p1[:, 16 * c:16 * c + W], F.Sign, "p1.0 p1.1 thr", "acc.%d" % c,
                scale=-1.0, bias=T.thr[:, c:c + 1], accum_out=T.acc[:, c:c + 1])
        for c in range(2, 4):
            ts(T.cb[:, W * c - 2 * W:W * c - W], T.p1[:, 16 * c:16 * c + W], T.thr[:, c:c + 1], A.is_lt,
               "p1.0 p1.1 thr", "cb.%d" % c)
        fill(1)
        for c in range(2, 4):
            v = T.cb[:, W * c - 2 * W:W * c - W]
            scan(T.cn[:, W * c - 2 * W:W * c - W], v, v, 16.0 * c, A.add, A.max, "cb.%d" % c, "cn.%d" % c)
        for c in range(2):
            ts(T.oa[:, c:c + 1], T.acc[:, c:c + 1], 0.5, A.mult, "acc.%d" % c, "oa.%d" % c, W / 2 + 16.0 * c, A.add)
        cp(T.oa[:, 2:4], T.cn[:, W - 1::W], "cn.2 cn.3", "oa.2")
        fill(1)

        oa = " oa.0 oa.1 oa.2"
        act(T.cd[:, 0::2], T.se[:].indirect(T.oa[:]), F.Copy, "se.0 se.1" + oa, "cd.0")
        act(T.cd[:, 1::2], T.so[:].indirect(T.oa[:]), F.Copy, "so.0 so.1" + oa, "cd.1")
        tt(T.a2[:, 0::2], T.se[:].indirect(T.oa[:]), T.km[:, 0:128:2], A.subtract, "se.0 se.1 km" + oa, "a2.0")
        tt(T.a2[:, 1::2], T.so[:].indirect(T.oa[:]), T.km[:, 1:128:2], A.subtract, "so.0 so.1 km" + oa, "a2.1")
        fill(1)
        wrap_scan(T.w2, T.a2, 128, "a2.0 a2.1", "w2")
        fill(1)
        act(T.col[:, 1::2], T.iof[:].indirect(T.oa[:]), F.Identity, "iof" + oa, "col.0", scale=2.0 / 1024.0)
        vcol, eqs = compare(T.cd, 1, 128, T.w2, "w2", "cd.0 cd.1", T.et, "et", T.sg2, "sh",
                            [(4, 0), (5, 1), (6, 6)], 8)
        act(T.col[:, 2::2], T.col[:, 1::2], F.Identity, "col.0", "col.1", bias=1.0 / 1024.0)
        half_x(t, 2)
        half_x(t, 3)
        if t == 0:
            act(c2v, T.iof[:, 0:K], F.Identity, "iof", "c2v", scale=2.0, bias=2.0)
            act(T.pw[:], T.pws[:], F.Abs, "pws pc.2", "pw", scale=U, bias=T.pc[:, 2:3])

        def tile2(q, first, last):
            quant(T.eq[:, 128 * q:128 * q + 128], T.es[:, 128 * q:128 * q + 128], T.et[:, 512 * q:512 * q + 512],
                  names("et", q) + " et.z0 et.z1", "eq.%d" % q)
            mm(5, 128, T.ekq[:], T.eks[:], T.eq[:, 128 * q:128 * q + 128], T.es[:, 128 * q:128 * q + 128],
               "ekq eq.%d" % q, first, last)
        slots = [(0, 7), (1, 3), (2, 4), (3, 2), (7, 5), (4, 0), (5, 1), (6, 6)]

        def beaten(s, c):
            v = T.et[:, 512 * (s // 4) + s % 4:512 * (s // 4) + 512:4]
            scan(T.cw[:, 128 * c:128 * c + 128], v, v, T.ec[:, 16 * c + 15:16 * c + 16], A.add, A.max,
                 "et.%d.0 et.%d.1 ec" % (s, s), "cw.%d" % c)
        eqs()
        vcol(*slots[0])
        vcol(*slots[1])
        tile2(2, True, False)
        scan(T.ec[:], T.rz[:], T.et[:, 1024::4], 0.0, A.mult, A.add, "rz et.8.0", "ec")
        for s, c in slots[2:5]:
            vcol(s, c)
        beaten(*slots[0])
        tile2(0, False, False)
        beaten(*slots[1])
        tile2(1, False, True)
        for s, c in slots[2:]:
            beaten(s, c)
        tt(T.dc[:, 0::2], T.col[:, 1::2], T.col[:, 0:128:2], A.subtract, "col.z col.0 col.1", "dc.0")
        ts(T.f2[:], bank(5, 0, 128), 64.5, A.is_le, "ps5", "f2", 2.0, A.mult)
        ts(T.or2[:], T.cw[:, 127::128], -1.0, A.mult, " ".join("cw.%d" % c for c in range(8)), "or2", 128.0, A.add)
        fill(1)
        scan(T.p2[:], T.f2[:], T.dc[:], 0.0, A.add, A.add, "f2 dc.0 dc.1", "p2")
        fill(2)
        cp(ra[:].indirect(T.or2[:]), T.p2[:], "p2 or2", "ra%d" % t)
        send(t, [(lra[:], ra[:, 0:K])], "ra%d" % t, "ar%d" % (2 * t + 1), "lra")
        if t == 0:
            clear_tables(1, "lra")

        fill(9)
        if t == 1:
            quant(T.vq[:], T.vs[:], T.vin[:], "vin", "vq")
        tt(T.a3[:, 0:K], ra[:, 0:K], T.km[:, 0:K], A.subtract, "ra%d km" % t, "a3.0")
        wrap_scan(T.w3, T.a3, K, "a3.0", "w3")
        ts(T.ora[:], T.w3[:, 15:K:16], 0.5, A.mult, "w3", "ora", -1.0, A.add)
        if t == 0:
            tt(T.a3[:, 0:K], T.nb[:, 2:66], kp, A.subtract, "nb kp", "a3.0")
            tt(T.a3[:, K:], T.nb[:, 1:65], kp, A.subtract, "nb kp", "a3.1")
        cp(T.av[:].indirect(T.ora[:]), ra[:, 0:K], "ra%d ora" % t, "av")
        if t == 0:
            wrap_scan(T.w3, T.a3, 128, "a3.0 a3.1", "w3")

        bv, x = T.bv, T.w4[:, 15::16]
        bf, t1, dl, b2, gl, k0, kq = [T.sf[:, K * i:K * i + K] for i in range(7)]

        def sm(i):
            return T.sm[:, 32 * i:32 * i + 21]

        def put(d, what, h):
            tab = (tf, tb)[d][:, S * MID * h:S * (MID + 1) if h == 0 else TB]
            odd = d if what else 1 - d
            vals, vn = ((T.vf, "vf.0 vf.1 vf.2"), (T.vb, "vb.0 vb.1 vb.2"))[d] if what else (T.ones, "ones")
            n = "t%d.%d" % (d, h)
            cp(tab.indirect(T.od[:, 4 * odd + 2 * h:4 * odd + 2 * h + 2]), vals[:, 32 * h:32 * h + 32],
               "od.%d tz%d t%d.%d %s" % (odd, t, d, 1 - h, vn), n)
        cp(bv[:].indirect(T.ora[:]), lra[:], "lra ora", "bv")
        tt(af, T.av[:], c2v, A.subtract, "av c2v", "af")
        for c in range(28):
            act(T.jv[:, K * c:K * c + K], af, F.Sign, "af thr", "va.%d" % c, scale=-1024.0,
                bias=T.thr[:, c:c + 1], accum_out=T.vacc[:, c:c + 1])
        tt(T.a4[:], bv[:], kb, A.subtract, "bv kb", "a4")
        tt(sm(0), bv[:, 0:63:3], bv[:, 1:63:3], A.is_lt, "bv", "s0")
        tt(sm(1), bv[:, 1:63:3], bv[:, 2:63:3], A.is_gt, "bv", "s1")
        wrap_scan(T.w4, T.a4, K, "a4", "w4")
        tt(sm(2), bv[:, 2:63:3], bv[:, 0:63:3], A.is_gt, "bv", "s2")
        tt(sm(3), sm(0), sm(1), A.subtract, "s0 s1", "s3")
        ts(T.od[:, 4:8], x, -1.0, A.add, "w4", "od.1")
        ts(T.od[:, 0:4], x, -2.0, A.add, "w4", "od.0")
        tt(T.vf[:, 1:63:3], sm(3), sm(2), A.subtract, "s2 s3", "vf.1")
        tt(T.vb[:, 1:63:3], sm(3), sm(2), A.subtract, "s2 s3", "vb.1")
        put(0, 0, 0)
        put(1, 0, 1)
        ts(T.fb[:, TB - S:TB], T.iof[:, 2:S + 2], bv[:, K - 1:K], A.is_le, "iof bv", "fb.%d" % (NB - 1))
        put(0, 1, 0)
        put(1, 1, 1)

        def unpack(b):
            v = slice(128 * b, 128 * b + 128)
            if t == 0:
                quant(T.ebq[:, v], T.ebs[:, v], T.eb[:, 512 * b:512 * b + 512], "eb.%d" % b, "ebq.%d" % b)
            mm(b, C, T.ebq[:, v], T.ebs[:, v], lq[:], ls[:], "ebq.%d lq" % b)
            act(T.dh[:, C * b:C * b + C], bank(b, 0, C), F.Copy, "ps%d" % b, "dh.%d" % b, scale=0.5)
        inside = [
            lambda: put(0, 0, 1), lambda: put(1, 0, 0), lambda: put(0, 1, 1), lambda: put(1, 1, 0),
            lambda: unpack(0), lambda: unpack(1), lambda: unpack(2), lambda: unpack(3),
            lambda: tt(T.oes[:, 0:4], x, T.ce[:, 0:4], A.add, "w4 ce.0", "oes.0"),
            lambda: tt(T.oes[:, 4:8], x, T.ce[:, 4:8], A.add, "w4 ce.1", "oes.1"),
            lambda: cp(T.bi[:], bv[:], "bv", "bi"),
            lambda: cp(T.oe[:], T.oes[:], "oes.0 oes.1", "oe"),
            lambda: tt(bf, bv[:], T.bi[:], A.subtract, "bv bi", "bf"),
            lambda: tt(t1, bf, af, A.subtract, "bf af", "t1"),
            lambda: ts(b2, bf, 1024.0 * U, A.mult, "bf", "b2", 1023.0 * U, A.add),
            lambda: ts(dl, t1, 1024.0 * U, A.mult, "t1", "dl", 512.0 * U, A.add),
            lambda: ts(T.ov[:], T.vacc[:], 0.5, A.mult, " ".join("va.%d" % c for c in range(28)), "ov", 32.0, A.add),
        ]
        if t == 0:
            inside[4:4] = [lambda: ts(T.ce[:, 0:4], T.w3[:, 15:K:16], -2.0, A.add, "w3", "ce.0"),
                           lambda: ts(T.ce[:, 4:8], T.w3[:, K + 15::16], -1.0, A.add, "w3", "ce.1")]

        def back(buf, m):
            return buf[:, S * m + S - 1:S * m - 1 if m else None:-1]
        for k in range(NB - 1):
            m = NB - 2 - k
            scan(T.ff[:, S * k + S:S * k + 2 * S], tf[:, S * k:S * k + S], T.ff[:, S * k:S * k + S], 0.0, A.add, A.max,
                 "ff.%d t0.0" % k + (" t0.1" if k >= MID else ""), "ff.%d" % (k + 1))
            scan(back(T.fb, m), back(tb, m), back(T.fb, m + 1), 0.0, A.add, A.max,
                 "fb.%d t1.1" % (m + 1) + (" t1.0" if m <= MID else ""), "fb.%d" % m)
            if inside:
                inside.pop(0)()

        ffs = " ".join("ff.%d" % k for k in range(NB))
        fbs = " ".join("fb.%d" % k for k in range(NB))
        act(gl, T.ff[:].indirect(T.oe[:, 0:4]), F.Copy, ffs + " oe", "gl", scale=129.0 / 128.0)
        tt(T.gr[:, 0:K], T.fb[:].indirect(T.oe[:, 4:8]), dl, A.add, fbs + " oe dl", "gr.0")
        ts(T.m0[:, 0:1], T.fb[:, 0:1], -1.0, A.add, "fb.0", "m0.0")
        tt(k0, T.fb[:].indirect(T.oe[:, 4:8]), gl, A.add, fbs + " oe gl", "k0")
        tt(T.gr[:, K:], T.gr[:, 0:K], gl, A.add, "gr.0 gl", "gr.1")
        scan(T.m0[:, 1:], k0, k0, T.m0[:, 0:1], A.max, A.max, "k0 m0.0", "m0.1")
        tt(kq, k0, b2, A.subtract, "k0 b2", "kq")
        scan(T.m1[:], T.gr[:], T.gr[:], 0.0, A.max, A.max, "gr.0 gr.1", "m1")
        tt(T.xu[:], T.m0[:, 0:K], kq, A.subtract, "m0.0 m0.1 kq", "xu")
        tt(T.dq[:], T.m1[:, K - 1:], T.m0[:], A.subtract, "m1 m0.0 m0.1", "dq")
        scan(T.ut[:, K - 1::-1], T.xu[:, ::-1], T.xu[:, ::-1], (C - 1) * U, A.min, A.min, "xu", "ut")
        cut = (0, CUT[t], C)
        halves = [(slice(cut[h], cut[h + 1]), slice(cut[h] // 16, cut[h + 1] // 16), h) for h in range(2)]
        for v, o, h in halves:
            act(T.ug[:, v], T.ut[:].indirect(T.ov[:, o]), F.Copy, "ut ut.e ov", "ug.%d" % h)
            tt(T.fw[:, v], T.dq[:].indirect(T.ov[:, o]), T.pw[:, v], A.subtract, "dq ov pw", "fw.%d" % h)

        def warp(v, o, h):
            scan(T.qs[:, v], T.fw[:, v], T.ug[:, v], 0.0, A.max, A.min, "fw.%d ug.%d" % (h, h), "qs.%d" % h)

        def offsets(v, o, h):
            ts(T.oqo[:, o], T.qs[:, cut[h] + 15:cut[h + 1]:16], 1.0 / U, A.mult, "qs.%d" % h, "oqo.%d" % h)
        warp(*halves[0])
        offsets(*halves[0])
        warp(*halves[1])

        xn = xs[t + 1]
        xhs = " xh.0 xh.1 xh.2 xh.3"

        def cols(h, b):
            return slice(4 * cut[h] + b, 4 * cut[h + 1], 4)

        def xname(h, b):
            return "X%d.%d.%d" % (t + 1, h, b)

        def picked(h, b):
            return T.dh[:, C * b:C * b + C].indirect(T.oqo[:, halves[h][1]])

        def mid(h, b):
            tt(xn[:, cols(h, b)], picked(h, b), T.xh[:, cols(h, b)], A.add, "dh.%d oqo.%d" % (b, h) + xhs, xname(h, b))

        def add(b):
            tt(xn[:, cols(1, b)], T.yt[:, cols(1, b)], T.xh[:, cols(1, b)], A.add, "yt.%d" % b + xhs, xname(1, b))

        def layer(h):
            lo, hi = cut[h], cut[h + 1]
            quant(T.gq[:, lo:hi], T.gs[:, lo:hi], xn[:, 4 * lo:4 * hi], xnames(t + 1, h), "gq.%d" % h)
            for b in range(4):
                k = 4 * h + b
                mm(k, hi - lo, T.wq[:, 128 * b:128 * b + 128], T.wsc[:, 128 * b:128 * b + 128],
                   T.gq[:, lo:hi], T.gs[:, lo:hi], "wq wsc gq.%d" % h)
                act(T.rl[:, cols(h, b)], bank(k, 0, hi - lo), F.Relu, "ps%d" % k, "rl.%d.%d" % (h, b), scale=0.015625)

        def last(h, b):
            v = cols(h, b)
            tt(xn[:, v], xn[:, v], T.rl[:, v], A.add, "rl.%d.%d" % (h, b), xname(h, b))

        def done(h):
            if t == 0:
                quant_state(1, h)
                score(1, h)
                return
            lo, hi = cut[h], cut[h + 1]
            quant(T.tq2[:, lo:hi], T.ts2[:, lo:hi], xn[:, 4 * lo:4 * hi], xnames(2, h), "tq2.%d" % h)
            mm(h, hi - lo, T.vq[:], T.vs[:], T.tq2[:, lo:hi], T.ts2[:, lo:hi], "vq tq2.%d" % h)
            dma("s", T.oc[:, 4 * lo:4 * hi], T.tq2[:, lo:hi].bitcast(dt.uint8), r="tq2.%d" % h)
            act(T.ysb[:, lo:hi], bank(h, 0, hi - lo), F.Copy, "ps%d" % h, "ysb.%d" % h)
            dma("a", T.y[:, lo:hi], T.ysb[:, lo:hi], r="ysb.%d" % h)
        mid(0, 0)
        offsets(*halves[1])
        for b in range(NA):
            act(T.yt[:, cols(1, b)], picked(1, b), F.Copy, "dh.%d oqo.1" % b, "yt.%d" % b)
        for b in range(1, 4):
            mid(0, b)
        second = [lambda b=b: mid(1, b) for b in range(NA, 4)] + [lambda b=b: add(b) for b in range(NA)]
        second[0]()
        layer(0)
        for f in second[1:]:
            f()
        layer(1)
        qr = T.qr[:, C * t:C * t + C]
        act(qr, T.iof[:].indirect(T.oqo[:]), F.Copy, "iof oqo.0 oqo.1", "qr%d" % t)
        dma("s", T.oq[:, C * t:C * t + C], T.qr[0:128:16, C * t:C * t + C], r="qr%d" % t)
        for b in range(4):
            last(0, b)
        last(1, 0)
        done(0)
        last(1, 1)
        last(1, 2)
        if t == 0:
            masked(0)
        last(1, 3)
        if t == 0:
            wrapped(0)
            larger(0)
        done(1)
    for k in range(4):
        dma("s", T.osc[4 * k:4 * k + 4, :], T.ts2[32 * k:32 * k + 4, :], r="tq2.0 tq2.1")

    for s in total:
        if waited.get(s, 0) < total[s]:
            g.wait_ge(T.sem[s], total[s])
